import numpy as np, ml_dtypes
CORES = [3,7,11,15,131,135,139,143]
N = 8
import mx_ref
BF = ml_dtypes.bfloat16
def gentries(a):
    return np.ascontiguousarray(a.reshape(8, 16, -1).transpose(0, 2, 1)).reshape(8, -1)
def gtable(e):
    e = np.asarray(e); return np.ascontiguousarray(e.reshape(8, -1, 16).transpose(0, 2, 1)).reshape(128, -1).astype(np.int32)
def gcols(t, e):
    v = np.concatenate([t.reshape(8, 16, -1, 4), np.zeros((8, 16, 1, 4), BF)], axis=2)
    return np.ascontiguousarray(np.stack([v[g][:, e[g]] for g in range(8)])).reshape(128, -1)
def tile(rs):
    return np.stack(rs, axis=2).reshape(128, -1).astype(BF)
def pick(q, e):
    c = np.concatenate([q[0].reshape(128, -1, 4), np.zeros((128, 1, 4), np.uint8)], axis=1); s = np.concatenate([q[1], np.ones((16, 1), np.uint8)], axis=1)
    return (np.ascontiguousarray(c[:, e].reshape(128, -1)), np.ascontiguousarray(s[:, e]))
def join(*qs):
    return (np.concatenate([q[0] for q in qs], axis=1), np.concatenate([q[1] for q in qs], axis=1))
def put(q, e, v):
    c, s = q[0].reshape(128, -1, 4).copy(), q[1].copy(); c[:, e] = v[0].reshape(128, -1, 4); s[:, e] = v[1]
    return (c.reshape(128, -1), s)
def pk(c, s):
    return (np.ascontiguousarray(c), mx_ref.live(s))
def emit(q):
    return q[0], q[1]
def packed(v, rng):
    q = [mx_ref.quantize(np.ascontiguousarray(v[r])) for r in range(N)]
    return np.stack([a for a, b in q]), np.stack([mx_ref.plane(b, rng) for a, b in q])
def values_of_codes():
    e, c = np.zeros((128, 128, 4), np.float32), np.zeros((128, 2, 4), np.uint8)
    e[np.arange(128), np.arange(128), 0] = 1
    c[:127, :, 0] = np.arange(256).reshape(2, 128).T[:127]
    return mx_ref.matmul(mx_ref.quantize(e.reshape(128, 512).astype(BF)), (c.reshape(128, 8), np.full((16, 2), 127, np.uint8))).T.reshape(-1).astype(np.float64)
CODE_VALUE, SCALE_VALUE = values_of_codes(), 2.0 ** (np.arange(256) - 127.0)
def decode(q):
    return (CODE_VALUE[q[0]].reshape(16, 8, -1, 4) * SCALE_VALUE[q[1]][:, None, :, None] + 0.0).reshape(128, -1).astype(np.float32)
def f(rng, *shape):
    return mx_ref.flush((rng.standard_normal(shape, dtype=np.float32) * np.exp2(rng.integers(-2, 3, shape[:-1] + (1,)))).astype(BF))
def wide(rng, *shape, cols=0):
    v = rng.standard_normal(shape, dtype=np.float32) * np.exp2(rng.integers(-12, 13, shape)).astype(np.float32)
    if cols: v *= np.repeat(np.exp2(rng.integers(-cols, cols + 1, shape[:-2] + (1, shape[-1] // 4))) * (rng.random(shape[:-2] + (1, shape[-1] // 4)) > 0.0625), 4, axis=-1).astype(np.float32)
    return mx_ref.flush(v.astype(BF))
C, STAGES = 288, 7
STEP = [4, 1, 2]
def numbers_of(rng):
    return {"x": np.array(f(rng, N, 128, 4 * C)), "u": np.array(f(rng, N, 128, 512)), "v": np.array(f(rng, N, 128, 512))}
def stored(a, b, s):
    return {"ta": np.stack([gtable(a[r]) for r in range(N)]), "tb": np.stack([gtable(b[r]) for r in range(N)]), "st": np.stack([gtable(s[r]) for r in range(N)])}
def lists(rng):
    e = np.tile(np.arange(C), (N, 8, 1))
    return stored(rng.permuted(e, axis=2), rng.permuted(e, axis=2), rng.permuted(e, axis=2))
def layers(rng):
    return np.array(f(rng, N, 128, 2048)).reshape(N, 8, 16, 4, 8, 16, 4)
def weights(rng, w):
    c, p = packed(np.ascontiguousarray(w).reshape(N, 128, 2048), rng)
    return {"wc": c, "ws": p}
def setup_inputs(rng):
    return {**numbers_of(rng), **lists(rng), **weights(rng, layers(rng))}
def setup_inputs_ties(rng):
    d = numbers_of(rng)
    o = rng.permutation(N)
    k = rng.integers(-1, 2, (2, N, 8, C)).astype(np.float32)
    k[0, o[1]] = 1
    x = d["x"].reshape(N, 8, 16, C, 4)
    x[:, :, [0, 1, 8]] = 0
    x[:, :, 0, :, 0] = k[0].astype(BF)
    x[:, :, 1, :, 0] = k[1].astype(BF)
    c = np.ones(N, np.float32)
    c[o[0]] = 0
    c[o[2]] = -1
    u = d["u"].reshape(N, 128, 128, 4)
    u[:, :, ::16] = 0
    for h in range(0, 128, 16):
        u[:, h, h, 0] = c.astype(BF)
        u[:, h + 8, h, 0] = c.astype(BF)
    w = layers(rng)
    w[:, :, :, :, :, [0, 1, 8]] = 0
    for g in range(8): w[:, g, 1, 0, g, 8, 0] = 32.0
    return {"x": x.reshape(N, 128, 4 * C), "u": u.reshape(N, 128, 512), "v": d["v"], **lists(rng), **weights(rng, w)}
def setup_inputs_near(rng):
    d = numbers_of(rng)
    o = rng.permutation(N) % 2
    k = np.where(o == 0, 2.0 ** -30, 1.0).astype(np.float32)
    x = np.zeros((N, 8, 16, C, 4), np.float32)
    s = rng.integers(-1, 2, (N, 8, C)) * k[:, None, None]
    x[:, :, 0, :, 0] = 1.125 * s
    x[:, :, 1, :, 0] = -1.25 * s
    for r in range(N):
        for g in rng.permutation(8)[:4]: x[r, g, 0, rng.integers(C), 0] = 2.0 ** 30 * rng.choice([-1.0, 1.0])
    x[:, :, 10, :, 0] = rng.integers(-1, 2, (N, 8, C)) * 2.0 ** -30
    x[:, :, 11, :, 0] = 2.0 ** -30
    u = d["u"].reshape(N, 128, 128, 4)
    u[:, :, ::16] = 0
    for h in range(0, 128, 16):
        u[:, h, h, 0] = (1.125 * k).astype(BF)
        u[:, h + 1, h, 0] = k.astype(BF)
        u[:, h + 8, h, 0] = k.astype(BF)
    w = np.zeros((N, 8, 16, 4, 8, 16, 4), np.float32)
    for g in range(8):
        w[:, g, 10, 0, g, 8, 0] = 2.0 ** -7
        w[:, g, 11, 0, g, 9, 0] = 2.0 ** 7
    for r in range(N):
        for g in rng.permutation(8)[:4]:
            w[r, g, 10, 0, g, 8, 0] = 2.0 ** -11
            w[r, g, 10, 0, g, 13, 0] = -2.0 ** -11
            w[r, g, 12, 0, g, 8, 0] = 2.0 ** -8
            w[r, g, 12, 0, g, 13, 0] = 2.0 ** -8
            w[r, g, 11, 0, g, 9, 0] = 2.0 ** 5
            u[r, 16 * g + 8, 16 * g, 0] = 1.125 * float(k[r])
            u[r, 16 * g + 13, 16 * g, 0] = float(k[r])
    return {"x": x.reshape(N, 128, 4 * C).astype(BF), "u": u.reshape(N, 128, 512), "v": d["v"], **lists(rng), **weights(rng, w.astype(BF))}
def setup_inputs_odd(rng):
    d = numbers_of(rng)
    x = (1.0 + (2 * rng.integers(0, 64, (N, 8, 16, C, 4)) + 1) * 2.0 ** -7) * np.exp2(-rng.integers(0, 7, (N, 8, 16, C, 4)).astype(np.float64)) * rng.choice([-1.0, 1.0], (N, 8, 16, C, 4))
    x[:, :, 0, :, 0] = 1.96875 * 2.0 ** 8 * rng.choice([-1.0, 1.0], (N, 8, C))
    x[:, :, 1:3] = 0
    x[:, :, 1, :, 0] = (8 + rng.integers(0, 2, (N, 8, C))) * 2.0 ** -8
    x[:, :, 2, :, 0] = -2.0 ** -5
    a = np.exp2(rng.integers(-3, 4, (N, 8, C)).astype(np.float64))
    x[:, :, 8:] = 0
    x[:, :, 8, :, 0] = 1.125 * a
    x[:, :, 11, :, 0] = (8 + rng.integers(0, 2, (N, 8, C))) * 2.0 ** -7 * a
    x[:, :, 12, :, 0] = 2.0 ** -4 * a
    u = d["u"].reshape(N, 128, 128, 4)
    u[:, :, ::16] = 0
    for h in range(0, 128, 16):
        for i in (1, 2, 9, 10): u[:, h + i, h, 0] = 1.0
    w = layers(rng)
    w[:, :, :3] = 0
    w[:, :, :, :, :, :3] = 0
    w[:, :, :, :, :, 8:] = 0
    for g in range(8):
        w[:, g, 8, 0, g, 8, 0] = 28.0
        w[:, g, 11, 0, g, 9, 0] = 2.0 ** -5
        w[:, g, 12, 0, g, 10, 0] = -2.0 ** -5
    return {"x": x.astype(np.float32).reshape(N, 128, 4 * C).astype(BF), "u": u.reshape(N, 128, 512), "v": d["v"], **lists(rng), **weights(rng, w)}
def setup_inputs_ends(rng):
    d = numbers_of(rng)
    o, e, h = rng.permutation(N) % 4, rng.permutation(N) % 4, rng.permutation(N) % 2
    s = rng.choice([-1.0, 1.0], (N, 8, 8, C, 4))
    s[o == 0] = -1
    s[o == 1] = rng.choice([-1.0, 1.0], (N, 1, 1, C, 1))[o == 1]
    low = s * (0.9 + 0.1 * rng.random((N, 8, 8, C, 4))) * 2.0 ** 30
    low[o == 3] = s[o == 3] * 2.0 ** -30
    x = d["x"].astype(np.float32).reshape(N, 8, 16, C, 4)
    x[:, :, :8] = low
    size = np.where(o == 3, 2.0 ** -30, 2.0 ** 30)
    c = np.stack([rng.permutation(8) % 2 * 2.0 - 1.0 for r in range(N)]) * size[:, None]
    u = d["u"].reshape(N, 128, 128, 4)
    u[:, :, ::16] = c.astype(np.float32).astype(BF)[:, None, :, None]
    v = rng.choice([-1.0, 1.0], (N, 128, 512)) * size[:, None, None]
    a, b, t = [rng.integers(0, C, (N, 8, C)) for i in range(3)]
    a[e == 0], b[e == 0], t[e == 0] = C - 1, C - 1, C - 1
    a[e == 1], b[e == 1], t[e == 1] = 0, C - 1, 0
    a[e == 2], b[e == 2], t[e == 2] = C - 1 - np.arange(C), np.arange(C), (np.arange(C) + 1) % 2 * (C - 1)
    w = np.zeros((N, 128, 4, 128, 4), np.float32)
    i = np.flatnonzero(np.arange(128) % 16 >= 8)
    for k in range(4): w[:, i, k, i, k] = np.where(h == 0, 2.0 ** 8, 2.0 ** -8)[:, None] * rng.choice([-1.0, 1.0], (N, 64))
    return {"x": x.reshape(N, 128, 4 * C).astype(BF), "u": u.reshape(N, 128, 512), "v": v.astype(np.float32).astype(BF), **stored(a, b, t), **weights(rng, w.astype(BF))}
def setup_inputs_spread(rng):
    d = setup_inputs(rng)
    d["x"] = wide(rng, N, 128, 4 * C, cols=6)
    return d
def check_inputs(d):
    b = []
    for k in ("x", "u", "v"):
        a = np.abs(d[k].astype(np.float32))
        if not (np.isfinite(a).all() and ((a == 0) | (a >= 2.0 ** -30) & (a <= 2.0 ** 30)).all()): b.append("a value of " + k)
    for k in ("ta", "tb", "st"):
        if not ((d[k] >= 0) & (d[k] < C)).all(): b.append("an entry of " + k)
    none, least, most = [emit(mx_ref.quantize(np.full((128, 16), k, np.float32).astype(BF)))[1][0, 0] for k in (0.0, 2.0 ** -8, 2.0 ** 8)]
    for r in range(N):
        if ((d["wc"][r] == 0x7F) | (d["wc"][r] == 0xFF)).any(): b.append("wc: a code that is no number")
        s = mx_ref.live(d["ws"][r])
        if ((s != none) & ((s < least) | (s > most))).any(): b.append("ws: a scale out of range")
    return b
def at(t, s):
    return np.take_along_axis(t, s, axis=2)
def reference(x, u, v, ta, tb, st, wc, ws):
    qu = [mx_ref.quantize(u[r]) for r in range(N)]
    lay = [pk(wc[r], ws[r]) for r in range(N)]
    a, b, s = [np.stack([gentries(k[r]) for r in range(N)]).astype(np.int64) for k in (ta, tb, st)]
    now = [x[r] for r in range(N)]
    for step in STEP:
        q = [mx_ref.quantize(now[r]) for r in range(N)]
        bit = np.stack([mx_ref.matmul(qu[r], q[r])[::16] > 0 for r in range(N)])
        for k in range(STAGES):
            right = np.roll(at(bit, s), -1, axis=2)
            s = np.where(right, at(b, s), at(a, s))
        z = [gcols(decode(q[r]).astype(BF), s[r]) for r in range(N)]
        qz = [mx_ref.quantize(z[r]) for r in range(N)]
        made, change = [], []
        for r in range(N):
            p = r ^ step
            h = tile([mx_ref.matmul(pick(lay[r], np.arange(128 * k, 128 * k + 128)), qz[p]) * np.float32(0.03125) for k in range(4)])
            change.append(mx_ref.matmul(qu[r], mx_ref.quantize(h))[::16] > 0)
            made.append((z[r].astype(np.float32) + gcols(h, s[p]).astype(np.float32)).astype(BF))
        c = np.stack(change)
        a, b = np.where(c, b, a), np.where(c, a, b)
        now = made
    y, op = np.zeros((N, 128, C), np.float32), np.zeros((N, 8, 3 * C), np.float32)
    oc, osc = np.zeros((N, 128, 4 * C), np.uint8), np.zeros((N, 16, C), np.uint8)
    for r in range(N):
        q = mx_ref.quantize(now[r])
        y[r] = mx_ref.matmul(mx_ref.quantize(v[r]), q)
        op[r] = np.concatenate([s[r], a[r], b[r]], axis=1)
        oc[r], osc[r] = emit(q)
    return {"y": y, "op": op, "oc": oc, "osc": osc}

@@ -1,0 +1,517 @@
+from concourse.bass import DstId, RemoteDMATransfer
+from concourse.mybir import dt, AluOpType, ActivationFunctionType
+
+STEP = [4, 1, 2]
+STAGES = 7
+C = 288
+HC = C // 2
+PART = [(0, 160), (160, 288)]
+MID = 336
+K = 672
+BIG = 2.0 ** 40
+UP = 2.0 ** 36
+TINY = -2.0 ** -100
+
+SCRATCH = {"ps": ("psum", [128, 4096], "float32")}
+
+
+def _bufs(where, dtype, **cols):
+    for k in cols:
+        SCRATCH[k] = (where, [128, cols[k]], dtype)
+
+
+_bufs("sbuf", "bfloat16", xin=1152, xt1=1152, xt2=1152, xt3=1152, ut=512, vt=512, ones=512, eb=2048, tm=304, tm4=288, ma=304, mb=304,
+      mask16=304, mask4=288, enc=288, sg=288, idsg=288, cs=288, w=1344, r=320, so1=304, son=304, soc=288,
+      tt=1152, tq=1152, zt=1152, zp=1152, h=1152)
+for _n, _c in [("u", 128), ("ur", 128), ("v", 128), ("w", 512), ("e", 512), ("z", 288), ("h", 288)] + [("x%d" % _r, 288) for _r in range(4)] + [("l%d" % _r, 288) for _r in range(3)]:
+    SCRATCH["q" + _n] = ("sbuf", [128, _c], "float8_e4m3fn_x4")
+    SCRATCH["p" + _n] = ("sbuf", [128, _c], "uint8")
+_bufs("sbuf", "int32", pi=8, pk=8, offui=8, tai=18, tbi=18, sti=18)
+_bufs("sbuf", "float32", pf=8, sc16=8, kp=8, sc4=8, revf=20, idf=288, ab=36, dd=36, m2=36, c01=18, za=20, tmp=20, yy=20,
+      wl=1344, rl=304, so4=288, sol=304, opr=864, yo=288)
+_bufs("sbuf", "uint16", offu=8, rev=20, sl=20, lab=36, off=20, own0=72, own1=72, own2=72, arr0=72, arr1=72, arr2=72)
+
+DMAS = ["d%d" % _i for _i in range(20)]
+SEMAPHORES = ["cV", "cS", "cT", "cP", "left"] + ["ax%d" % _r for _r in range(3)] + ["al%d" % _r for _r in range(3)] + DMAS
+
+
+def make_tracker(g, T):
+    queues = {"V": g.vector, "S": g.scalar, "T": g.tensor, "P": g, "Y": g.sync}
+    csem = {"V": "cV", "S": "cS", "T": "cT", "P": "cP"}
+    count = {}
+    known = {q: {} for q in queues}
+    clocks = {}
+    writes, reads = {}, {}
+    ndma = [0]
+
+    def wait(q, toks):
+        best = {}
+        for s, v in toks:
+            if known[q].get(s, 0) < v:
+                best[s] = max(best.get(s, 0), v)
+        items = sorted(best.items())
+        for s, v in items:
+            if not any(o[0] != s and clocks[o].get(s, 0) >= v for o in items):
+                queues[q].wait_ge(T.sem[s], v)
+        for s, v in items:
+            for s2, v2 in clocks[(s, v)].items():
+                known[q][s2] = max(known[q].get(s2, 0), v2)
+            known[q][s] = max(known[q].get(s, 0), v)
+
+    def deps(q, rd, wr):
+        toks = []
+        for k, a, b in rd + wr:
+            toks += [t for x, y, t, oq in writes.get(k, []) if x < b and a < y]
+        for k, a, b in wr:
+            toks += [t for x, y, t, oq in reads.get(k, []) if x < b and a < y and (oq != q or k in ("w", "wl"))]
+        return toks
+
+    def note(q, rd, wr, tok):
+        for k, a, b in wr:
+            writes[k] = [e for e in writes.get(k, []) if not (a <= e[0] and e[1] <= b)] + [(a, b, tok, q)]
+            reads[k] = [e for e in reads.get(k, []) if not (a <= e[0] and e[1] <= b)]
+        for k, a, b in rd:
+            reads.setdefault(k, []).append((a, b, tok, q))
+
+    def op(q, call, rd, wr, dma=False):
+        wait(q, deps(q, rd, wr))
+        s, inc = csem.get(q), 1
+        if dma:
+            s, inc = DMAS[ndma[0]], 16
+            ndma[0] += 1
+        count[s] = count.get(s, 0) + inc
+        tok = (s, count[s])
+        call(queues[q]).then_inc(T.sem[s], inc)
+        clocks[tok] = dict(known[q])
+        clocks[tok][s] = count[s]
+        note("dma" if dma else q, rd, wr, tok)
+
+    def arrival(s, v, wr):
+        clocks[(s, v)] = {s: v}
+        count[s] = v
+        note("net", [], wr, (s, v))
+
+    def before(q, rd):
+        wait(q, deps(q, rd, []))
+
+    def finish():
+        for s in sorted(count):
+            g.wait_ge(T.sem[s], count[s])
+
+    return op, arrival, before, finish, count
+
+
+def rank_program(g, core, T, topo):
+    rank = T.rank_of(core)
+    if rank is None:
+        return
+    A = AluOpType
+    F = ActivationFunctionType
+    op, arrival, before, finish, count = make_tracker(g, T)
+
+    def R(k, a=0, b=100000):
+        return (k, a, b)
+
+    def lanes(k, a=0, b=C):
+        return [(k + "_" + str(t), a, b) for t in range(4)]
+
+    def V(call, rd, wr):
+        op("V", call, rd, wr)
+
+    def S(call, rd, wr):
+        op("S", call, rd, wr)
+
+    def ap(x):
+        if not isinstance(x, tuple):
+            return x
+        return T[x[0]][:, x[1]:x[2]:x[3]] if len(x) > 3 else T[x[0]][:, x[1]:x[2]]
+
+    def rgs(*xs):
+        return [(x[0], x[1], x[2]) for x in xs if isinstance(x, tuple)]
+
+    def ts(out, in0, s1, s2, *ops):
+        V(lambda e: e.tensor_scalar(ap(out), ap(in0), ap(s1), ap(s2), *ops), rgs(in0, s1, s2), rgs(out))
+
+    def tt(out, in0, in1, o):
+        V(lambda e: e.tensor_tensor(ap(out), ap(in0), ap(in1), o), rgs(in0, in1), rgs(out))
+
+    def cp(out, in_):
+        V(lambda e: e.tensor_copy(ap(out), ap(in_)), rgs(in_), rgs(out))
+
+    def act(out, in_, fn, **k):
+        S(lambda e: e.activation(ap(out), ap(in_), fn, **{x: ap(k[x]) for x in k}), rgs(in_, *k.values()), rgs(out))
+
+    def gather(q, out, win, off, wr=None, rd=None):
+        rr, ww = rgs(off) + (rd if rd else rgs(win)), wr if wr else rgs(out)
+        if q == "V":
+            V(lambda e: e.tensor_copy(ap(out), ap(win).indirect(ap(off))), rr, ww)
+        else:
+            S(lambda e: e.activation(ap(out), ap(win).indirect(ap(off)), F.Copy), rr, ww)
+
+    def iota(out, pat, base, cm, flag=True):
+        if flag:
+            op("P", lambda e: e.iota(ap(out), pat, base, cm, allow_small_or_imprecise_dtypes=True), [], rgs(out))
+        else:
+            op("P", lambda e: e.iota(ap(out), pat, base, cm), [], rgs(out))
+
+    def quant(q, a, b, src, rd):
+        V(lambda e: e.quantize_mx(T["q" + q][:, a:b], T["p" + q][:, a:b], T[src][:, 4 * a:4 * b]), rd, [R("q" + q, a, b)])
+
+    def load(q, dst, src, key, a=0, b=100000):
+        op(q, lambda e: e.dma_start(dst, src), [], [(key, a, b)], dma=True)
+
+    def load_x(a, b):
+        load("Y", T.xin[:, 4 * a:4 * b], T.x[:, 4 * a:4 * b], "xin", a, b)
+    load_x(*PART[0])
+    load("S", T.ut[:, :], T.u[:, :], "ut")
+    load_x(*PART[1])
+    load("Y", T.sti[:, :], T.st[:, :], "sti")
+    load("S", T.tai[:, :], T.ta[:, :], "tai")
+    load("S", T.tbi[:, :], T.tb[:, :], "tbi")
+    load("Y", T.qw[:, :].bitcast(dt.uint8), T.wc[:, :], "qw")
+    load("Y", T.pw[:, :], T.ws[:, :], "pw")
+    load("Y", T.vt[:, :], T.v[:, :], "vt")
+
+    def unpacker(b):
+        op("P", lambda e: e.affine_select(T.eb[:, 512 * b:512 * b + 512], T.ones[:, :], [[1, 512]], A.is_equal, 0.0, -b, -4), [R("ones", 0, 512)], [R("eb", b, b + 1)])
+
+    iota(("pi", 0, 5), [[1, 5]], 0, 1, False)
+    iota(("offui", 0, 8), [[16, 8]], 0, 0, False)
+    iota(("tm", 0, 304), [[0, 19], [1, 16]], 0, 0)
+    iota(("revf", 0, 20), [[-16, 20]], 320, 0)
+    iota(("enc", 0, 256), [[1, 256]], 1, 0)
+    iota(("enc", 256, 288), [[2, 32]], 258, 0)
+    iota(("tm4", 0, 288), [[0, 72], [1, 4]], 0, 0)
+
+    def fill(win, a, b):
+        act((win, a, b), ("ones", 0, b - a), F.Copy)
+
+    V(lambda e: e.memset(T.ones[:, :], 1.0), [], [R("ones", 0, 512)])
+    V(lambda e: e.memset(T.r[:, 304:320], 1.0), [], [R("r", 304, 320)])
+    for a in (0, 448, 896):
+        fill("w", a, a + 448)
+    unpacker(0)
+    unpacker(1)
+    for j, (src, sh, an) in enumerate([(0, 0, 15), (1, 0, 15), (0, 2, 3), (0, 0, 3)]):
+        if sh:
+            ts(("pk", j, j + 1), ("pi", src, src + 1), sh, an, A.arith_shift_right, A.bitwise_and)
+        else:
+            ts(("pk", j, j + 1), ("pi", src, src + 1), an, None, A.bitwise_and)
+    cp(("offu", 0, 8), ("offui", 0, 8))
+    cp(("pf", 0, 4), ("pk", 0, 4))
+    p16, q16, p4, t4 = [("pf", j, j + 1) for j in range(4)]
+    ts(("ma", 0, 304), ("tm", 0, 304), q16, BIG, A.is_equal, A.mult)
+    ts(("mb", 0, 304), ("tm", 0, 304), p16, None, A.not_equal)
+    ts(("sc16", 0, 1), p16, 15.0, 1.0 / BIG, A.is_equal, A.max)
+    ts(("kp", 1, 2), p16, 15.0, K * BIG, A.not_equal, A.mult)
+    tt(("mask16", 0, 304), ("ma", 0, 304), ("mb", 0, 304), A.max)
+    ts(("revf", 0, 20), ("revf", 0, 20), p16, None, A.subtract)
+    ts(("kp", 0, 1), ("kp", 1, 2), float(K), None, A.max)
+    quant("u", 0, 128, "ut", [R("ut")])
+    cp(("rev", 0, 20), ("revf", 0, 20))
+    V(lambda e: e.tensor_copy(T.qur[:, 0:128].bitcast(dt.uint32), T.qu[:, 0:128].bitcast(dt.uint32).indirect(T.offu[:, 0:8])), [R("qu"), R("offu")], [R("qur", 0, 1)])
+    S(lambda e: e.activation(T.pur[:, 0:128], T.pu[:, 0:128].indirect(T.offu[:, 0:8]), F.Copy), [R("qu"), R("offu")], [R("qur", 1, 2)])
+
+    def quant_x(r, hf):
+        src = "xt%d" % r if r else "xin"
+        a, b = PART[hf]
+        quant("x%d" % r, a, b, src, [R(src, a, b)])
+
+    def bank(i, n):
+        return T.ps[:, 512 * i:512 * i + n]
+
+    def mm(i, st, sa, stk, mv, a, b):
+        op("T", lambda e: e.matmul_mx(bank(i, b - a), T["q" + st][:, sa:sa + 128], T["p" + st][:, sa:sa + 128], T["q" + mv][:, a:b], T["p" + mv][:, a:b], True, True),
+           stk + [R("q" + mv, a, b)], [R("B%d" % i)])
+
+    ukeys = [R("qur", 0, 2)]
+
+    def score_part(r, hf):
+        a, b = PART[hf]
+        mm(hf, "ur", 0, ukeys, "x%d" % r, a, b)
+        S(lambda e: e.activation(T.sg[:, a:b], bank(hf, b - a), F.Sign, bias=TINY), [R("B%d" % hf)], [R("sg", a, b)])
+
+    def idsg_part(hf):
+        a, b = PART[hf]
+        tt(("idsg", a, b), ("sg", a, b), ("enc", a, b), A.mult)
+
+    def scan(out, mask, row):
+        V(lambda e: e.tensor_tensor_scan(ap(out), ap(mask), ap(row), 0.0, A.mult, A.add), rgs(mask, row), rgs(out))
+
+    def table(q, dst, src, first, c, d):
+        m, o = (MID, 0) if first else (MID + K, 18)
+        if c == 16:
+            gather(q, (dst, m + 258, m + 321, 2), (src, 0, C), ("lab", o + c, o + d))
+        else:
+            gather(q, (dst, m + 1 + 16 * c, m + 1 + 16 * d), (src, 0, C), ("lab", o + c, o + d))
+
+    def mirror(win, first):
+        m = MID if first else MID + K
+        gather("S", (win, m - 320, m), (win, m, m + 336), ("rev", 0, 20))
+
+    VC = 10
+
+    def stage_gather(t):
+        row, win, off = "r", ("w", 0, 2 * K), "off"
+        if t == 0:
+            win, off = ("idsg", 0, C), "sl"
+        elif t == STAGES:
+            row, win = "rl", ("wl", 0, 2 * K)
+        gather("V", (row, 0, 16 * VC), win, (off, 0, VC))
+        gather("S", (row, 16 * VC, 304), win, (off, VC, 19))
+
+    M16, M4, SC16, SC4 = ("mask16", 0, 304), ("mask4", 0, 288), ("sc16", 0, 1), ("sc4", 4, 5)
+
+    def own_scan():
+        scan(("so1", 0, 304), M16, ("r", 0, 304))
+
+    def next_scan():
+        scan(("son", 0, 304), M16, ("r", 1, 305))
+
+    def nothing():
+        pass
+
+    def unsigned_list(scalar=nothing, vector=nothing, between=nothing):
+        own_scan()
+        next_scan()
+        scalar()
+        act(("za", 0, 19), ("so1", 15, 304, 16), F.Abs, scale=SC16)
+        vector()
+        ts(("tmp", 0, 19), ("son", 15, 304, 16), 0.0, float(K), A.is_gt, A.mult)
+        between()
+        tt(("yy", 0, 19), ("za", 0, 19), ("tmp", 0, 19), A.add)
+
+    def unsigned_end():
+        ts(("off", 0, 19), ("yy", 0, 19), float(MID), None, A.add)
+
+    def signed_list(between=nothing):
+        next_scan()
+        own_scan()
+        ts(("tmp", 0, 19), ("son", 15, 304, 16), 0.0, ("kp", 0, 1), A.is_gt, A.mult)
+        between()
+        tt(("yy", 0, 19), ("so1", 15, 304, 16), ("tmp", 0, 19), A.add)
+        ts(("off", 0, 19), ("yy", 0, 19), SC16, float(MID), A.mult, A.add)
+
+    def unpack_lane(mv, i, b):
+        mm(i, "e", 128 * b, [R("qe", 128 * b, 128 * b + 128)], mv, 0, C)
+
+    def piece(q, buf, i, b, hf):
+        a = hf * HC
+        out, src = T[buf][:, 4 * a + b:4 * (a + HC):4], T.ps[:, 512 * i + a:512 * i + a + HC]
+        rd, wr = [R("B%d" % i)], [(buf + "_" + str(b), a, a + HC)]
+        if q == "V":
+            V(lambda e: e.tensor_copy(out, src), rd, wr)
+        else:
+            S(lambda e: e.activation(out, src, F.Copy), rd, wr)
+
+    cp(("sl", 0, 18), ("sti", 0, 18))
+    cp(("sl", 18, 19), ("sti", 0, 1))
+    quant_x(0, 0)
+    quant_x(0, 1)
+    score_part(0, 0)
+    score_part(0, 1)
+    cp(("lab", 0, 18), ("tai", 0, 18))
+    cp(("lab", 18, 36), ("tbi", 0, 18))
+    idsg_part(0)
+    idsg_part(1)
+
+    def sc4_factor(k):
+        ts(("sc4", k, k + 1), p4, k + 1.0, 1.0 / UP, A.is_ge, A.max)
+
+    def later(t):
+        if t == 2:
+            ts(M4, ("tm4", 0, 288), p4, UP, A.not_equal, A.mult)
+        elif t == 3:
+            sc4_factor(0)
+            sc4_factor(1)
+        elif t == 4:
+            sc4_factor(2)
+            tt(("sc4", 3, 4), ("sc4", 0, 1), ("sc4", 1, 2), A.mult)
+        elif t == 5:
+            ts(SC4, ("sc4", 3, 4), ("sc4", 2, 3), 4.0, A.mult, A.mult)
+
+    def differences():
+        tt(("dd", 0, 18), ("ab", 18, 36), ("ab", 0, 18), A.subtract)
+        tt(("dd", 18, 36), ("ab", 0, 18), ("ab", 18, 36), A.subtract)
+
+    for r in range(3):
+        partner = T.cores[rank ^ STEP[r]]
+        rid, pid = topo.addr(partner, core)
+        engines = topo.engines(core, partner)[:8]
+        mask = sum(1 << e for e in engines)
+        ne = len(engines)
+        qx, lx, own, arr = "x%d" % r, "l%d" % r, "own%d" % r, "arr%d" % r
+        own_t, got_t = [2, 3, 4, 5], [6, 7, 0, 1]
+
+        before("P", [R("q" + qx)])
+        g.remote_dma(T["q" + lx][:, :].bitcast(dt.uint8), T["q" + qx][:, :].bitcast(dt.uint8), T.sem["ax%d" % r], T.sem.left, pid, rid, mask)
+        g.remote_dma(T["p" + lx][:, :], T["p" + qx][:, :], T.sem["ax%d" % r], T.sem.left, pid, rid, mask)
+        count["left"] = count.get("left", 0) + 2 * ne
+        arrival("ax%d" % r, 2 * ne, [R("q" + lx)])
+        arrival("al%d" % r, ne, [R(arr)])
+        if r == 0:
+            iota(("idf", 0, 288), [[1, 288]], 0, 0)
+            unpacker(2)
+            unpacker(3)
+
+        def tails():
+            table("S", "w", "idsg", True, 16, 18)
+            table("S", "w", "idsg", False, 16, 18)
+        stage_gather(0)
+        unsigned_list(tails, lambda: table("V", "w", "idsg", False, 0, 6))
+        table("S", "w", "idsg", True, 0, 16)
+        table("S", "w", "idsg", False, 12, 16)
+        table("V", "w", "idsg", False, 6, 12)
+        unsigned_end()
+        if r:
+            for b in range(4):
+                unpack_lane(qx, own_t[b], b)
+            for b in range(4):
+                unpack_lane(lx, got_t[b], b)
+        own_p = [(b, hf) for b in range(4) for hf in range(2)]
+
+        def own_pieces(n):
+            for i in range(n):
+                b, hf = own_p.pop(0)
+                piece("S", "tt", own_t[b], b, hf)
+
+        def plain_tails():
+            table("S", "wl", "idf", True, 16, 18)
+            table("S", "wl", "idf", False, 16, 18)
+
+        for t in range(1, STAGES):
+            stage_gather(t)
+            mine = nothing
+            if r == 0:
+                mine = lambda: later(t)
+                if t == 1:
+                    cp(("ab", 0, 18), ("tai", 0, 18))
+                    cp(("ab", 18, 36), ("tbi", 0, 18))
+                elif t <= 5:
+                    b = t - 2
+                    quant("e", 128 * b, 128 * b + 128, "eb", [R("eb", b, b + 1)])
+                    unpack_lane(qx, own_t[b], b)
+                    if b == 3:
+                        for b in range(4):
+                            unpack_lane(lx, got_t[b], b)
+            if t == 1:
+                unsigned_list(nothing if r else lambda: fill("wl", 0, 336))
+                unsigned_end()
+                mirror("w", True)
+            elif t == 2:
+                mirror("w", False)
+                if r == 0:
+                    fill("wl", 336, 672)
+                signed_list(mine)
+                differences()
+            elif t == 6 and r == 0:
+                unsigned_list(lambda: own_pieces(2))
+                own_pieces(2)
+                unsigned_end()
+            else:
+                if t < 5:
+                    if r == 0:
+                        fill("wl", 336 * t - 336, 336 * t)
+                    table("S", "wl", "idf", t == 3, 0, 16)
+                elif r:
+                    mirror("wl", t == 5)
+                if t == (4 if r else 5):
+                    plain_tails()
+                if t == 5 or r and t != 4:
+                    own_pieces(2)
+                signed_list(mine)
+        stage_gather(STAGES)
+        own_pieces(2)
+        scan(("so4", 0, 288), M4, ("rl", 0, 288))
+        ts((own, 0, 72), ("so4", 3, 288, 4), SC4, t4, A.mult, A.add)
+        before("P", [R(own)])
+        g.remote_dma(T[arr][:, :], T[own][:, :], T.sem["al%d" % r], T.sem.left, pid, rid, mask)
+        count["left"] += ne
+
+        gather("S", ("zt", 576, 1152), ("tt", 0, 1152), (own, 36, 72), [R("zt", HC, C)], lanes("tt"))
+        scan(("sol", 0, 304), M16, ("rl", 0, 304))
+        gather("V", ("zt", 0, 576), ("tt", 0, 1152), (own, 0, 36), [R("zt", 0, HC)], lanes("tt"))
+        ts(("sl", 0, 18), ("sol", 15, 288, 16), SC16, None, A.mult)
+        ts(("sl", 18, 19), ("sol", 15, 16), SC16, None, A.mult)
+        for hf in range(2):
+            for b in (0, 1):
+                piece("S", "tq", got_t[b], b, hf)
+                piece("V", "tq", got_t[b + 2], b + 2, hf)
+        if r == 0:
+            quant("v", 0, 128, "vt", [R("vt")])
+
+        for hf in range(2):
+            a, b = PART[hf]
+            m = (a + b) // 2
+            gather("V", ("zp", 4 * a, 4 * m), ("tq", 0, 1152), (arr, a // 4, m // 4), [R("zp", a, m)], lanes("tq"))
+            gather("S", ("zp", 4 * m, 4 * b), ("tq", 0, 1152), (arr, m // 4, b // 4), [R("zp", m, b)], lanes("tq"))
+            quant("z", a, b, "zp", [R("zp", a, b)])
+            for k in (0, 2, 1, 3):
+                mm(4 * hf + k, "w", 128 * k, [R("qw"), R("pw")], "z", a, b)
+        for hf in range(2):
+            a, b = PART[hf]
+            for k in (0, 2, 1, 3):
+                i = 4 * hf + k
+                out, wr = T.h[:, 4 * a + k:4 * b:4], [("h_%d" % k, a, b)]
+                if k < 2:
+                    V(lambda e: e.tensor_scalar(out, bank(i, b - a), 0.03125, None, A.mult), [R("B%d" % i)], wr)
+                else:
+                    S(lambda e: e.activation(out, bank(i, b - a), F.Copy, scale=0.03125), [R("B%d" % i)], wr)
+
+        xt, last = "xt%d" % (r + 1), r == 2
+
+        def new_part(hf):
+            a, b = PART[hf]
+            V(lambda e: e.tensor_tensor(T[xt][:, 4 * a:4 * b], T.h[:, 0:1152].indirect(T[arr][:, a // 4:b // 4]), T.zt[:, 4 * a:4 * b], A.add),
+              lanes("h") + [R(arr), R("zt", a, b)], [R(xt, a, b)])
+
+        def change_scan():
+            scan(("soc", 0, 288), ("mask16", 0, 288), ("cs", 0, 288))
+
+        def change():
+            ts(("c01", 0, 18), ("soc", 15, 288, 16), 0.0, None, A.is_gt)
+        if not last:
+            new_part(0)
+        quant("h", 0, C, "h", lanes("h"))
+        mm(2, "ur", 0, ukeys, "h", 0, C)
+        S(lambda e: e.activation(T.cs[:, :], bank(2, C), F.Sign, bias=TINY), [R("B2")], [R("cs", 0, C)])
+        if last:
+            new_part(0)
+            change_scan()
+        quant_x(r + 1, 0)
+        if last:
+            change()
+            new_part(1)
+        else:
+            score_part(r + 1, 0)
+            new_part(1)
+            change_scan()
+            quant_x(r + 1, 1)
+            change()
+            score_part(r + 1, 1)
+            idsg_part(0)
+        tt(("m2", 0, 18), ("dd", 0, 18), ("c01", 0, 18), A.mult)
+        tt(("m2", 18, 36), ("dd", 18, 36), ("c01", 0, 18), A.mult)
+        if last:
+            quant_x(r + 1, 1)
+        tt(("ab", 0, 36), ("ab", 0, 36), ("m2", 0, 36), A.add)
+        if not last:
+            idsg_part(1)
+        cp(("lab", 0, 36), ("ab", 0, 36))
+
+    def out(q, dst, src, rd):
+        op(q, lambda e: e.dma_start(dst, src), rd, [], dma=True)
+    for hf in range(2):
+        mm(3 + hf, "v", 0, [R("qv")], "x3", *PART[hf])
+    out("Y", T.oc[:, :], T.qx3[:, :].bitcast(dt.uint8), [R("qx3")])
+    gather("S", ("opr", 0, C), ("idf", 0, C), ("sl", 0, 18))
+    for hf in range(2):
+        a, b = PART[hf]
+        V(lambda e: e.tensor_copy(T.yo[:, a:b], bank(3 + hf, b - a)), [R("B%d" % (3 + hf))], [R("yo", a, b)])
+    gather("V", ("opr", C, 2 * C), ("idf", 0, C), ("lab", 0, 18))
+    gather("S", ("opr", 2 * C, 3 * C), ("idf", 0, C), ("lab", 18, 36))
+    out("Y", T.y[:, :], T.yo[:, :], [R("yo")])
+    for k in range(4):
+        out("S" if k % 2 else "Y", T.osc[4 * k:4 * k + 4, :], T.px3[32 * k:32 * k + 4, :], [R("qx3")])
+    out("S", T.op[:, :], T.opr[0:128:16, :], [R("opr")])
+    finish()

@@ -4,13 +4,16 @@ from concourse.mybir import dt, AluOpType, ActivationFunctionType
 STEP = [4, 1, 2]
 STAGES = 7
 C = 288
-HC = C // 2
 PART = [(0, 160), (160, 288)]
-MID = 336
-K = 672
+COLS = 18 + STAGES
+CHUNK = [(0, 9), (9, 15), (15, 21), (21, 25)]
+AT = [0, 10, 16, 22]
+MID = 576
 BIG = 2.0 ** 40
-UP = 2.0 ** 36
+CARRY = 6000.0
+BASE = 2047 * CARRY + 1024
 TINY = -2.0 ** -100
+OPT = {"fill": [0, 2], "fill0": [0, 2], "early": 3, "early0": 0, "mir": "VVVV", "mat": [0, 0, 0, 1], "ga": 10, "gb": 18, "zv": [80, 64]}
 
 SCRATCH = {"ps": ("psum", [128, 4096], "float32")}
 
@@ -20,16 +23,16 @@ def _bufs(where, dtype, **cols):
         SCRATCH[k] = (where, [128, cols[k]], dtype)
 
 
-_bufs("sbuf", "bfloat16", xin=1152, xt1=1152, xt2=1152, xt3=1152, ut=512, vt=512, ones=512, eb=2048, tm=304, tm4=288, ma=304, mb=304,
-      mask16=304, mask4=288, enc=288, sg=288, idsg=288, cs=288, w=1344, r=320, so1=304, son=304, soc=288,
+_bufs("sbuf", "bfloat16", xin=1152, xt1=1152, xt2=1152, xt3=1152, ut=512, vt=512, ones=516, eb=516, tm=16, ma=32, mb=32, m16=32,
+      pure=400, chain=400, mask4=288, sg=288, cs=288, r0=400, so0=400, soc=288,
       tt=1152, tq=1152, zt=1152, zp=1152, h=1152)
 for _n, _c in [("u", 128), ("ur", 128), ("v", 128), ("w", 512), ("e", 512), ("z", 288), ("h", 288)] + [("x%d" % _r, 288) for _r in range(4)] + [("l%d" % _r, 288) for _r in range(3)]:
     SCRATCH["q" + _n] = ("sbuf", [128, _c], "float8_e4m3fn_x4")
     SCRATCH["p" + _n] = ("sbuf", [128, _c], "uint8")
 _bufs("sbuf", "int32", pi=8, pk=8, offui=8, tai=18, tbi=18, sti=18)
-_bufs("sbuf", "float32", pf=8, sc16=8, kp=8, sc4=8, revf=20, idf=288, ab=36, dd=36, m2=36, c01=18, za=20, tmp=20, yy=20,
-      wl=1344, rl=304, so4=288, sol=304, opr=864, yo=288)
-_bufs("sbuf", "uint16", offu=8, rev=20, sl=20, lab=36, off=20, own0=72, own1=72, own2=72, arr0=72, arr1=72, arr2=72)
+_bufs("sbuf", "float32", pf=8, sc=8, enc=288, idf=288, lam=288, val=288, ab=36, dd=36, m2=36, c01=18, yy=26, ca=26, cb=8,
+      w=1160, r=400, so=480, rn=288, so4=288, sol=400, opr=864, yo=288)
+_bufs("sbuf", "uint16", offu=8, l16=26, l4=18, order=18, halo=26, ahead=8, sn=18, sl=28, lab=36, off=28, own0=72, own1=72, own2=72, arr0=72, arr1=72, arr2=72)
 
 DMAS = ["d%d" % _i for _i in range(20)]
 SEMAPHORES = ["cV", "cS", "cT", "cP", "left"] + ["ax%d" % _r for _r in range(3)] + ["al%d" % _r for _r in range(3)] + DMAS
@@ -43,6 +46,11 @@ def make_tracker(g, T):
     clocks = {}
     writes, reads = {}, {}
     ndma = [0]
+
+    def cols(x):
+        if x[0] == "ps":
+            return frozenset(range(x[1] // 512, (x[2] - 1) // 512 + 1))
+        return frozenset(range(*x[1:]))
 
     def wait(q, toks):
         best = {}
@@ -60,20 +68,21 @@ def make_tracker(g, T):
 
     def deps(q, rd, wr):
         toks = []
-        for k, a, b in rd + wr:
-            toks += [t for x, y, t, oq in writes.get(k, []) if x < b and a < y]
-        for k, a, b in wr:
-            toks += [t for x, y, t, oq in reads.get(k, []) if x < b and a < y and (oq != q or k in ("w", "wl"))]
+        for x in rd + wr:
+            toks += [t for c, t in writes.get(x[0], []) if c & cols(x)]
+        for x in wr + [x for x in rd if x[0] == "ps"]:
+            toks += [t for c, t, oq in reads.get(x[0], []) if c & cols(x) and oq != q]
         return toks
 
     def note(q, rd, wr, tok):
-        for k, a, b in wr:
-            writes[k] = [e for e in writes.get(k, []) if not (a <= e[0] and e[1] <= b)] + [(a, b, tok, q)]
-            reads[k] = [e for e in reads.get(k, []) if not (a <= e[0] and e[1] <= b)]
-        for k, a, b in rd:
-            reads.setdefault(k, []).append((a, b, tok, q))
+        for x in wr:
+            k, c = x[0], cols(x)
+            writes[k] = [e for e in writes.get(k, []) if not e[0] <= c] + [(c, tok)]
+            reads[k] = [e for e in reads.get(k, []) if not e[0] <= c]
+        for x in rd:
+            reads.setdefault(x[0], []).append((cols(x), tok, q))
 
-    def op(q, call, rd, wr, dma=False):
+    def op(q, call, rd, wr, dma=False, listed=False):
         wait(q, deps(q, rd, wr))
         s, inc = csem.get(q), 1
         if dma:
@@ -84,12 +93,12 @@ def make_tracker(g, T):
         call(queues[q]).then_inc(T.sem[s], inc)
         clocks[tok] = dict(known[q])
         clocks[tok][s] = count[s]
-        note("dma" if dma else q, rd, wr, tok)
+        note("any" if dma or listed else q, rd, wr, tok)
 
     def arrival(s, v, wr):
         clocks[(s, v)] = {s: v}
         count[s] = v
-        note("net", [], wr, (s, v))
+        note("any", [], wr, (s, v))
 
     def before(q, rd):
         wait(q, deps(q, rd, []))
@@ -109,409 +118,413 @@ def rank_program(g, core, T, topo):
     F = ActivationFunctionType
     op, arrival, before, finish, count = make_tracker(g, T)
 
-    def R(k, a=0, b=100000):
-        return (k, a, b)
-
-    def lanes(k, a=0, b=C):
-        return [(k + "_" + str(t), a, b) for t in range(4)]
-
-    def V(call, rd, wr):
-        op("V", call, rd, wr)
-
-    def S(call, rd, wr):
-        op("S", call, rd, wr)
-
     def ap(x):
         if not isinstance(x, tuple):
             return x
         return T[x[0]][:, x[1]:x[2]:x[3]] if len(x) > 3 else T[x[0]][:, x[1]:x[2]]
 
     def rgs(*xs):
-        return [(x[0], x[1], x[2]) for x in xs if isinstance(x, tuple)]
+        return [x for x in xs if isinstance(x, tuple)]
 
     def ts(out, in0, s1, s2, *ops):
-        V(lambda e: e.tensor_scalar(ap(out), ap(in0), ap(s1), ap(s2), *ops), rgs(in0, s1, s2), rgs(out))
+        op("V", lambda e: e.tensor_scalar(ap(out), ap(in0), ap(s1), ap(s2), *ops), rgs(in0, s1, s2), [out])
 
     def tt(out, in0, in1, o):
-        V(lambda e: e.tensor_tensor(ap(out), ap(in0), ap(in1), o), rgs(in0, in1), rgs(out))
+        op("V", lambda e: e.tensor_tensor(ap(out), ap(in0), ap(in1), o), [in0, in1], [out])
 
     def cp(out, in_):
-        V(lambda e: e.tensor_copy(ap(out), ap(in_)), rgs(in_), rgs(out))
+        op("V", lambda e: e.tensor_copy(ap(out), ap(in_)), [in_], [out])
+
+    def fill(out, c):
+        op("V", lambda e: e.memset(ap(out), c), [], [out])
 
     def act(out, in_, fn, **k):
-        S(lambda e: e.activation(ap(out), ap(in_), fn, **{x: ap(k[x]) for x in k}), rgs(in_, *k.values()), rgs(out))
+        op("S", lambda e: e.activation(ap(out), ap(in_), fn, **{x: ap(k[x]) for x in k}), rgs(in_, *k.values()), [out])
 
-    def gather(q, out, win, off, wr=None, rd=None):
-        rr, ww = rgs(off) + (rd if rd else rgs(win)), wr if wr else rgs(out)
-        if q == "V":
-            V(lambda e: e.tensor_copy(ap(out), ap(win).indirect(ap(off))), rr, ww)
+    def move(q, out, in_, scale=None):
+        if q == "S":
+            act(out, in_, F.Copy, **({"scale": scale} if scale else {}))
+        elif scale:
+            ts(out, in_, scale, None, A.mult)
         else:
-            S(lambda e: e.activation(ap(out), ap(win).indirect(ap(off)), F.Copy), rr, ww)
+            cp(out, in_)
+
+    def gather(q, out, win, off, add=None, scale=None, fn=None):
+        src = ap(win).indirect(ap(off))
+        if q == "S":
+            k = {"bias": add} if add else {"scale": scale} if scale else {}
+            call = lambda e: e.activation(ap(out), src, fn if fn else F.Identity if add else F.Copy, **k)
+        elif add or scale:
+            call = lambda e: e.tensor_scalar(ap(out), src, add if add else scale, None, A.add if add else A.mult)
+        else:
+            call = lambda e: e.tensor_copy(ap(out), src)
+        op(q, call, [win, off], [out], listed=True)
 
     def iota(out, pat, base, cm, flag=True):
         if flag:
-            op("P", lambda e: e.iota(ap(out), pat, base, cm, allow_small_or_imprecise_dtypes=True), [], rgs(out))
+            op("P", lambda e: e.iota(ap(out), pat, base, cm, allow_small_or_imprecise_dtypes=True), [], [out])
         else:
-            op("P", lambda e: e.iota(ap(out), pat, base, cm), [], rgs(out))
+            op("P", lambda e: e.iota(ap(out), pat, base, cm), [], [out])
 
-    def quant(q, a, b, src, rd):
-        V(lambda e: e.quantize_mx(T["q" + q][:, a:b], T["p" + q][:, a:b], T[src][:, 4 * a:4 * b]), rd, [R("q" + q, a, b)])
+    def scan(out, mask, row, first=0.0):
+        op("V", lambda e: e.tensor_tensor_scan(ap(out), ap(mask), ap(row), ap(first), A.mult, A.add), rgs(mask, row, first), [out])
 
-    def load(q, dst, src, key, a=0, b=100000):
-        op(q, lambda e: e.dma_start(dst, src), [], [(key, a, b)], dma=True)
-
-    def load_x(a, b):
-        load("Y", T.xin[:, 4 * a:4 * b], T.x[:, 4 * a:4 * b], "xin", a, b)
-    load_x(*PART[0])
-    load("S", T.ut[:, :], T.u[:, :], "ut")
-    load_x(*PART[1])
-    load("Y", T.sti[:, :], T.st[:, :], "sti")
-    load("S", T.tai[:, :], T.ta[:, :], "tai")
-    load("S", T.tbi[:, :], T.tb[:, :], "tbi")
-    load("Y", T.qw[:, :].bitcast(dt.uint8), T.wc[:, :], "qw")
-    load("Y", T.pw[:, :], T.ws[:, :], "pw")
-    load("Y", T.vt[:, :], T.v[:, :], "vt")
-
-    def unpacker(b):
-        op("P", lambda e: e.affine_select(T.eb[:, 512 * b:512 * b + 512], T.ones[:, :], [[1, 512]], A.is_equal, 0.0, -b, -4), [R("ones", 0, 512)], [R("eb", b, b + 1)])
-
-    iota(("pi", 0, 5), [[1, 5]], 0, 1, False)
-    iota(("offui", 0, 8), [[16, 8]], 0, 0, False)
-    iota(("tm", 0, 304), [[0, 19], [1, 16]], 0, 0)
-    iota(("revf", 0, 20), [[-16, 20]], 320, 0)
-    iota(("enc", 0, 256), [[1, 256]], 1, 0)
-    iota(("enc", 256, 288), [[2, 32]], 258, 0)
-    iota(("tm4", 0, 288), [[0, 72], [1, 4]], 0, 0)
-
-    def fill(win, a, b):
-        act((win, a, b), ("ones", 0, b - a), F.Copy)
-
-    V(lambda e: e.memset(T.ones[:, :], 1.0), [], [R("ones", 0, 512)])
-    V(lambda e: e.memset(T.r[:, 304:320], 1.0), [], [R("r", 304, 320)])
-    for a in (0, 448, 896):
-        fill("w", a, a + 448)
-    unpacker(0)
-    unpacker(1)
-    for j, (src, sh, an) in enumerate([(0, 0, 15), (1, 0, 15), (0, 2, 3), (0, 0, 3)]):
-        if sh:
-            ts(("pk", j, j + 1), ("pi", src, src + 1), sh, an, A.arith_shift_right, A.bitwise_and)
-        else:
-            ts(("pk", j, j + 1), ("pi", src, src + 1), an, None, A.bitwise_and)
-    cp(("offu", 0, 8), ("offui", 0, 8))
-    cp(("pf", 0, 4), ("pk", 0, 4))
-    p16, q16, p4, t4 = [("pf", j, j + 1) for j in range(4)]
-    ts(("ma", 0, 304), ("tm", 0, 304), q16, BIG, A.is_equal, A.mult)
-    ts(("mb", 0, 304), ("tm", 0, 304), p16, None, A.not_equal)
-    ts(("sc16", 0, 1), p16, 15.0, 1.0 / BIG, A.is_equal, A.max)
-    ts(("kp", 1, 2), p16, 15.0, K * BIG, A.not_equal, A.mult)
-    tt(("mask16", 0, 304), ("ma", 0, 304), ("mb", 0, 304), A.max)
-    ts(("revf", 0, 20), ("revf", 0, 20), p16, None, A.subtract)
-    ts(("kp", 0, 1), ("kp", 1, 2), float(K), None, A.max)
-    quant("u", 0, 128, "ut", [R("ut")])
-    cp(("rev", 0, 20), ("revf", 0, 20))
-    V(lambda e: e.tensor_copy(T.qur[:, 0:128].bitcast(dt.uint32), T.qu[:, 0:128].bitcast(dt.uint32).indirect(T.offu[:, 0:8])), [R("qu"), R("offu")], [R("qur", 0, 1)])
-    S(lambda e: e.activation(T.pur[:, 0:128], T.pu[:, 0:128].indirect(T.offu[:, 0:8]), F.Copy), [R("qu"), R("offu")], [R("qur", 1, 2)])
-
-    def quant_x(r, hf):
-        src = "xt%d" % r if r else "xin"
-        a, b = PART[hf]
-        quant("x%d" % r, a, b, src, [R(src, a, b)])
+    def quant(q, a, b, src, at=None):
+        x = (src, 4 * a, 4 * b) if at is None else (src, at, at + 4 * (b - a))
+        op("V", lambda e: e.quantize_mx(T["q" + q][:, a:b], T["p" + q][:, a:b], ap(x)), [x], [("q" + q, a, b)])
 
     def bank(i, n):
-        return T.ps[:, 512 * i:512 * i + n]
+        return ("ps", 512 * i, 512 * i + n)
 
-    def mm(i, st, sa, stk, mv, a, b):
-        op("T", lambda e: e.matmul_mx(bank(i, b - a), T["q" + st][:, sa:sa + 128], T["p" + st][:, sa:sa + 128], T["q" + mv][:, a:b], T["p" + mv][:, a:b], True, True),
-           stk + [R("q" + mv, a, b)], [R("B%d" % i)])
+    def mm(i, st, sa, mv, a, b):
+        op("T", lambda e: e.matmul_mx(ap(bank(i, b - a)), T["q" + st][:, sa:sa + 128], T["p" + st][:, sa:sa + 128], T["q" + mv][:, a:b], T["p" + mv][:, a:b], True, True),
+           [("q" + st, sa, sa + 128), ("p" + st, sa, sa + 128), ("q" + mv, a, b)], [bank(i, b - a)])
 
-    ukeys = [R("qur", 0, 2)]
+    def readout(buf, a, b):
+        return (buf, 16 * a + 15, 16 * b, 16)
+
+    def load(q, dst, src):
+        view = ap(dst).bitcast(dt.uint8) if dst[0] == "qw" else ap(dst)
+        op(q, lambda e: e.dma_start(view, src), [], [dst], dma=True)
+
+    load("S", ("ut", 0, 512), T.u[:, :])
+    load("Y", ("sti", 0, 18), T.st[:, :])
+    for a, b in PART:
+        load("Y", ("xin", 4 * a, 4 * b), T.x[:, 4 * a:4 * b])
+    load("S", ("tai", 0, 18), T.ta[:, :])
+    load("S", ("tbi", 0, 18), T.tb[:, :])
+    load("Y", ("qw", 0, 512), T.wc[:, :])
+    load("Y", ("pw", 0, 512), T.ws[:, :])
+    load("Y", ("vt", 0, 512), T.v[:, :])
+
+    iota(("pi", 0, 5), [[1, 5]], 0, 1, False)
+    iota(("tm", 0, 16), [[1, 16]], 0, 0)
+    iota(("ca", 0, COLS), [[-1, COLS]], COLS - 1, 0)
+    iota(("idf", 0, C), [[1, C]], 0, 0)
+    iota(("offui", 0, 8), [[16, 8]], 0, 0, False)
+    fill(("ones", 0, 516), 1.0)
+    op("P", lambda e: e.affine_select(T.eb[:, :], T.ones[:, :], [[1, 516]], A.is_equal, 0.0, -3, -4), [("ones", 0, 516)], [("eb", 0, 516)])
+    iota(("lam", 0, C), [[1, 16], [-16, 18]], 16 * 17 + 1, 0)
+    iota(("cb", 0, 8), [[16, 8]], 16 * (18 - STAGES), 0)
+
+    ts(("pk", 0, 2), ("pi", 0, 2), 15, None, A.bitwise_and)
+    ts(("pk", 2, 4), ("pi", 0, 5, 4), 2, 3, A.arith_shift_right, A.bitwise_and)
+    ts(("pk", 4, 5), ("pi", 0, 1), 3, None, A.bitwise_and)
+    fill(("w", MID, MID + 2), 0.0)
+    cp(("pf", 0, 5), ("pk", 0, 5))
+    p16, q16, p4, q4, t4 = [("pf", j, j + 1) for j in range(5)]
+    SC, HALF, START, T4, SC4 = [("sc", j, j + 1) for j in range(5)]
+    act(("enc", 0, C), ("idf", 0, C), F.Identity, scale=2.0, bias=2.0)
+    for a, (here, after) in enumerate([(p16, q16), (p4, q4)]):
+        ts(("ma", 16 * a, 16 * a + 16), ("tm", 0, 16), after, BIG, A.is_equal, A.mult)
+        ts(("mb", 16 * a, 16 * a + 16), ("tm", 0, 16), here, None, A.not_equal)
+    ts(("l16", 0, 26), ("ones", 0, 26), p16, None, A.mult)
+    ts(("sc", 5, 6), p16, 18.0, None, A.mult)
+    tt(("m16", 0, 32), ("ma", 0, 32), ("mb", 0, 32), A.max)
+    ts(SC, p16, 15.0, 1.0 / BIG, A.is_equal, A.max)
+    ts(("ca", 0, COLS), ("ca", 0, COLS), ("sc", 5, 6), None, A.add)
+    gather("S", ("pure", 0, 400), ("m16", 0, 16), ("l16", 0, COLS))
+    ts(("sc", 6, 7), p16, 15.0, BIG, A.not_equal, A.mult)
+    ts(("l4", 0, 18), ("ones", 0, 18), t4, None, A.mult)
+    ts(("yy", 0, COLS), ("ca", 0, COLS), C - 0.5, float(C), A.is_gt, A.mult)
+    ts(HALF, SC, 0.5, None, A.mult)
+    ts(START, ("sc", 6, 7), 1.0, BASE + CARRY, A.max, A.mult)
+    tt(("ca", 0, COLS), ("ca", 0, COLS), ("yy", 0, COLS), A.subtract)
+    ts(("sc", 7, 8), p4, 3.0, 1.0 / BIG, A.is_equal, A.max)
+    cp(("offu", 0, 8), ("offui", 0, 8))
+    cp(("halo", 0, COLS), ("ca", 0, COLS))
+    ts(SC4, ("sc", 7, 8), 2.0, None, A.mult)
+    ts(T4, t4, -4.0, None, A.add)
+
+    def first_list():
+        for a, b, at in ((0, CHUNK[0][1], 0), (CHUNK[0][1], COLS, AT[1])):
+            ts(("sl", at, at + b - a), readout("sol", a, b), HALF, -1.0, A.mult, A.add)
+
+    cp(("sn", 0, 18), ("sti", 0, 18))
+    gather("S", ("rn", 0, C), ("enc", 0, C), ("sn", 0, 18))
+    quant("u", 0, 128, "ut")
+    gather("S", ("r", 0, 400), ("rn", 0, C), ("halo", 0, COLS))
+    ts(("chain", 0, 400), ("pure", 0, 400), 1.0 / (2048 * BIG), None, A.max)
+    op("V", lambda e: e.tensor_copy(T.qur[:, 0:128].bitcast(dt.uint32), T.qu[:, 0:128].bitcast(dt.uint32).indirect(T.offu[:, 0:8])), [("qu", 0, 128), ("offu", 0, 8)], [("qur", 0, 128)])
+    op("S", lambda e: e.activation(T.pur[:, 0:128], T.pu[:, 0:128].indirect(T.offu[:, 0:8]), F.Copy), [("qu", 0, 128), ("offu", 0, 8)], [("pur", 0, 128)])
+
+    def quant_x(r, hf):
+        quant("x%d" % r, *PART[hf], "xt%d" % r if r else "xin")
 
     def score_part(r, hf):
         a, b = PART[hf]
-        mm(hf, "ur", 0, ukeys, "x%d" % r, a, b)
-        S(lambda e: e.activation(T.sg[:, a:b], bank(hf, b - a), F.Sign, bias=TINY), [R("B%d" % hf)], [R("sg", a, b)])
+        mm(hf, "ur", 0, "x%d" % r, a, b)
+        act(("sg", a, b), bank(hf, b - a), F.Sign, bias=TINY)
 
-    def idsg_part(hf):
+    def piece(q, buf, i, b, a, n, at):
+        move(q, (buf, 4 * a + b, 4 * (a + n), 4), ("ps", 512 * i + at, 512 * i + at + n))
+
+    def unpack(r, hf, b):
+        mm(3 - hf + b, "e", 128 * b, "x%d" % r, *PART[hf])
+
+    def unpacked(q, hf, b):
+        piece(q, "tt", 3 - hf + b, b, PART[hf][0], PART[hf][1] - PART[hf][0], 0)
+
+    def early_lanes(r):
+        for b in range(OPT["early"]):
+            unpack(r, 0, b)
+            unpacked("S", 0, b)
+
+    def val_part(hf):
         a, b = PART[hf]
-        tt(("idsg", a, b), ("sg", a, b), ("enc", a, b), A.mult)
+        tt(("val", a, b), ("sg", a, b), ("enc", a, b), A.mult)
 
-    def scan(out, mask, row):
-        V(lambda e: e.tensor_tensor_scan(ap(out), ap(mask), ap(row), 0.0, A.mult, A.add), rgs(mask, row), rgs(out))
+    def quant_e(b):
+        quant("e", 128 * b, 128 * b + 128, "eb", 3 - b)
 
-    def table(q, dst, src, first, c, d):
-        m, o = (MID, 0) if first else (MID + K, 18)
-        if c == 16:
-            gather(q, (dst, m + 258, m + 321, 2), (src, 0, C), ("lab", o + c, o + d))
-        else:
-            gather(q, (dst, m + 1 + 16 * c, m + 1 + 16 * d), (src, 0, C), ("lab", o + c, o + d))
-
-    def mirror(win, first):
-        m = MID if first else MID + K
-        gather("S", (win, m - 320, m), (win, m, m + 336), ("rev", 0, 20))
-
-    VC = 10
-
-    def stage_gather(t):
-        row, win, off = "r", ("w", 0, 2 * K), "off"
-        if t == 0:
-            win, off = ("idsg", 0, C), "sl"
-        elif t == STAGES:
-            row, win = "rl", ("wl", 0, 2 * K)
-        gather("V", (row, 0, 16 * VC), win, (off, 0, VC))
-        gather("S", (row, 16 * VC, 304), win, (off, VC, 19))
-
-    M16, M4, SC16, SC4 = ("mask16", 0, 304), ("mask4", 0, 288), ("sc16", 0, 1), ("sc4", 4, 5)
-
-    def own_scan():
-        scan(("so1", 0, 304), M16, ("r", 0, 304))
-
-    def next_scan():
-        scan(("son", 0, 304), M16, ("r", 1, 305))
-
-    def nothing():
-        pass
-
-    def unsigned_list(scalar=nothing, vector=nothing, between=nothing):
-        own_scan()
-        next_scan()
-        scalar()
-        act(("za", 0, 19), ("so1", 15, 304, 16), F.Abs, scale=SC16)
-        vector()
-        ts(("tmp", 0, 19), ("son", 15, 304, 16), 0.0, float(K), A.is_gt, A.mult)
-        between()
-        tt(("yy", 0, 19), ("za", 0, 19), ("tmp", 0, 19), A.add)
-
-    def unsigned_end():
-        ts(("off", 0, 19), ("yy", 0, 19), float(MID), None, A.add)
-
-    def signed_list(between=nothing):
-        next_scan()
-        own_scan()
-        ts(("tmp", 0, 19), ("son", 15, 304, 16), 0.0, ("kp", 0, 1), A.is_gt, A.mult)
-        between()
-        tt(("yy", 0, 19), ("so1", 15, 304, 16), ("tmp", 0, 19), A.add)
-        ts(("off", 0, 19), ("yy", 0, 19), SC16, float(MID), A.mult, A.add)
-
-    def unpack_lane(mv, i, b):
-        mm(i, "e", 128 * b, [R("qe", 128 * b, 128 * b + 128)], mv, 0, C)
-
-    def piece(q, buf, i, b, hf):
-        a = hf * HC
-        out, src = T[buf][:, 4 * a + b:4 * (a + HC):4], T.ps[:, 512 * i + a:512 * i + a + HC]
-        rd, wr = [R("B%d" % i)], [(buf + "_" + str(b), a, a + HC)]
-        if q == "V":
-            V(lambda e: e.tensor_copy(out, src), rd, wr)
-        else:
-            S(lambda e: e.activation(out, src, F.Copy), rd, wr)
-
-    cp(("sl", 0, 18), ("sti", 0, 18))
-    cp(("sl", 18, 19), ("sti", 0, 1))
     quant_x(0, 0)
     quant_x(0, 1)
     score_part(0, 0)
+    scan(("sol", 0, 400), ("pure", 0, 400), ("r", 0, 400))
     score_part(0, 1)
     cp(("lab", 0, 18), ("tai", 0, 18))
     cp(("lab", 18, 36), ("tbi", 0, 18))
-    idsg_part(0)
-    idsg_part(1)
-
-    def sc4_factor(k):
-        ts(("sc4", k, k + 1), p4, k + 1.0, 1.0 / UP, A.is_ge, A.max)
-
-    def later(t):
-        if t == 2:
-            ts(M4, ("tm4", 0, 288), p4, UP, A.not_equal, A.mult)
-        elif t == 3:
-            sc4_factor(0)
-            sc4_factor(1)
-        elif t == 4:
-            sc4_factor(2)
-            tt(("sc4", 3, 4), ("sc4", 0, 1), ("sc4", 1, 2), A.mult)
-        elif t == 5:
-            ts(SC4, ("sc4", 3, 4), ("sc4", 2, 3), 4.0, A.mult, A.mult)
+    first_list()
+    val_part(0)
+    val_part(1)
 
     def differences():
         tt(("dd", 0, 18), ("ab", 18, 36), ("ab", 0, 18), A.subtract)
         tt(("dd", 18, 36), ("ab", 0, 18), ("ab", 18, 36), A.subtract)
 
+    def both(f, h):
+        return lambda: (f(), h())
+
+    later = [
+        both(lambda: quant_e(0), lambda: ts(("ahead", 0, 8), ("cb", 0, 8), q16, None, A.add)),
+        lambda: quant_e(1), lambda: quant_e(2), lambda: quant_e(3),
+        lambda: scan(("so4", 0, C), ("pure", 0, C), ("lam", 0, C)),
+        both(lambda: cp(("ab", 0, 18), ("tai", 0, 18)), lambda: cp(("ab", 18, 36), ("tbi", 0, 18))),
+        lambda: ts(("order", 0, 18), readout("so4", 0, 18), SC, -1.0, A.mult, A.add),
+    ]
+
+    def span(k, t):
+        a, b = CHUNK[k]
+        return max(a, t), b
+
+    def mirror(q, c, a, b):
+        end = MID - 2 * b - 2 + c
+        out, src = T.w[:, MID - 2 * a - 2 + c:(end if end >= 0 else None):-2], T.w[:, MID + 2 * a + 2 + c:MID + 2 * b + 2 + c:2]
+        op(q, (lambda e: e.tensor_copy(out, src)) if q == "V" else lambda e: e.activation(out, src, F.Copy),
+           [("w", MID + 2 * a + 2 + c, MID + 2 * b + 2 + c, 2)], [("w", MID - 2 * a - 2 + c, end, -2)])
+
+    def table(q, c, a, b):
+        gather(q, ("w", MID + 2 + 32 * a + c, MID + 2 + 32 * b + c, 2), ("val", 0, C), ("lab", 18 * c + a, 18 * c + b))
+
     for r in range(3):
         partner = T.cores[rank ^ STEP[r]]
         rid, pid = topo.addr(partner, core)
-        engines = topo.engines(core, partner)[:8]
+        engines = topo.engines(core, partner)
         mask = sum(1 << e for e in engines)
         ne = len(engines)
         qx, lx, own, arr = "x%d" % r, "l%d" % r, "own%d" % r, "arr%d" % r
-        own_t, got_t = [2, 3, 4, 5], [6, 7, 0, 1]
+        got_t = [7, 0, 1, 6]
 
-        before("P", [R("q" + qx)])
+        before("P", [("q" + qx, 0, C)])
         g.remote_dma(T["q" + lx][:, :].bitcast(dt.uint8), T["q" + qx][:, :].bitcast(dt.uint8), T.sem["ax%d" % r], T.sem.left, pid, rid, mask)
         g.remote_dma(T["p" + lx][:, :], T["p" + qx][:, :], T.sem["ax%d" % r], T.sem.left, pid, rid, mask)
         count["left"] = count.get("left", 0) + 2 * ne
-        arrival("ax%d" % r, 2 * ne, [R("q" + lx)])
-        arrival("al%d" % r, ne, [R(arr)])
-        if r == 0:
-            iota(("idf", 0, 288), [[1, 288]], 0, 0)
-            unpacker(2)
-            unpacker(3)
+        arrival("ax%d" % r, 2 * ne, [("q" + lx, 0, C)])
+        arrival("al%d" % r, ne, [(arr, 0, 72)])
+        early = OPT["early"] if r else 0
+        lanes = [(0, b) for b in range(early, 4)] + [(1, b) for b in range(4)]
+        products = [(3 - hf + b, lambda hf=hf, b=b: unpack(r, hf, b)) for hf, b in lanes]
+        products += [(got_t[b], lambda b=b: mm(got_t[b], "e", 128 * b, lx, 0, C)) for b in range(4)]
+        held = set()
 
-        def tails():
-            table("S", "w", "idsg", True, 16, 18)
-            table("S", "w", "idsg", False, 16, 18)
-        stage_gather(0)
-        unsigned_list(tails, lambda: table("V", "w", "idsg", False, 0, 6))
-        table("S", "w", "idsg", True, 0, 16)
-        table("S", "w", "idsg", False, 12, 16)
-        table("V", "w", "idsg", False, 6, 12)
-        unsigned_end()
+        def multiply():
+            while products and products[0][0] not in held:
+                i, call = products.pop(0)
+                held.add(i)
+                call()
+
+        def lane(q):
+            hf, b = lanes.pop(0)
+            unpacked(q, hf, b)
+            held.discard(3 - hf + b)
+            multiply()
+
+        head = [(0, CHUNK[0][1], 0), (CHUNK[0][1], COLS, AT[1])]
+
+        def signs(k):
+            a, b, at = head[k]
+            gather("S", ("r0", 16 * a, 16 * b), ("sg", 0, C), ("sl", at, at + b - a), scale=0.5)
+
+        def sign_scan(k):
+            a, b, at = head[k]
+            scan(("so0", 16 * a, 16 * b), ("pure", 16 * a, 16 * b), ("r0", 16 * a, 16 * b))
+
+        def sign_add(k):
+            a, b = max(head[k][0], 1), head[k][1]
+            tt(("yy", a, b), readout("so0", a - 1, b - 1), readout("sol", a, b), A.add)
+
+        def sign_list(k):
+            a, b, at = max(head[k][0], 1), head[k][1], head[k][2]
+            ts(("off", at, at + b - a), ("yy", a, b), SC, 0.5, A.mult, A.add)
+
+        ga, gb = OPT["ga"], OPT["gb"]
+        signs(0)
+        signs(1)
+        sign_scan(0)
+        table("V", 0, 0, ga)
+        table("S", 1, 0, gb)
+        sign_add(0)
+        sign_scan(1)
+        table("V", 0, ga, 18)
+        sign_list(0)
+        sign_add(1)
+        if gb < 18:
+            table("V", 1, gb, 18)
+        sign_list(1)
+
+        rest = list(later) if r == 0 else []
         if r:
-            for b in range(4):
-                unpack_lane(qx, own_t[b], b)
-            for b in range(4):
-                unpack_lane(lx, got_t[b], b)
-        own_p = [(b, hf) for b in range(4) for hf in range(2)]
+            multiply()
+        else:
+            rest[3] = both(rest[3], multiply)
+        rest += [differences]
+        rest += [lambda: lane("V")] * len(lanes)
+        late_pieces = [(b, a) for a in (0, 144) for b in range(4)]
 
-        def own_pieces(n):
-            for i in range(n):
-                b, hf = own_p.pop(0)
-                piece("S", "tt", own_t[b], b, hf)
-
-        def plain_tails():
-            table("S", "wl", "idf", True, 16, 18)
-            table("S", "wl", "idf", False, 16, 18)
-
-        for t in range(1, STAGES):
-            stage_gather(t)
-            mine = nothing
-            if r == 0:
-                mine = lambda: later(t)
-                if t == 1:
-                    cp(("ab", 0, 18), ("tai", 0, 18))
-                    cp(("ab", 18, 36), ("tbi", 0, 18))
-                elif t <= 5:
-                    b = t - 2
-                    quant("e", 128 * b, 128 * b + 128, "eb", [R("eb", b, b + 1)])
-                    unpack_lane(qx, own_t[b], b)
-                    if b == 3:
-                        for b in range(4):
-                            unpack_lane(lx, got_t[b], b)
-            if t == 1:
-                unsigned_list(nothing if r else lambda: fill("wl", 0, 336))
-                unsigned_end()
-                mirror("w", True)
-            elif t == 2:
-                mirror("w", False)
-                if r == 0:
-                    fill("wl", 336, 672)
-                signed_list(mine)
-                differences()
-            elif t == 6 and r == 0:
-                unsigned_list(lambda: own_pieces(2))
-                own_pieces(2)
-                unsigned_end()
+        def stage_gather(k, t):
+            a, b = span(k, t)
+            win = ("w", MID, MID + 2 * C + 2) if t == 1 else ("w", 0, MID + 2 * C + 2)
+            off = ("off", AT[k], AT[k] + b - a)
+            if t == STAGES:
+                gather("S", ("r", 16 * a, 16 * b), win, off, fn=F.Abs)
             else:
-                if t < 5:
-                    if r == 0:
-                        fill("wl", 336 * t - 336, 336 * t)
-                    table("S", "wl", "idf", t == 3, 0, 16)
-                elif r:
-                    mirror("wl", t == 5)
-                if t == (4 if r else 5):
-                    plain_tails()
-                if t == 5 or r and t != 4:
-                    own_pieces(2)
-                signed_list(mine)
-        stage_gather(STAGES)
-        own_pieces(2)
-        scan(("so4", 0, 288), M4, ("rl", 0, 288))
-        ts((own, 0, 72), ("so4", 3, 288, 4), SC4, t4, A.mult, A.add)
-        before("P", [R(own)])
+                gather("S", ("r", 16 * a, 16 * b), win, off, add=BASE)
+
+        def stage_scan(k, t):
+            a, b = span(k, t)
+            a -= min(k, 1)
+            scan(("so", 16 * (a + k), 16 * (b + k)), ("chain", 16 * a, 16 * b), ("r", 16 * a, 16 * b), START)
+
+        def stage_list(k, t):
+            a, b = span(k, t + 1)
+            ts(("off", AT[k], AT[k] + b - a), readout("so", a + k, b + k), SC, MID - BASE - CARRY, A.mult, A.add)
+
+        mir = [(lambda n=n: mirror(OPT["mir"][n], n // 2, 144 * (n % 2), 144 * (n % 2) + 144)) for n in range(4)]
+        steps = [(k, t) for t in range(1, STAGES) for k in range(len(CHUNK))]
+        for n, (k, t) in enumerate(steps):
+            stage_gather(k, t)
+            for i in range(4):
+                if OPT["mat"][i] == n:
+                    mir[i]()
+            stage_scan(k, t)
+            if n:
+                stage_list(*steps[n - 1])
+            if t > 1 and rest and k in OPT["fill" if r else "fill0"]:
+                rest.pop(0)()
+        if r == 0:
+            gather("V", ("mask4", 0, C), ("m16", 16, 20), ("l4", 0, 18))
+        for k in range(len(CHUNK)):
+            if k == 0:
+                stage_list(*steps[-1])
+            stage_gather(k, STAGES)
+        while rest:
+            rest.pop(0)()
+
+        done = ("r", 16 * STAGES, 400)
+        gather("V", ("rn", 0, 160), done, ("order", 0, 10))
+        gather("S", ("rn", 160, C), done, ("order", 10, 18))
+        scan(("so4", 0, C), ("mask4", 0, C), ("rn", 0, C))
+        ts((own, 0, 72), ("so4", 3, C, 4), SC4, T4, A.mult, A.add)
+        before("P", [(own, 0, 72)])
         g.remote_dma(T[arr][:, :], T[own][:, :], T.sem["al%d" % r], T.sem.left, pid, rid, mask)
         count["left"] += ne
 
-        gather("S", ("zt", 576, 1152), ("tt", 0, 1152), (own, 36, 72), [R("zt", HC, C)], lanes("tt"))
-        scan(("sol", 0, 304), M16, ("rl", 0, 304))
-        gather("V", ("zt", 0, 576), ("tt", 0, 1152), (own, 0, 36), [R("zt", 0, HC)], lanes("tt"))
-        ts(("sl", 0, 18), ("sol", 15, 288, 16), SC16, None, A.mult)
-        ts(("sl", 18, 19), ("sol", 15, 16), SC16, None, A.mult)
-        for hf in range(2):
-            for b in (0, 1):
-                piece("S", "tq", got_t[b], b, hf)
-                piece("V", "tq", got_t[b + 2], b + 2, hf)
-        if r == 0:
-            quant("v", 0, 128, "vt", [R("vt")])
-
-        for hf in range(2):
-            a, b = PART[hf]
-            m = (a + b) // 2
-            gather("V", ("zp", 4 * a, 4 * m), ("tq", 0, 1152), (arr, a // 4, m // 4), [R("zp", a, m)], lanes("tq"))
-            gather("S", ("zp", 4 * m, 4 * b), ("tq", 0, 1152), (arr, m // 4, b // 4), [R("zp", m, b)], lanes("tq"))
-            quant("z", a, b, "zp", [R("zp", a, b)])
-            for k in (0, 2, 1, 3):
-                mm(4 * hf + k, "w", 128 * k, [R("qw"), R("pw")], "z", a, b)
-        for hf in range(2):
-            a, b = PART[hf]
-            for k in (0, 2, 1, 3):
-                i = 4 * hf + k
-                out, wr = T.h[:, 4 * a + k:4 * b:4], [("h_%d" % k, a, b)]
-                if k < 2:
-                    V(lambda e: e.tensor_scalar(out, bank(i, b - a), 0.03125, None, A.mult), [R("B%d" % i)], wr)
-                else:
-                    S(lambda e: e.activation(out, bank(i, b - a), F.Copy, scale=0.03125), [R("B%d" % i)], wr)
-
         xt, last = "xt%d" % (r + 1), r == 2
+        if not last:
+            gather("S", ("r", 0, 16 * STAGES), done, ("ahead", 0, STAGES))
+        for b, a in late_pieces[:2]:
+            piece("S", "tq", got_t[b], b, a, 144, a)
+        gather("S", ("zt", 576, 1152), ("tt", 0, 1152), (own, 36, 72))
+        if not last:
+            scan(("sol", 0, 400), ("pure", 0, 400), ("r", 0, 400))
+        gather("V", ("zt", 0, 576), ("tt", 0, 1152), (own, 0, 36))
+        if not last:
+            first_list()
+        for n, (b, a) in enumerate(late_pieces[2:]):
+            piece("V" if n % 2 == 0 else "S", "tq", got_t[b], b, a, 144, a)
+        if r == 0:
+            quant("v", 0, 128, "vt")
+        if last:
+            act(("opr", 0, C), ("rn", 0, C), F.Identity, scale=0.5, bias=-1.0)
+
+        for hf in range(2):
+            a, b = PART[hf]
+            m = a + OPT["zv"][hf]
+            gather("V", ("zp", 4 * a, 4 * m), ("tq", 0, 1152), (arr, a // 4, m // 4))
+            gather("S", ("zp", 4 * m, 4 * b), ("tq", 0, 1152), (arr, m // 4, b // 4))
+            quant("z", a, b, "zp")
+            for k in (0, 2, 1, 3):
+                mm(4 * hf + k, "w", 128 * k, "z", a, b)
+        for hf in range(2):
+            a, b = PART[hf]
+            for k in (0, 2, 1, 3):
+                move("V" if k < 2 else "S", ("h", 4 * a + k, 4 * b, 4), bank(4 * hf + k, b - a), 0.03125)
 
         def new_part(hf):
             a, b = PART[hf]
-            V(lambda e: e.tensor_tensor(T[xt][:, 4 * a:4 * b], T.h[:, 0:1152].indirect(T[arr][:, a // 4:b // 4]), T.zt[:, 4 * a:4 * b], A.add),
-              lanes("h") + [R(arr), R("zt", a, b)], [R(xt, a, b)])
+            op("V", lambda e: e.tensor_tensor(T[xt][:, 4 * a:4 * b], T.h[:, 0:1152].indirect(T[arr][:, a // 4:b // 4]), T.zt[:, 4 * a:4 * b], A.add),
+               [("h", 0, 1152), (arr, a // 4, b // 4), ("zt", 4 * a, 4 * b)], [(xt, 4 * a, 4 * b)], listed=True)
 
         def change_scan():
-            scan(("soc", 0, 288), ("mask16", 0, 288), ("cs", 0, 288))
+            scan(("soc", 0, C), ("pure", 0, C), ("cs", 0, C))
 
         def change():
-            ts(("c01", 0, 18), ("soc", 15, 288, 16), 0.0, None, A.is_gt)
+            ts(("c01", 0, 18), readout("soc", 0, 18), 0.0, None, A.is_gt)
+
+        def moves():
+            tt(("m2", 0, 18), ("dd", 0, 18), ("c01", 0, 18), A.mult)
+            tt(("m2", 18, 36), ("dd", 18, 36), ("c01", 0, 18), A.mult)
         if not last:
             new_part(0)
-        quant("h", 0, C, "h", lanes("h"))
-        mm(2, "ur", 0, ukeys, "h", 0, C)
-        S(lambda e: e.activation(T.cs[:, :], bank(2, C), F.Sign, bias=TINY), [R("B2")], [R("cs", 0, C)])
+        quant("h", 0, C, "h")
+        mm(2, "ur", 0, "h", 0, C)
+        act(("cs", 0, C), bank(2, C), F.Sign, bias=TINY)
         if last:
             new_part(0)
             change_scan()
-        quant_x(r + 1, 0)
-        if last:
+            quant_x(r + 1, 0)
             change()
             new_part(1)
+            moves()
+            quant_x(r + 1, 1)
+            tt(("ab", 0, 36), ("ab", 0, 36), ("m2", 0, 36), A.add)
         else:
+            quant_x(r + 1, 0)
             score_part(r + 1, 0)
+            early_lanes(r + 1)
             new_part(1)
             change_scan()
             quant_x(r + 1, 1)
-            change()
             score_part(r + 1, 1)
-            idsg_part(0)
-        tt(("m2", 0, 18), ("dd", 0, 18), ("c01", 0, 18), A.mult)
-        tt(("m2", 18, 36), ("dd", 18, 36), ("c01", 0, 18), A.mult)
-        if last:
-            quant_x(r + 1, 1)
-        tt(("ab", 0, 36), ("ab", 0, 36), ("m2", 0, 36), A.add)
-        if not last:
-            idsg_part(1)
+            change()
+            val_part(0)
+            moves()
+            tt(("ab", 0, 36), ("ab", 0, 36), ("m2", 0, 36), A.add)
+            val_part(1)
         cp(("lab", 0, 36), ("ab", 0, 36))
 
     def out(q, dst, src, rd):
-        op(q, lambda e: e.dma_start(dst, src), rd, [], dma=True)
+        op(q, lambda e: e.dma_start(dst, src), [rd], [], dma=True)
     for hf in range(2):
-        mm(3 + hf, "v", 0, [R("qv")], "x3", *PART[hf])
-    out("Y", T.oc[:, :], T.qx3[:, :].bitcast(dt.uint8), [R("qx3")])
-    gather("S", ("opr", 0, C), ("idf", 0, C), ("sl", 0, 18))
+        mm(3 + hf, "v", 0, "x3", *PART[hf])
+    out("Y", T.oc[:, :], T.qx3[:, :].bitcast(dt.uint8), ("qx3", 0, C))
     for hf in range(2):
         a, b = PART[hf]
-        V(lambda e: e.tensor_copy(T.yo[:, a:b], bank(3 + hf, b - a)), [R("B%d" % (3 + hf))], [R("yo", a, b)])
+        cp(("yo", a, b), bank(3 + hf, b - a))
     gather("V", ("opr", C, 2 * C), ("idf", 0, C), ("lab", 0, 18))
     gather("S", ("opr", 2 * C, 3 * C), ("idf", 0, C), ("lab", 18, 36))
-    out("Y", T.y[:, :], T.yo[:, :], [R("yo")])
+    out("Y", T.y[:, :], T.yo[:, :], ("yo", 0, C))
     for k in range(4):
-        out("S" if k % 2 else "Y", T.osc[4 * k:4 * k + 4, :], T.px3[32 * k:32 * k + 4, :], [R("qx3")])
-    out("S", T.op[:, :], T.opr[0:128:16, :], [R("opr")])
+        out("S" if k % 2 else "Y", T.osc[4 * k:4 * k + 4, :], T.px3[32 * k:32 * k + 4, :], ("qx3", 0, C))
+    out("S", T.op[:, :], T.opr[0:128:16, :], ("opr", 0, 3 * C))
     finish()

@@ -6,14 +6,15 @@ STAGES = 7
 C = 288
 PART = [(0, 160), (160, 288)]
 COLS = 18 + STAGES
-CHUNK = [(0, 9), (9, 15), (15, 21), (21, 25)]
-AT = [0, 10, 16, 22]
+ZPART = [(0, 160), (160, 288)]
+CHUNK = [(0, 9), (9, 13), (13, 17), (17, 21), (21, 25)]
+AT = [0, 10, 14, 18, 22]
 MID = 576
 BIG = 2.0 ** 40
 CARRY = 6000.0
 BASE = 2047 * CARRY + 1024
 TINY = -2.0 ** -100
-OPT = {"fill": [0, 2], "fill0": [0, 2], "early": 3, "early0": 0, "mir": "VVVV", "mat": [0, 0, 0, 1], "ga": 10, "gb": 18, "zv": [80, 64]}
+OPT = {"ga": [10], "zv": [88, 16, 56], "new": [160], "wake": 200.0, "grain": 30.0, "list": 1400.0, "tile": 5000.0, "gat": 1.56, "pe": 1.0, "mos": 48, "load": 1600.0, "passes": 6, "turn": "SVN", "newlast": [160, 192, 224, 256], "between": [1, 1, 2, 1, 0], "gq": "VS", "g0": "S", "hq": ["V", "V", "S", "S"], "zq": None}
 
 SCRATCH = {"ps": ("psum", [128, 4096], "float32")}
 
@@ -26,88 +27,147 @@ def _bufs(where, dtype, **cols):
 _bufs("sbuf", "bfloat16", xin=1152, xt1=1152, xt2=1152, xt3=1152, ut=512, vt=512, ones=516, eb=516, tm=16, ma=32, mb=32, m16=32,
       pure=400, chain=400, mask4=288, sg=288, cs=288, r0=400, so0=400, soc=288,
       tt=1152, tq=1152, zt=1152, zp=1152, h=1152)
-for _n, _c in [("u", 128), ("ur", 128), ("v", 128), ("w", 512), ("e", 512), ("z", 288), ("h", 288)] + [("x%d" % _r, 288) for _r in range(4)] + [("l%d" % _r, 288) for _r in range(3)]:
+for _n, _c in [("u", 128), ("ur", 128), ("v", 128), ("w", 512), ("e", 512), ("z", 288), ("h", 288), ("n", 288), ("o", 288)] + [("x%d" % _r, 288) for _r in range(4)] + [("l%d" % _r, 288) for _r in range(3)]:
     SCRATCH["q" + _n] = ("sbuf", [128, _c], "float8_e4m3fn_x4")
     SCRATCH["p" + _n] = ("sbuf", [128, _c], "uint8")
 _bufs("sbuf", "int32", pi=8, pk=8, offui=8, tai=18, tbi=18, sti=18)
-_bufs("sbuf", "float32", pf=8, sc=8, enc=288, idf=288, lam=288, val=288, ab=36, dd=36, m2=36, c01=18, yy=26, ca=26, cb=8,
-      w=1160, r=400, so=480, rn=288, so4=288, sol=400, opr=864, yo=288)
-_bufs("sbuf", "uint16", offu=8, l16=26, l4=18, order=18, halo=26, ahead=8, sn=18, sl=28, lab=36, off=28, own0=72, own1=72, own2=72, arr0=72, arr1=72, arr2=72)
+_bufs("sbuf", "float32", pf=8, sc=8, enc=288, lam=288, nat=288, rowa=576, rowb=576, sot=576, soo=288, val=288, ab=36, dd=18, mean=18, m2=36, yy=26, ca=26, cb=8, cc=26, cd=26,
+      w=1160, r=400, so=496, rn=288, so4=288, sol=400, opr=864, yo=288)
+_bufs("sbuf", "uint16", offu=8, l16=26, l4=18, order=18, natl=18, ln=36, halo=26, ahead=8, sn=18, sl=28, lab=36, off=28, own0=72, own1=72, own2=72, arr0=72, arr1=72, arr2=72)
 
 DMAS = ["d%d" % _i for _i in range(20)]
-SEMAPHORES = ["cV", "cS", "cT", "cP", "left"] + ["ax%d" % _r for _r in range(3)] + ["al%d" % _r for _r in range(3)] + DMAS
+SEMAPHORES = ["cV", "cS", "cT", "cP", "left"] + ["ax%d" % _r for _r in range(3)] + ["al%d%d" % (_r, _h) for _r in range(3) for _h in range(2)] + DMAS
+CYCLE = 0.83
+ORDER = []
+
+
+def plan(nodes):
+    wake, n = OPT["wake"], len(nodes)
+    after = [{} for i in range(n)]
+    for i in range(n):
+        for p, hard in nodes[i]["pre"].items():
+            after[p][i] = hard
+
+    def held(i, q):
+        return nodes[i]["on"][q][1] if nodes[i]["busy"] is None else nodes[i]["busy"]
+
+    def lag(p, qp, i, hard):
+        return nodes[p]["on"][qp][1] + wake if hard else nodes[p]["on"][qp][1] if None in nodes[i]["on"] else held(p, qp)
+
+    def place(turn, back):
+        at, taken = {}, {}
+        for i in turn:
+            best = None
+            for q in nodes[i]["on"]:
+                d = held(i, q)
+                if back:
+                    t = max([nodes[i]["on"][q][1]] + [at[j][0] + lag(i, q, j, h) for j, h in after[i].items()]) - d
+                else:
+                    t = max([0.0] + [at[p][0] + lag(p, at[p][1], i, h) for p, h in nodes[i]["pre"].items()])
+                for a, b in taken.get(q, []) if q else []:
+                    if t + d <= a:
+                        break
+                    t = max(t, b)
+                if best is None or t + d < best[0] + best[2]:
+                    best = (t, q, d)
+            t, q, d = best
+            at[i] = (t + d if back else t, q)
+            taken.setdefault(q, []).append((t, t + d))
+            taken[q].sort()
+        return at
+    first = [list(x["on"])[0] for x in nodes]
+    ahead = [0.0] * n
+    for i in range(n - 1, -1, -1):
+        ahead[i] = max([nodes[i]["on"][first[i]][1]] + [ahead[j] + lag(i, first[i], j, h) for j, h in after[i].items()])
+    turn, best = sorted(range(n), key=lambda i: (-ahead[i], i)), None
+    for k in range(OPT["passes"]):
+        at = place(turn, False)
+        length = max(at[i][0] + nodes[i]["on"][at[i][1]][1] for i in range(n))
+        if best is None or length < best[0]:
+            best = (length, at)
+        late = place(sorted(range(n), key=lambda i: (-at[i][0], -i)), True)
+        turn = sorted(range(n), key=lambda i: (-late[i][0], i))
+    at = best[1]
+    return [(i, at[i][1]) for i in sorted(range(n), key=lambda i: (at[i][0], i))]
 
 
 def make_tracker(g, T):
     queues = {"V": g.vector, "S": g.scalar, "T": g.tensor, "P": g, "Y": g.sync}
     csem = {"V": "cV", "S": "cS", "T": "cT", "P": "cP"}
-    count = {}
-    known = {q: {} for q in queues}
-    clocks = {}
+    nodes = []
     writes, reads = {}, {}
-    ndma = [0]
 
     def cols(x):
         if x[0] == "ps":
             return frozenset(range(x[1] // 512, (x[2] - 1) // 512 + 1))
         return frozenset(range(*x[1:]))
 
-    def wait(q, toks):
-        best = {}
-        for s, v in toks:
-            if known[q].get(s, 0) < v:
-                best[s] = max(best.get(s, 0), v)
-        items = sorted(best.items())
-        for s, v in items:
-            if not any(o[0] != s and clocks[o].get(s, 0) >= v for o in items):
-                queues[q].wait_ge(T.sem[s], v)
-        for s, v in items:
-            for s2, v2 in clocks[(s, v)].items():
-                known[q][s2] = max(known[q].get(s2, 0), v2)
-            known[q][s] = max(known[q].get(s, 0), v)
-
-    def deps(q, rd, wr):
-        toks = []
+    def op(on, rd, wr, kind="call", listed=False, behind=(), busy=None):
+        me, q = len(nodes), list(on)[0] if len(on) == 1 else "either"
+        pre = {p: False for p in behind}
         for x in rd + wr:
-            toks += [t for c, t in writes.get(x[0], []) if c & cols(x)]
+            pre.update({p: True for c, p in writes.get(x[0], []) if c & cols(x)})
         for x in wr + [x for x in rd if x[0] == "ps"]:
-            toks += [t for c, t, oq in reads.get(x[0], []) if c & cols(x) and oq != q]
-        return toks
-
-    def note(q, rd, wr, tok):
+            for c, p, oq in reads.get(x[0], []):
+                if c & cols(x) and (oq != q or x in wr):
+                    pre[p] = pre.get(p, False) or oq != q
         for x in wr:
             k, c = x[0], cols(x)
-            writes[k] = [e for e in writes.get(k, []) if not e[0] <= c] + [(c, tok)]
+            writes[k] = [e for e in writes.get(k, []) if not e[0] <= c] + [(c, me)]
             reads[k] = [e for e in reads.get(k, []) if not e[0] <= c]
-        for x in rd:
-            reads.setdefault(x[0], []).append((cols(x), tok, q))
+        for x in rd if kind != "remote" else []:
+            reads.setdefault(x[0], []).append((cols(x), me, q if kind == "call" and not listed and len(on) == 1 else "any"))
+        nodes.append({"on": on, "kind": kind, "busy": busy, "pre": pre})
+        return me
 
-    def op(q, call, rd, wr, dma=False, listed=False):
-        wait(q, deps(q, rd, wr))
-        s, inc = csem.get(q), 1
-        if dma:
-            s, inc = DMAS[ndma[0]], 16
-            ndma[0] += 1
-        count[s] = count.get(s, 0) + inc
-        tok = (s, count[s])
-        call(queues[q]).then_inc(T.sem[s], inc)
-        clocks[tok] = dict(known[q])
-        clocks[tok][s] = count[s]
-        note("any" if dma or listed else q, rd, wr, tok)
+    turn = {}
 
-    def arrival(s, v, wr):
-        clocks[(s, v)] = {s: v}
-        count[s] = v
-        note("any", [], wr, (s, v))
-
-    def before(q, rd):
-        wait(q, deps(q, rd, []))
+    def in_turn(name):
+        if name in turn and name in OPT["turn"]:
+            nodes[-1]["pre"].setdefault(turn[name], False)
+        turn[name] = len(nodes) - 1
 
     def finish():
+        if not ORDER:
+            ORDER.extend(plan(nodes))
+        count, clocks, token = {}, {}, {}
+        known = {q: {} for q in queues}
+        ndma = 0
+        for i, q in ORDER:
+            n = nodes[i]
+            call = n["on"][q][0]
+            if n["kind"] == "arrival":
+                token[i] = call
+                clocks[call] = {call[0]: call[1]}
+                count[call[0]] = call[1]
+                continue
+            best = {}
+            for p, hard in n["pre"].items():
+                if hard and known[q].get(token[p][0], 0) < token[p][1]:
+                    best[token[p][0]] = max(best.get(token[p][0], 0), token[p][1])
+            items = sorted(best.items())
+            for s, v in items:
+                if not any(o[0] != s and clocks[o].get(s, 0) >= v for o in items):
+                    queues[q].wait_ge(T.sem[s], v)
+            for s, v in items:
+                for s2, v2 in clocks[(s, v)].items():
+                    known[q][s2] = max(known[q].get(s2, 0), v2)
+            if n["kind"] == "remote":
+                count["left"] = count.get("left", 0) + call(g)
+                continue
+            s, inc = csem.get(q), 1
+            if n["kind"] == "dma":
+                s, inc = DMAS[ndma], 16
+                ndma += 1
+            count[s] = count.get(s, 0) + inc
+            token[i] = (s, count[s])
+            call(queues[q]).then_inc(T.sem[s], inc)
+            clocks[token[i]] = dict(known[q])
+            clocks[token[i]][s] = count[s]
         for s in sorted(count):
             g.wait_ge(T.sem[s], count[s])
 
-    return op, arrival, before, finish, count
+    return op, in_turn, finish
 
 
 def rank_program(g, core, T, topo):
@@ -116,415 +176,333 @@ def rank_program(g, core, T, topo):
         return
     A = AluOpType
     F = ActivationFunctionType
-    op, arrival, before, finish, count = make_tracker(g, T)
+    op, in_turn, finish = make_tracker(g, T)
 
     def ap(x):
         if not isinstance(x, tuple):
             return x
-        return T[x[0]][:, x[1]:x[2]:x[3]] if len(x) > 3 else T[x[0]][:, x[1]:x[2]]
+        if len(x) == 3:
+            return T[x[0]][:, x[1]:x[2]]
+        return T[x[0]][:, x[1]:(x[2] if x[2] >= 0 else None):x[3]]
 
     def rgs(*xs):
         return [x for x in xs if isinstance(x, tuple)]
 
+    def size(x):
+        return len(range(*x[1:]))
+
+    def cycles(out, *ins, rate=1.0):
+        if all(SCRATCH[x[0]][2] in ("bfloat16", "uint16") for x in (out,) + ins):
+            rate /= 2
+        return max(64, size(out) * rate) * CYCLE
+
+    def fetch(q, n):
+        return (65 if q == "S" else 50) + n * OPT["gat"] * CYCLE
+
     def ts(out, in0, s1, s2, *ops):
-        op("V", lambda e: e.tensor_scalar(ap(out), ap(in0), ap(s1), ap(s2), *ops), rgs(in0, s1, s2), [out])
+        op({"V": (lambda e: e.tensor_scalar(ap(out), ap(in0), ap(s1), ap(s2), *ops), cycles(out, in0))}, rgs(in0, s1, s2), [out])
 
     def tt(out, in0, in1, o):
-        op("V", lambda e: e.tensor_tensor(ap(out), ap(in0), ap(in1), o), [in0, in1], [out])
+        op({"V": (lambda e: e.tensor_tensor(ap(out), ap(in0), ap(in1), o), cycles(out, in0, in1, rate=2.0))}, [in0, in1], [out])
 
     def cp(out, in_):
-        op("V", lambda e: e.tensor_copy(ap(out), ap(in_)), [in_], [out])
+        move("V", out, in_)
 
     def fill(out, c):
-        op("V", lambda e: e.memset(ap(out), c), [], [out])
+        op({"V": (lambda e: e.memset(ap(out), c), cycles(out))}, [], [out])
 
-    def act(out, in_, fn, **k):
-        op("S", lambda e: e.activation(ap(out), ap(in_), fn, **{x: ap(k[x]) for x in k}), rgs(in_, *k.values()), [out])
+    def sign(out, in_):
+        op({"S": (lambda e: e.activation(ap(out), ap(in_), F.Sign, bias=TINY), cycles(out, in_))}, [in_], [out])
 
-    def move(q, out, in_, scale=None):
-        if q == "S":
-            act(out, in_, F.Copy, **({"scale": scale} if scale else {}))
-        elif scale:
-            ts(out, in_, scale, None, A.mult)
-        else:
-            cp(out, in_)
+    def move(qs, out, in_, scale=None):
+        on = {"V": (lambda e: e.tensor_scalar(ap(out), ap(in_), scale, None, A.mult) if scale else e.tensor_copy(ap(out), ap(in_)), cycles(out, in_)),
+              "S": (lambda e: e.activation(ap(out), ap(in_), F.Copy, scale=scale if scale else 1.0), max(64, size(out)) * CYCLE)}
+        op({q: on[q] for q in qs}, [in_], [out])
 
-    def gather(q, out, win, off, add=None, scale=None, fn=None):
+    def gather(qs, out, win, off, add=None, scale=None, fn=None):
         src = ap(win).indirect(ap(off))
-        if q == "S":
-            k = {"bias": add} if add else {"scale": scale} if scale else {}
-            call = lambda e: e.activation(ap(out), src, fn if fn else F.Identity if add else F.Copy, **k)
-        elif add or scale:
-            call = lambda e: e.tensor_scalar(ap(out), src, add if add else scale, None, A.add if add else A.mult)
-        else:
-            call = lambda e: e.tensor_copy(ap(out), src)
-        op(q, call, [win, off], [out], listed=True)
+        k = {"bias": add} if add else {"scale": scale} if scale else {}
+        on = {"S": lambda e: e.activation(ap(out), src, fn if fn else F.Identity if add else F.Copy, **k),
+              "V": lambda e: e.tensor_scalar(ap(out), src, add if add else scale, None, A.add if add else A.mult) if k else e.tensor_copy(ap(out), src)}
+        op({q: (on[q], fetch(q, size(out))) for q in qs}, [win, off], [out], listed=True)
 
-    def iota(out, pat, base, cm, flag=True):
-        if flag:
-            op("P", lambda e: e.iota(ap(out), pat, base, cm, allow_small_or_imprecise_dtypes=True), [], [out])
-        else:
-            op("P", lambda e: e.iota(ap(out), pat, base, cm), [], [out])
+    def iota(out, pat, base, cm):
+        k = {} if SCRATCH[out[0]][2] == "int32" else {"allow_small_or_imprecise_dtypes": True}
+        op({"P": (lambda e: e.iota(ap(out), pat, base, cm, **k), 130 + 2 * size(out) * CYCLE)}, [], [out])
 
     def scan(out, mask, row, first=0.0):
-        op("V", lambda e: e.tensor_tensor_scan(ap(out), ap(mask), ap(row), ap(first), A.mult, A.add), rgs(mask, row, first), [out])
+        op({"V": (lambda e: e.tensor_tensor_scan(ap(out), ap(mask), ap(row), ap(first), A.mult, A.add), cycles(out, mask, row))}, rgs(mask, row, first), [out])
 
     def quant(q, a, b, src, at=None):
         x = (src, 4 * a, 4 * b) if at is None else (src, at, at + 4 * (b - a))
-        op("V", lambda e: e.quantize_mx(T["q" + q][:, a:b], T["p" + q][:, a:b], ap(x)), [x], [("q" + q, a, b)])
+        op({"V": (lambda e: e.quantize_mx(T["q" + q][:, a:b], T["p" + q][:, a:b], ap(x)), 12 + 0.22 * size(x))}, [x], [("q" + q, a, b)])
 
-    def bank(i, n):
-        return ("ps", 512 * i, 512 * i + n)
+    def pick(dst, a, b, src, n, off):
+        rd = [("q" + src, 0, n), off]
+        op({"V": (lambda e: e.tensor_copy(T["q" + dst][:, a:b].bitcast(dt.uint32), T["q" + src][:, 0:n].bitcast(dt.uint32).indirect(ap(off))), fetch("V", b - a))},
+           rd, [("q" + dst, a, b)], listed=True)
+        op({"S": (lambda e: e.activation(T["p" + dst][:, a:b], T["p" + src][:, 0:n].indirect(ap(off)), F.Copy), fetch("S", b - a))}, rd, [("p" + dst, a, b)], listed=True)
+
+    def bank(i, n, at=0):
+        return ("ps", 512 * i + at, 512 * i + at + n)
 
     def mm(i, st, sa, mv, a, b):
-        op("T", lambda e: e.matmul_mx(ap(bank(i, b - a)), T["q" + st][:, sa:sa + 128], T["p" + st][:, sa:sa + 128], T["q" + mv][:, a:b], T["p" + mv][:, a:b], True, True),
-           [("q" + st, sa, sa + 128), ("p" + st, sa, sa + 128), ("q" + mv, a, b)], [bank(i, b - a)])
+        call = lambda e: e.matmul_mx(ap(bank(i, b - a)), T["q" + st][:, sa:sa + 128], T["p" + st][:, sa:sa + 128], T["q" + mv][:, a:b], T["p" + mv][:, a:b], True, True)
+        op({"T": (call, (b - a + 16) * CYCLE * OPT["pe"])}, [("q" + st, sa, sa + 128), ("p" + st, sa, sa + 128), ("q" + mv, a, b), ("p" + mv, a, b)], [bank(i, b - a)])
 
     def readout(buf, a, b):
         return (buf, 16 * a + 15, 16 * b, 16)
 
-    def load(q, dst, src):
-        view = ap(dst).bitcast(dt.uint8) if dst[0] == "qw" else ap(dst)
-        op(q, lambda e: e.dma_start(view, src), [], [dst], dma=True)
+    moved, loads = [0], {"S": [], "Y": []}
 
-    load("S", ("ut", 0, 512), T.u[:, :])
-    load("Y", ("sti", 0, 18), T.st[:, :])
-    for a, b in PART:
-        load("Y", ("xin", 4 * a, 4 * b), T.x[:, 4 * a:4 * b])
-    load("S", ("tai", 0, 18), T.ta[:, :])
-    load("S", ("tbi", 0, 18), T.tb[:, :])
-    load("Y", ("qw", 0, 512), T.wc[:, :])
-    load("Y", ("pw", 0, 512), T.ws[:, :])
-    load("Y", ("vt", 0, 512), T.v[:, :])
+    def dma(q, dst, src, rd, wr, nbytes, behind=()):
+        moved[0] += nbytes + 300
+        return op({q: (lambda e: e.dma_start(dst, src), OPT["load"] + 0.4 * moved[0])}, rd, wr, kind="dma", busy=50.0, behind=behind)
 
-    iota(("pi", 0, 5), [[1, 5]], 0, 1, False)
+    def load(q, dst, src, nbytes):
+        loads[q].append(dma(q, ap(dst).bitcast(dt.uint8) if dst[0] == "qw" else ap(dst), src, [], [dst], nbytes, loads[q][-1:]))
+
+    cut = 4 * PART[0][1]
+    load("Y", ("tai", 0, 18), T.ta[:, :], 72)
+    load("S", ("tbi", 0, 18), T.tb[:, :], 72)
+    load("Y", ("xin", 0, cut), T.x[:, 0:cut], 2 * cut)
+    load("S", ("sti", 0, 18), T.st[:, :], 72)
+    load("S", ("ut", 0, 512), T.u[:, :], 1024)
+    load("Y", ("xin", cut, 4 * C), T.x[:, cut:4 * C], 8 * C - 2 * cut)
+    load("Y", ("qw", 0, 512), T.wc[:, :], 2048)
+    load("Y", ("pw", 0, 512), T.ws[:, :], 512)
+    load("Y", ("vt", 0, 512), T.v[:, :], 1024)
+
+    iota(("pi", 0, 5), [[1, 5]], 0, 1)
     iota(("tm", 0, 16), [[1, 16]], 0, 0)
     iota(("ca", 0, COLS), [[-1, COLS]], COLS - 1, 0)
-    iota(("idf", 0, C), [[1, C]], 0, 0)
-    iota(("offui", 0, 8), [[16, 8]], 0, 0, False)
-    fill(("ones", 0, 516), 1.0)
-    op("P", lambda e: e.affine_select(T.eb[:, :], T.ones[:, :], [[1, 516]], A.is_equal, 0.0, -3, -4), [("ones", 0, 516)], [("eb", 0, 516)])
     iota(("lam", 0, C), [[1, 16], [-16, 18]], 16 * 17 + 1, 0)
+    iota(("nat", 0, C), [[-1, 18], [18, 16]], 17, 0)
+    iota(("offui", 0, 8), [[16, 8]], 0, 0)
+    iota(("enc", 0, C), [[2, C]], 2, 0)
     iota(("cb", 0, 8), [[16, 8]], 16 * (18 - STAGES), 0)
+    fill(("ones", 0, 516), 1.0)
+    fill(("w", MID, MID + 2), 0.0)
+    op({"P": (lambda e: e.affine_select(T.eb[:, :], T.ones[:, :], [[1, 516]], A.is_equal, 0.0, -3, -4), 170 + 2 * 516 * CYCLE)}, [("ones", 0, 516)], [("eb", 0, 516)])
+    for b in range(4):
+        quant("e", 128 * b, 128 * b + 128, "eb", 3 - b)
 
     ts(("pk", 0, 2), ("pi", 0, 2), 15, None, A.bitwise_and)
     ts(("pk", 2, 4), ("pi", 0, 5, 4), 2, 3, A.arith_shift_right, A.bitwise_and)
     ts(("pk", 4, 5), ("pi", 0, 1), 3, None, A.bitwise_and)
-    fill(("w", MID, MID + 2), 0.0)
-    cp(("pf", 0, 5), ("pk", 0, 5))
+    cp(("pf", 0, 2), ("pk", 0, 2))
+    cp(("pf", 2, 5), ("pk", 2, 5))
     p16, q16, p4, q4, t4 = [("pf", j, j + 1) for j in range(5)]
     SC, HALF, START, T4, SC4 = [("sc", j, j + 1) for j in range(5)]
-    act(("enc", 0, C), ("idf", 0, C), F.Identity, scale=2.0, bias=2.0)
-    for a, (here, after) in enumerate([(p16, q16), (p4, q4)]):
-        ts(("ma", 16 * a, 16 * a + 16), ("tm", 0, 16), after, BIG, A.is_equal, A.mult)
+    for a, (here, behind) in enumerate([(p16, q16), (p4, q4)]):
+        ts(("ma", 16 * a, 16 * a + 16), ("tm", 0, 16), behind, BIG, A.is_equal, A.mult)
         ts(("mb", 16 * a, 16 * a + 16), ("tm", 0, 16), here, None, A.not_equal)
+        tt(("m16", 16 * a, 16 * a + 16), ("ma", 16 * a, 16 * a + 16), ("mb", 16 * a, 16 * a + 16), A.max)
     ts(("l16", 0, 26), ("ones", 0, 26), p16, None, A.mult)
-    ts(("sc", 5, 6), p16, 18.0, None, A.mult)
-    tt(("m16", 0, 32), ("ma", 0, 32), ("mb", 0, 32), A.max)
-    ts(SC, p16, 15.0, 1.0 / BIG, A.is_equal, A.max)
-    ts(("ca", 0, COLS), ("ca", 0, COLS), ("sc", 5, 6), None, A.add)
-    gather("S", ("pure", 0, 400), ("m16", 0, 16), ("l16", 0, COLS))
-    ts(("sc", 6, 7), p16, 15.0, BIG, A.not_equal, A.mult)
     ts(("l4", 0, 18), ("ones", 0, 18), t4, None, A.mult)
-    ts(("yy", 0, COLS), ("ca", 0, COLS), C - 0.5, float(C), A.is_gt, A.mult)
+    for a, b in ((0, 10), (10, 18), (18, COLS)):
+        gather("SV", ("pure", 16 * a, 16 * b), ("m16", 0, 16), ("l16", 0, b - a))
+    for a, b in ((0, 6), (6, 12), (12, 18)):
+        gather("SV", ("mask4", 16 * a, 16 * b), ("m16", 16, 20), ("l4", 0, b - a))
+    ts(("chain", 0, 400), ("pure", 0, 400), 1.0 / (2048 * BIG), None, A.max)
+    ts(SC, p16, 15.0, 1.0 / BIG, A.is_equal, A.max)
     ts(HALF, SC, 0.5, None, A.mult)
+    ts(("sc", 6, 7), p16, 15.0, BIG, A.not_equal, A.mult)
     ts(START, ("sc", 6, 7), 1.0, BASE + CARRY, A.max, A.mult)
-    tt(("ca", 0, COLS), ("ca", 0, COLS), ("yy", 0, COLS), A.subtract)
     ts(("sc", 7, 8), p4, 3.0, 1.0 / BIG, A.is_equal, A.max)
-    cp(("offu", 0, 8), ("offui", 0, 8))
-    cp(("halo", 0, COLS), ("ca", 0, COLS))
     ts(SC4, ("sc", 7, 8), 2.0, None, A.mult)
     ts(T4, t4, -4.0, None, A.add)
+    ts(("sc", 5, 6), p16, 18.0, None, A.mult)
+    ts(("cc", 0, COLS), ("ca", 0, COLS), ("sc", 5, 6), None, A.add)
+    ts(("natl", 0, 18), ("ca", STAGES, COLS), ("sc", 5, 6), None, A.add)
+    ts(("cd", 0, COLS), ("cc", 0, COLS), C - 0.5, float(C), A.is_gt, A.mult)
+    tt(("cc", 0, COLS), ("cc", 0, COLS), ("cd", 0, COLS), A.subtract)
+    cp(("halo", 0, COLS), ("cc", 0, COLS))
+    cp(("offu", 0, 8), ("offui", 0, 8))
+    ts(("ahead", 0, 8), ("cb", 0, 8), q16, None, A.add)
+    scan(("soo", 0, C), ("pure", 0, C), ("lam", 0, C))
+    ts(("order", 0, 18), readout("soo", 0, 18), SC, -1.0, A.mult, A.add)
+
+    quant("u", 0, 128, "ut")
+    pick("ur", 0, 128, "u", 128, ("offu", 0, 8))
+    quant("v", 0, 128, "vt")
+    for a, b in PART:
+        quant("n", a, b, "xin")
+    for a, b in PART:
+        pick("x0", a, b, "n", C, ("natl", a // 16, b // 16))
+    for c, src in enumerate(("tai", "tbi")):
+        cp(("ln", 18 * c, 18 * c + 18), (src, 0, 18))
+        for a, b in ((0, 8), (8, 18)):
+            gather("SV", ("rowa", C * c + 16 * a, C * c + 16 * b), ("lam", 0, C), ("ln", 18 * c + a, 18 * c + b))
+        for a, b in ((0, 8), (8, 18)):
+            gather("SV", ("rowb", C * c + 16 * a, C * c + 16 * b), ("rowa", C * c, C * c + C), ("natl", a, b))
+        scan(("sot", C * c, C * c + C), ("pure", 0, C), ("rowb", C * c, C * c + C))
+        for dst in ("lab", "ab"):
+            ts((dst, 18 * c, 18 * c + 18), readout("sot", 18 * c, 18 * c + 18), SC, -1.0, A.mult, A.add)
+    tt(("m2", 0, 18), ("ab", 0, 18), ("ab", 18, 36), A.add)
+    tt(("m2", 18, 36), ("ab", 18, 36), ("ab", 0, 18), A.subtract)
+    ts(("mean", 0, 18), ("m2", 0, 18), 0.5, None, A.mult)
+    ts(("dd", 0, 18), ("m2", 18, 36), HALF, None, A.mult)
+    cp(("sn", 0, 18), ("sti", 0, 18))
+    for a, b in ((0, 8), (8, 18)):
+        gather("SV", ("rn", 16 * a, 16 * b), ("lam", 0, C), ("sn", a, b), scale=2.0)
+    for a, b in ((0, 8), (8, 16), (16, COLS)):
+        gather("SV", ("r", 16 * a, 16 * b), ("rn", 0, C), ("halo", a, b))
+
+    head = [(0, CHUNK[0][1], 0), (CHUNK[0][1], COLS, AT[1])]
 
     def first_list():
-        for a, b, at in ((0, CHUNK[0][1], 0), (CHUNK[0][1], COLS, AT[1])):
+        for a, b, at in head:
+            scan(("sol", 16 * a, 16 * b), ("pure", 16 * a, 16 * b), ("r", 16 * a, 16 * b))
             ts(("sl", at, at + b - a), readout("sol", a, b), HALF, -1.0, A.mult, A.add)
-
-    cp(("sn", 0, 18), ("sti", 0, 18))
-    gather("S", ("rn", 0, C), ("enc", 0, C), ("sn", 0, 18))
-    quant("u", 0, 128, "ut")
-    gather("S", ("r", 0, 400), ("rn", 0, C), ("halo", 0, COLS))
-    ts(("chain", 0, 400), ("pure", 0, 400), 1.0 / (2048 * BIG), None, A.max)
-    op("V", lambda e: e.tensor_copy(T.qur[:, 0:128].bitcast(dt.uint32), T.qu[:, 0:128].bitcast(dt.uint32).indirect(T.offu[:, 0:8])), [("qu", 0, 128), ("offu", 0, 8)], [("qur", 0, 128)])
-    op("S", lambda e: e.activation(T.pur[:, 0:128], T.pu[:, 0:128].indirect(T.offu[:, 0:8]), F.Copy), [("qu", 0, 128), ("offu", 0, 8)], [("pur", 0, 128)])
-
-    def quant_x(r, hf):
-        quant("x%d" % r, *PART[hf], "xt%d" % r if r else "xin")
-
-    def score_part(r, hf):
-        a, b = PART[hf]
-        mm(hf, "ur", 0, "x%d" % r, a, b)
-        act(("sg", a, b), bank(hf, b - a), F.Sign, bias=TINY)
-
-    def piece(q, buf, i, b, a, n, at):
-        move(q, (buf, 4 * a + b, 4 * (a + n), 4), ("ps", 512 * i + at, 512 * i + at + n))
-
-    def unpack(r, hf, b):
-        mm(3 - hf + b, "e", 128 * b, "x%d" % r, *PART[hf])
-
-    def unpacked(q, hf, b):
-        piece(q, "tt", 3 - hf + b, b, PART[hf][0], PART[hf][1] - PART[hf][0], 0)
-
-    def early_lanes(r):
-        for b in range(OPT["early"]):
-            unpack(r, 0, b)
-            unpacked("S", 0, b)
-
-    def val_part(hf):
-        a, b = PART[hf]
-        tt(("val", a, b), ("sg", a, b), ("enc", a, b), A.mult)
-
-    def quant_e(b):
-        quant("e", 128 * b, 128 * b + 128, "eb", 3 - b)
-
-    quant_x(0, 0)
-    quant_x(0, 1)
-    score_part(0, 0)
-    scan(("sol", 0, 400), ("pure", 0, 400), ("r", 0, 400))
-    score_part(0, 1)
-    cp(("lab", 0, 18), ("tai", 0, 18))
-    cp(("lab", 18, 36), ("tbi", 0, 18))
     first_list()
-    val_part(0)
-    val_part(1)
-
-    def differences():
-        tt(("dd", 0, 18), ("ab", 18, 36), ("ab", 0, 18), A.subtract)
-        tt(("dd", 18, 36), ("ab", 0, 18), ("ab", 18, 36), A.subtract)
-
-    def both(f, h):
-        return lambda: (f(), h())
-
-    later = [
-        both(lambda: quant_e(0), lambda: ts(("ahead", 0, 8), ("cb", 0, 8), q16, None, A.add)),
-        lambda: quant_e(1), lambda: quant_e(2), lambda: quant_e(3),
-        lambda: scan(("so4", 0, C), ("pure", 0, C), ("lam", 0, C)),
-        both(lambda: cp(("ab", 0, 18), ("tai", 0, 18)), lambda: cp(("ab", 18, 36), ("tbi", 0, 18))),
-        lambda: ts(("order", 0, 18), readout("so4", 0, 18), SC, -1.0, A.mult, A.add),
-    ]
 
     def span(k, t):
         a, b = CHUNK[k]
         return max(a, t), b
 
-    def mirror(q, c, a, b):
-        end = MID - 2 * b - 2 + c
-        out, src = T.w[:, MID - 2 * a - 2 + c:(end if end >= 0 else None):-2], T.w[:, MID + 2 * a + 2 + c:MID + 2 * b + 2 + c:2]
-        op(q, (lambda e: e.tensor_copy(out, src)) if q == "V" else lambda e: e.activation(out, src, F.Copy),
-           [("w", MID + 2 * a + 2 + c, MID + 2 * b + 2 + c, 2)], [("w", MID - 2 * a - 2 + c, end, -2)])
-
-    def table(q, c, a, b):
-        gather(q, ("w", MID + 2 + 32 * a + c, MID + 2 + 32 * b + c, 2), ("val", 0, C), ("lab", 18 * c + a, 18 * c + b))
-
-    for r in range(3):
+    def one_round(r):
         partner = T.cores[rank ^ STEP[r]]
         rid, pid = topo.addr(partner, core)
         engines = topo.engines(core, partner)
         mask = sum(1 << e for e in engines)
-        ne = len(engines)
-        qx, lx, own, arr = "x%d" % r, "l%d" % r, "own%d" % r, "arr%d" % r
-        got_t = [7, 0, 1, 6]
+        qx, lx, own, arr, xt, last = "x%d" % r, "l%d" % r, "own%d" % r, "arr%d" % r, "xt%d" % (r + 1), r == 2
 
-        before("P", [("q" + qx, 0, C)])
-        g.remote_dma(T["q" + lx][:, :].bitcast(dt.uint8), T["q" + qx][:, :].bitcast(dt.uint8), T.sem["ax%d" % r], T.sem.left, pid, rid, mask)
-        g.remote_dma(T["p" + lx][:, :], T["p" + qx][:, :], T.sem["ax%d" % r], T.sem.left, pid, rid, mask)
-        count["left"] = count.get("left", 0) + 2 * ne
-        arrival("ax%d" % r, 2 * ne, [("q" + lx, 0, C)])
-        arrival("al%d" % r, ne, [(arr, 0, 72)])
-        early = OPT["early"] if r else 0
-        lanes = [(0, b) for b in range(early, 4)] + [(1, b) for b in range(4)]
-        products = [(3 - hf + b, lambda hf=hf, b=b: unpack(r, hf, b)) for hf, b in lanes]
-        products += [(got_t[b], lambda b=b: mm(got_t[b], "e", 128 * b, lx, 0, C)) for b in range(4)]
-        held = set()
+        def send(sem, pairs, rd, wr, time):
+            def call(dst, src):
+                return lambda e: (e.remote_dma(dst, src, T.sem[sem], T.sem.left, pid, rid, mask), len(engines))[1]
+            sent = [op({"P": (call(dst, src), time)}, rd, [], kind="remote", busy=200.0) for dst, src in pairs]
+            op({None: ((sem, len(pairs) * len(engines)), 0.0)}, [], wr, kind="arrival", behind=sent)
 
-        def multiply():
-            while products and products[0][0] not in held:
-                i, call = products.pop(0)
-                held.add(i)
-                call()
+        for hf, (a, b) in enumerate(PART):
+            mm(hf, "ur", 0, qx, a, b)
+            sign(("sg", a, b), bank(hf, b - a))
+            tt(("val", a, b), ("sg", a, b), ("enc", a, b), A.mult)
 
-        def lane(q):
-            hf, b = lanes.pop(0)
-            unpacked(q, hf, b)
-            held.discard(3 - hf + b)
-            multiply()
+        send("ax%d" % r, [(T["q" + lx][:, :].bitcast(dt.uint8), T["q" + qx][:, :].bitcast(dt.uint8)), (T["p" + lx][:, :], T["p" + qx][:, :])],
+             [("q" + qx, 0, C), ("p" + qx, 0, C)], [("q" + lx, 0, C)], OPT["tile"])
+        for hf, (a, b) in enumerate(PART):
+            for k in range(4):
+                mm(3 - hf + k, "e", 128 * k, qx, a, b)
+                move("SV", ("tt", 4 * a + k, 4 * b, 4), bank(3 - hf + k, b - a))
+        for k, i in enumerate((7, 0, 1, 6)):
+            mm(i, "e", 128 * k, lx, 0, C)
+            for a in (0, C // 2):
+                move("SV", ("tq", 4 * a + k, 4 * a + 2 * C, 4), bank(i, C // 2, a))
 
-        head = [(0, CHUNK[0][1], 0), (CHUNK[0][1], COLS, AT[1])]
-
-        def signs(k):
-            a, b, at = head[k]
-            gather("S", ("r0", 16 * a, 16 * b), ("sg", 0, C), ("sl", at, at + b - a), scale=0.5)
-
-        def sign_scan(k):
-            a, b, at = head[k]
+        for c, q, cuts in ((0, OPT["gq"][0], OPT["ga"]), (1, OPT["gq"][1], OPT.get("gb", []))):
+            for a, b in zip([0] + cuts, cuts + [18]):
+                gather(q, ("w", MID + 2 + 32 * a + c, MID + 2 + 32 * b + c, 2), ("val", 0, C), ("lab", 18 * c + a, 18 * c + b))
+        for a, b, at in head:
+            gather(OPT["g0"], ("r0", 16 * a, 16 * b), ("sg", 0, C), ("sl", at, at + b - a), scale=0.5)
             scan(("so0", 16 * a, 16 * b), ("pure", 16 * a, 16 * b), ("r0", 16 * a, 16 * b))
-
-        def sign_add(k):
-            a, b = max(head[k][0], 1), head[k][1]
+            a = max(a, 1)
             tt(("yy", a, b), readout("so0", a - 1, b - 1), readout("sol", a, b), A.add)
-
-        def sign_list(k):
-            a, b, at = max(head[k][0], 1), head[k][1], head[k][2]
             ts(("off", at, at + b - a), ("yy", a, b), SC, 0.5, A.mult, A.add)
+        for c in range(2):
+            for a in (0, C // 2):
+                b = a + C // 2
+                move("SV", ("w", MID - 2 * a - 2 + c, MID - 2 * b - 2 + c, -2), ("w", MID + 2 * a + 2 + c, MID + 2 * b + 2 + c, 2))
 
-        ga, gb = OPT["ga"], OPT["gb"]
-        signs(0)
-        signs(1)
-        sign_scan(0)
-        table("V", 0, 0, ga)
-        table("S", 1, 0, gb)
-        sign_add(0)
-        sign_scan(1)
-        table("V", 0, ga, 18)
-        sign_list(0)
-        sign_add(1)
-        if gb < 18:
-            table("V", 1, gb, 18)
-        sign_list(1)
-
-        rest = list(later) if r == 0 else []
-        if r:
-            multiply()
-        else:
-            rest[3] = both(rest[3], multiply)
-        rest += [differences]
-        rest += [lambda: lane("V")] * len(lanes)
-        late_pieces = [(b, a) for a in (0, 144) for b in range(4)]
-
-        def stage_gather(k, t):
-            a, b = span(k, t)
-            win = ("w", MID, MID + 2 * C + 2) if t == 1 else ("w", 0, MID + 2 * C + 2)
-            off = ("off", AT[k], AT[k] + b - a)
-            if t == STAGES:
-                gather("S", ("r", 16 * a, 16 * b), win, off, fn=F.Abs)
-            else:
-                gather("S", ("r", 16 * a, 16 * b), win, off, add=BASE)
-
-        def stage_scan(k, t):
-            a, b = span(k, t)
-            a -= min(k, 1)
-            scan(("so", 16 * (a + k), 16 * (b + k)), ("chain", 16 * a, 16 * b), ("r", 16 * a, 16 * b), START)
-
-        def stage_list(k, t):
+        def offsets(k, t):
             a, b = span(k, t + 1)
             ts(("off", AT[k], AT[k] + b - a), readout("so", a + k, b + k), SC, MID - BASE - CARRY, A.mult, A.add)
-
-        mir = [(lambda n=n: mirror(OPT["mir"][n], n // 2, 144 * (n % 2), 144 * (n % 2) + 144)) for n in range(4)]
-        steps = [(k, t) for t in range(1, STAGES) for k in range(len(CHUNK))]
+            in_turn("V")
+        steps = [(k, t) for t in range(1, STAGES + 1) for k in range(len(CHUNK))]
         for n, (k, t) in enumerate(steps):
-            stage_gather(k, t)
-            for i in range(4):
-                if OPT["mat"][i] == n:
-                    mir[i]()
-            stage_scan(k, t)
+            a, b = span(k, t)
+            win = ("w", MID if t == 1 else 0, MID + 2 * C + 2)
+            if t == STAGES:
+                if k == 0:
+                    offsets(*steps[n - 1])
+                gather("S", ("r", 16 * a, 16 * b), win, ("off", AT[k], AT[k] + b - a), fn=F.Abs)
+                in_turn("S")
+                continue
+            gather("S", ("r", 16 * a, 16 * b), win, ("off", AT[k], AT[k] + b - a), add=BASE)
+            in_turn("S")
+            a -= min(k, 1)
+            scan(("so", 16 * (a + k), 16 * (b + k)), ("chain", 16 * a, 16 * b), ("r", 16 * a, 16 * b), START)
+            in_turn("V")
             if n:
-                stage_list(*steps[n - 1])
-            if t > 1 and rest and k in OPT["fill" if r else "fill0"]:
-                rest.pop(0)()
-        if r == 0:
-            gather("V", ("mask4", 0, C), ("m16", 16, 20), ("l4", 0, 18))
-        for k in range(len(CHUNK)):
-            if k == 0:
-                stage_list(*steps[-1])
-            stage_gather(k, STAGES)
-        while rest:
-            rest.pop(0)()
+                offsets(*steps[n - 1])
 
         done = ("r", 16 * STAGES, 400)
-        gather("V", ("rn", 0, 160), done, ("order", 0, 10))
-        gather("S", ("rn", 160, C), done, ("order", 10, 18))
-        scan(("so4", 0, C), ("mask4", 0, C), ("rn", 0, C))
-        ts((own, 0, 72), ("so4", 3, C, 4), SC4, T4, A.mult, A.add)
-        before("P", [(own, 0, 72)])
-        g.remote_dma(T[arr][:, :], T[own][:, :], T.sem["al%d" % r], T.sem.left, pid, rid, mask)
-        count["left"] += ne
+        cuts = [0, ZPART[0][1], 16 * (CHUNK[-1][0] - STAGES), C]
+        for a, b in zip(cuts, cuts[1:]):
+            scan(("so4", a, b), ("mask4", a, b), ("r", 16 * STAGES + a, 16 * STAGES + b))
+        for hf, (a, b) in enumerate(ZPART):
+            ts((own, a // 4, b // 4), ("so4", a + 3, b, 4), SC4, T4, A.mult, A.add)
+            send("al%d%d" % (r, hf), [(T[arr][:, a // 4:b // 4], T[own][:, a // 4:b // 4])], [(own, a // 4, b // 4)], [(arr, a // 4, b // 4)], OPT["list"])
 
-        xt, last = "xt%d" % (r + 1), r == 2
-        if not last:
-            gather("S", ("r", 0, 16 * STAGES), done, ("ahead", 0, STAGES))
-        for b, a in late_pieces[:2]:
-            piece("S", "tq", got_t[b], b, a, 144, a)
-        gather("S", ("zt", 576, 1152), ("tt", 0, 1152), (own, 36, 72))
-        if not last:
-            scan(("sol", 0, 400), ("pure", 0, 400), ("r", 0, 400))
-        gather("V", ("zt", 0, 576), ("tt", 0, 1152), (own, 0, 36))
-        if not last:
-            first_list()
-        for n, (b, a) in enumerate(late_pieces[2:]):
-            piece("V" if n % 2 == 0 else "S", "tq", got_t[b], b, a, 144, a)
-        if r == 0:
-            quant("v", 0, 128, "vt")
+        for a in range(0, C, OPT["mos"]):
+            b = min(C, a + OPT["mos"])
+            gather("SV", ("zt", 4 * a, 4 * b), ("tt", 0, 4 * C), (own, a // 4, b // 4))
         if last:
-            act(("opr", 0, C), ("rn", 0, C), F.Identity, scale=0.5, bias=-1.0)
+            scan(("sol", 16 * STAGES, 400), ("pure", 0, C), done)
+            ts(("sn", 0, 18), readout("sol", STAGES, COLS), HALF, -1.0, A.mult, A.add)
+            gather("S", ("rn", 0, C), ("nat", 0, C), ("sn", 0, 18))
+            gather("S", ("opr", 0, C), ("rn", 0, C), ("order", 0, 18))
+        else:
+            gather("SV", ("r", 0, 16 * STAGES), done, ("ahead", 0, STAGES))
+            first_list()
 
-        for hf in range(2):
-            a, b = PART[hf]
-            m = a + OPT["zv"][hf]
-            gather("V", ("zp", 4 * a, 4 * m), ("tq", 0, 1152), (arr, a // 4, m // 4))
-            gather("S", ("zp", 4 * m, 4 * b), ("tq", 0, 1152), (arr, m // 4, b // 4))
+        cut = ZPART[0][1]
+        z0, z1, z2 = OPT["zv"]
+        zq = (("V", 0, z0), ("S", z0, cut), ("V", cut, cut + z1), ("V", cut + z1, cut + z2), ("S", cut + z2, C))
+        if OPT["zq"]:
+            zq = [("SV", a, b) for a, b in zip([0] + OPT["zq"], OPT["zq"] + [C])]
+        for q, a, b in zq:
+            if a < b:
+                gather(q, ("zp", 4 * a, 4 * b), ("tq", 0, 4 * C), (arr, a // 4, b // 4))
+        for hf, (a, b) in enumerate(ZPART):
             quant("z", a, b, "zp")
             for k in (0, 2, 1, 3):
                 mm(4 * hf + k, "w", 128 * k, "z", a, b)
-        for hf in range(2):
-            a, b = PART[hf]
-            for k in (0, 2, 1, 3):
-                move("V" if k < 2 else "S", ("h", 4 * a + k, 4 * b, 4), bank(4 * hf + k, b - a), 0.03125)
+                move(OPT["hq"][k], ("h", 4 * a + k, 4 * b, 4), bank(4 * hf + k, b - a), 0.03125)
+        for hf, (a, b) in enumerate(ZPART):
+            quant("h", a, b, "h")
+            in_turn("N")
+            mm(2 + 5 * hf, "ur", 0, "h", a, b)
+            sign(("cs", a, b), bank(2 + 5 * hf, b - a))
 
-        def new_part(hf):
-            a, b = PART[hf]
-            op("V", lambda e: e.tensor_tensor(T[xt][:, 4 * a:4 * b], T.h[:, 0:1152].indirect(T[arr][:, a // 4:b // 4]), T.zt[:, 4 * a:4 * b], A.add),
-               [("h", 0, 1152), (arr, a // 4, b // 4), ("zt", 4 * a, 4 * b)], [(xt, 4 * a, 4 * b)], listed=True)
-
-        def change_scan():
-            scan(("soc", 0, C), ("pure", 0, C), ("cs", 0, C))
-
-        def change():
-            ts(("c01", 0, 18), readout("soc", 0, 18), 0.0, None, A.is_gt)
-
-        def moves():
-            tt(("m2", 0, 18), ("dd", 0, 18), ("c01", 0, 18), A.mult)
-            tt(("m2", 18, 36), ("dd", 18, 36), ("c01", 0, 18), A.mult)
+        def new_cols(a, b):
+            call = lambda e: e.tensor_tensor(T[xt][:, 4 * a:4 * b], T.h[:, 0:4 * C].indirect(T[arr][:, a // 4:b // 4]), T.zt[:, 4 * a:4 * b], A.add)
+            op({"V": (call, fetch("V", 4 * (b - a)))}, [("h", 0, 4 * C), (arr, a // 4, b // 4), ("zt", 4 * a, 4 * b)], [(xt, 4 * a, 4 * b)], listed=True)
+        exchange = [lambda: scan(("soc", 0, C), ("pure", 0, C), ("cs", 0, C)),
+                    lambda: tt(("m2", 0, 18), readout("soc", 0, 18), ("dd", 0, 18), A.mult),
+                    lambda: tt(("ab", 0, 18), ("mean", 0, 18), ("m2", 0, 18), A.add),
+                    lambda: tt(("ab", 18, 36), ("mean", 0, 18), ("m2", 0, 18), A.subtract),
+                    lambda: cp(("lab", 0, 36), ("ab", 0, 36))]
+        cuts = OPT["newlast" if last else "new"]
+        for n, (a, b) in enumerate(zip([0] + cuts, cuts + [C])):
+            new_cols(a, b)
+            in_turn("N")
+            for i in range(OPT["between"][n] if last else 0):
+                exchange.pop(0)()
+                in_turn("N")
+        for a, b in PART:
+            quant("x%d" % (r + 1), a, b, xt)
+        for step in exchange:
+            step()
         if not last:
-            new_part(0)
-        quant("h", 0, C, "h")
-        mm(2, "ur", 0, "h", 0, C)
-        act(("cs", 0, C), bank(2, C), F.Sign, bias=TINY)
-        if last:
-            new_part(0)
-            change_scan()
-            quant_x(r + 1, 0)
-            change()
-            new_part(1)
-            moves()
-            quant_x(r + 1, 1)
-            tt(("ab", 0, 36), ("ab", 0, 36), ("m2", 0, 36), A.add)
-        else:
-            quant_x(r + 1, 0)
-            score_part(r + 1, 0)
-            early_lanes(r + 1)
-            new_part(1)
-            change_scan()
-            quant_x(r + 1, 1)
-            score_part(r + 1, 1)
-            change()
-            val_part(0)
-            moves()
-            tt(("ab", 0, 36), ("ab", 0, 36), ("m2", 0, 36), A.add)
-            val_part(1)
-        cp(("lab", 0, 36), ("ab", 0, 36))
+            ts(("dd", 0, 18), ("m2", 0, 18), SC, -1.0, A.mult, A.mult)
 
-    def out(q, dst, src, rd):
-        op(q, lambda e: e.dma_start(dst, src), [rd], [], dma=True)
-    for hf in range(2):
-        mm(3 + hf, "v", 0, "x3", *PART[hf])
-    out("Y", T.oc[:, :], T.qx3[:, :].bitcast(dt.uint8), ("qx3", 0, C))
-    for hf in range(2):
-        a, b = PART[hf]
-        cp(("yo", a, b), bank(3 + hf, b - a))
-    gather("V", ("opr", C, 2 * C), ("idf", 0, C), ("lab", 0, 18))
-    gather("S", ("opr", 2 * C, 3 * C), ("idf", 0, C), ("lab", 18, 36))
-    out("Y", T.y[:, :], T.yo[:, :], ("yo", 0, C))
+    for r in range(3):
+        one_round(r)
+
+    moved[0] = 0
+    for c in range(2):
+        for a, b in ((0, 8), (8, 18)):
+            gather("SV", ("rowa", C * c + 16 * a, C * c + 16 * b), ("nat", 0, C), ("lab", 18 * c + a, 18 * c + b))
+        for a, b in ((0, 8), (8, 18)):
+            gather("SV", ("opr", C * c + C + 16 * a, C * c + C + 16 * b), ("rowa", C * c, C * c + C), ("order", a, b))
+    for hf, (a, b) in enumerate(PART):
+        pick("o", a, b, "x3", C, ("order", a // 16, b // 16))
+        mm(3 + hf, "v", 0, "o", a, b)
+        move("SV", ("yo", a, b), bank(3 + hf, b - a))
+    dma("S", T.op[:, :], T.opr[0:128:16, :], [("opr", 0, 3 * C)], [], 0)
+    dma("Y", T.y[:, :], T.yo[:, :], [("yo", 0, C)], [], 4 * C)
+    dma("Y", T.oc[:, :], T.qo[:, :].bitcast(dt.uint8), [("qo", 0, C)], [], 0)
     for k in range(4):
-        out("S" if k % 2 else "Y", T.osc[4 * k:4 * k + 4, :], T.px3[32 * k:32 * k + 4, :], ("qx3", 0, C))
-    out("S", T.op[:, :], T.opr[0:128:16, :], ("opr", 0, 3 * C))
+        dma("Y", T.osc[4 * k:4 * k + 4, :], T.po[32 * k:32 * k + 4, :], [("po", 0, C)], [], -300)
     finish()

@@ -14,7 +14,7 @@ BIG = 2.0 ** 40
 CARRY = 6000.0
 BASE = 2047 * CARRY + 1024
 TINY = -2.0 ** -100
-OPT = {"ga": [10], "zv": [88, 16, 56], "new": [160], "wake": 200.0, "grain": 30.0, "list": 1400.0, "tile": 5000.0, "gat": 1.56, "pe": 1.0, "mos": 48, "load": 1600.0, "passes": 6, "turn": "SVN", "newlast": [160, 192, 224, 256], "between": [1, 1, 2, 1, 0], "gq": "VS", "g0": "S", "hq": ["V", "V", "S", "S"], "zq": None}
+OPT = {"ga": [10], "zv": [88, 16, 56], "new": [160], "wake": 200.0, "grain": 30.0, "list": 1400.0, "tile": 5000.0, "gat": 1.56, "pe": 1.3, "vg": [], "cut": 1, "mos": 48, "load": 1600.0, "passes": 6, "turn": "SVNEFP", "assist": [], "lpart": [(0, 160), (160, 288)], "begin": ["g0", "g1", "s0", ("V", 0, 8), ("S", 18, 36), "a0", "s1", ("V", 8, 18), "o0", "a1", "o1"], "newlast": [160], "between": [1, 1, 2, 1, 0], "gq": "VS", "g0": "S", "hq": ["V", "V", "S", "S"], "zq": None}
 
 SCRATCH = {"ps": ("psum", [128, 4096], "float32")}
 
@@ -26,17 +26,17 @@ def _bufs(where, dtype, **cols):
 
 _bufs("sbuf", "bfloat16", xin=1152, xt1=1152, xt2=1152, xt3=1152, ut=512, vt=512, ones=516, eb=516, tm=16, ma=32, mb=32, m16=32,
       pure=400, chain=400, mask4=288, sg=288, cs=288, r0=400, so0=400, soc=288,
-      tt=1152, tq=1152, zt=1152, zp=1152, h=1152)
-for _n, _c in [("u", 128), ("ur", 128), ("v", 128), ("w", 512), ("e", 512), ("z", 288), ("h", 288), ("n", 288), ("o", 288)] + [("x%d" % _r, 288) for _r in range(4)] + [("l%d" % _r, 288) for _r in range(3)]:
+      tt=1152, tq=1152, zt=1152, zp=1152, h=1152, hg=1152)
+for _n, _c in [("u", 128), ("ur", 128), ("v", 128), ("w", 512), ("e", 512), ("z", 288), ("h", 288)] + [("x%d" % _r, 288) for _r in range(4)] + [("l%d" % _r, 288) for _r in range(3)]:
     SCRATCH["q" + _n] = ("sbuf", [128, _c], "float8_e4m3fn_x4")
     SCRATCH["p" + _n] = ("sbuf", [128, _c], "uint8")
-_bufs("sbuf", "int32", pi=8, pk=8, offui=8, tai=18, tbi=18, sti=18)
-_bufs("sbuf", "float32", pf=8, sc=8, enc=288, lam=288, nat=288, rowa=576, rowb=576, sot=576, soo=288, val=288, ab=36, dd=18, mean=18, m2=36, yy=26, ca=26, cb=8, cc=26, cd=26,
-      w=1160, r=400, so=496, rn=288, so4=288, sol=400, opr=864, yo=288)
-_bufs("sbuf", "uint16", offu=8, l16=26, l4=18, order=18, natl=18, ln=36, halo=26, ahead=8, sn=18, sl=28, lab=36, off=28, own0=72, own1=72, own2=72, arr0=72, arr1=72, arr2=72)
+_bufs("sbuf", "int32", pi=8, pk=8, offui=8, tai=18, tbi=18, sti=18, qi=36, lo=36, hi=36, d18=72)
+_bufs("sbuf", "float32", pf=8, sc=12, enc=288, lam=288, nat=288, rowa=576, soo=288, val=288, ab=36, dd=18, mean=18, m2=36, yy=26, f1=72, f2=72, cb=8, gl=36, tl=36, nv=36, abn=36,
+      w=1160, r=400, so=496, rn=320, so4=288, sol=400, opr=288, yo=288, ra=288, so5=288, so6=288)
+_bufs("sbuf", "uint16", offu=8, l16=26, l4=18, order=18, ownn=72, arrn=72, sout=24, sin=24, ahead=8, sn=18, sl=28, lab=36, off=28, own0=72, own1=72, own2=72, arr0=72, arr1=72, arr2=72)
 
-DMAS = ["d%d" % _i for _i in range(20)]
-SEMAPHORES = ["cV", "cS", "cT", "cP", "left"] + ["ax%d" % _r for _r in range(3)] + ["al%d%d" % (_r, _h) for _r in range(3) for _h in range(2)] + DMAS
+DMAS = ["d%d" % _i for _i in range(26)]
+SEMAPHORES = ["cV", "cS", "cT", "cP", "left", "as"] + ["ax%d" % _r for _r in range(3)] + ["al%d%d" % (_r, _h) for _r in range(3) for _h in range(3)] + DMAS
 CYCLE = 0.83
 ORDER = []
 
@@ -229,6 +229,7 @@ def rank_program(g, core, T, topo):
     def iota(out, pat, base, cm):
         k = {} if SCRATCH[out[0]][2] == "int32" else {"allow_small_or_imprecise_dtypes": True}
         op({"P": (lambda e: e.iota(ap(out), pat, base, cm, **k), 130 + 2 * size(out) * CYCLE)}, [], [out])
+        in_turn("P")
 
     def scan(out, mask, row, first=0.0):
         op({"V": (lambda e: e.tensor_tensor_scan(ap(out), ap(mask), ap(row), ap(first), A.mult, A.add), cycles(out, mask, row))}, rgs(mask, row, first), [out])
@@ -263,27 +264,24 @@ def rank_program(g, core, T, topo):
         loads[q].append(dma(q, ap(dst).bitcast(dt.uint8) if dst[0] == "qw" else ap(dst), src, [], [dst], nbytes, loads[q][-1:]))
 
     cut = 4 * PART[0][1]
+    load("S", ("sti", 0, 18), T.st[:, :], 72)
     load("Y", ("tai", 0, 18), T.ta[:, :], 72)
     load("S", ("tbi", 0, 18), T.tb[:, :], 72)
     load("Y", ("xin", 0, cut), T.x[:, 0:cut], 2 * cut)
-    load("S", ("sti", 0, 18), T.st[:, :], 72)
     load("S", ("ut", 0, 512), T.u[:, :], 1024)
     load("Y", ("xin", cut, 4 * C), T.x[:, cut:4 * C], 8 * C - 2 * cut)
-    load("Y", ("qw", 0, 512), T.wc[:, :], 2048)
-    load("Y", ("pw", 0, 512), T.ws[:, :], 512)
-    load("Y", ("vt", 0, 512), T.v[:, :], 1024)
 
     iota(("pi", 0, 5), [[1, 5]], 0, 1)
     iota(("tm", 0, 16), [[1, 16]], 0, 0)
-    iota(("ca", 0, COLS), [[-1, COLS]], COLS - 1, 0)
-    iota(("lam", 0, C), [[1, 16], [-16, 18]], 16 * 17 + 1, 0)
-    iota(("nat", 0, C), [[-1, 18], [18, 16]], 17, 0)
-    iota(("offui", 0, 8), [[16, 8]], 0, 0)
     iota(("enc", 0, C), [[2, C]], 2, 0)
-    iota(("cb", 0, 8), [[16, 8]], 16 * (18 - STAGES), 0)
     fill(("ones", 0, 516), 1.0)
     fill(("w", MID, MID + 2), 0.0)
     op({"P": (lambda e: e.affine_select(T.eb[:, :], T.ones[:, :], [[1, 516]], A.is_equal, 0.0, -3, -4), 170 + 2 * 516 * CYCLE)}, [("ones", 0, 516)], [("eb", 0, 516)])
+    in_turn("P")
+    iota(("offui", 0, 8), [[16, 8]], 0, 0)
+    iota(("lam", 0, C), [[1, 16], [-16, 18]], 16 * 17 + 1, 0)
+    iota(("cb", 0, 8), [[16, 8]], 16 * (18 - STAGES), 0)
+    iota(("nat", 0, C), [[-1, 18], [18, 16]], 17, 0)
     for b in range(4):
         quant("e", 128 * b, 128 * b + 128, "eb", 3 - b)
 
@@ -307,17 +305,14 @@ def rank_program(g, core, T, topo):
     ts(("chain", 0, 400), ("pure", 0, 400), 1.0 / (2048 * BIG), None, A.max)
     ts(SC, p16, 15.0, 1.0 / BIG, A.is_equal, A.max)
     ts(HALF, SC, 0.5, None, A.mult)
-    ts(("sc", 6, 7), p16, 15.0, BIG, A.not_equal, A.mult)
-    ts(START, ("sc", 6, 7), 1.0, BASE + CARRY, A.max, A.mult)
+    ts(("sc", 8, 9), p16, 15.0, BIG, A.not_equal, A.mult)
+    ts(("sc", 6, 7), ("sc", 8, 9), 1.0, None, A.max)
+    ts(START, ("sc", 8, 9), 1.0, BASE + CARRY, A.max, A.mult)
     ts(("sc", 7, 8), p4, 3.0, 1.0 / BIG, A.is_equal, A.max)
     ts(SC4, ("sc", 7, 8), 2.0, None, A.mult)
     ts(T4, t4, -4.0, None, A.add)
-    ts(("sc", 5, 6), p16, 18.0, None, A.mult)
-    ts(("cc", 0, COLS), ("ca", 0, COLS), ("sc", 5, 6), None, A.add)
-    ts(("natl", 0, 18), ("ca", STAGES, COLS), ("sc", 5, 6), None, A.add)
-    ts(("cd", 0, COLS), ("cc", 0, COLS), C - 0.5, float(C), A.is_gt, A.mult)
-    tt(("cc", 0, COLS), ("cc", 0, COLS), ("cd", 0, COLS), A.subtract)
-    cp(("halo", 0, COLS), ("cc", 0, COLS))
+    ts(("sc", 9, 10), t4, -1.0, -34.0, A.mult, A.add)
+    ts(("sc", 10, 11), t4, 17.0, 4.0 * 272, A.mult, A.add)
     cp(("offu", 0, 8), ("offui", 0, 8))
     ts(("ahead", 0, 8), ("cb", 0, 8), q16, None, A.add)
     scan(("soo", 0, C), ("pure", 0, C), ("lam", 0, C))
@@ -325,37 +320,45 @@ def rank_program(g, core, T, topo):
 
     quant("u", 0, 128, "ut")
     pick("ur", 0, 128, "u", 128, ("offu", 0, 8))
-    quant("v", 0, 128, "vt")
     for a, b in PART:
-        quant("n", a, b, "xin")
-    for a, b in PART:
-        pick("x0", a, b, "n", C, ("natl", a // 16, b // 16))
-    for c, src in enumerate(("tai", "tbi")):
-        cp(("ln", 18 * c, 18 * c + 18), (src, 0, 18))
-        for a, b in ((0, 8), (8, 18)):
-            gather("SV", ("rowa", C * c + 16 * a, C * c + 16 * b), ("lam", 0, C), ("ln", 18 * c + a, 18 * c + b))
-        for a, b in ((0, 8), (8, 18)):
-            gather("SV", ("rowb", C * c + 16 * a, C * c + 16 * b), ("rowa", C * c, C * c + C), ("natl", a, b))
-        scan(("sot", C * c, C * c + C), ("pure", 0, C), ("rowb", C * c, C * c + C))
-        for dst in ("lab", "ab"):
-            ts((dst, 18 * c, 18 * c + 18), readout("sot", 18 * c, 18 * c + 18), SC, -1.0, A.mult, A.add)
-    tt(("m2", 0, 18), ("ab", 0, 18), ("ab", 18, 36), A.add)
-    tt(("m2", 18, 36), ("ab", 18, 36), ("ab", 0, 18), A.subtract)
-    ts(("mean", 0, 18), ("m2", 0, 18), 0.5, None, A.mult)
-    ts(("dd", 0, 18), ("m2", 18, 36), HALF, None, A.mult)
+        quant("x0", a, b, "xin")
     cp(("sn", 0, 18), ("sti", 0, 18))
-    for a, b in ((0, 8), (8, 18)):
-        gather("SV", ("rn", 16 * a, 16 * b), ("lam", 0, C), ("sn", a, b), scale=2.0)
-    for a, b in ((0, 8), (8, 16), (16, COLS)):
-        gather("SV", ("r", 16 * a, 16 * b), ("rn", 0, C), ("halo", a, b))
+    for a, b, at in ((0, 8, 0), (8, 18, 8), (0, 2, 18)):
+        gather("SV", ("rn", 16 * at, 16 * (at + b - a)), ("enc", 0, C), ("sn", a, b))
+
+    def deal(dst, at, src, a):
+        loads["Y"].append(dma("Y", T[dst][:, at:at + 18], T[src][0:128:16, a:a + C], [(src, a, a + C)], [(dst, at, at + 18)], 72, loads["Y"][-1:]))
+    moved[0] = 0
+    deal("gl", 0, "rn", 0)
+    deal("gl", 18, "rn", 18)
+    load("Y", ("qw", 0, 512), T.wc[:, :], 2048)
+    load("Y", ("pw", 0, 512), T.ws[:, :], 512)
+    load("Y", ("vt", 0, 512), T.v[:, :], 1024)
+    quant("v", 0, 128, "vt")
+    moved[0] = 8000
+    for c, src in enumerate(("tai", "tbi")):
+        cp(("lab", 18 * c, 18 * c + 18), (src, 0, 18))
+        for a, b in ((0, 6), (6, 12), (12, 18)):
+            gather("SV", ("rowa", C * c + 16 * a, C * c + 16 * b), ("lam", 0, C), ("lab", 18 * c + a, 18 * c + b))
+        deal("tl", 18 * c, "rowa", C * c)
+        ts(("ab", 18 * c, 18 * c + 18), ("tl", 18 * c + 17, 18 * c - 1, -1), -1.0, None, A.add)
+
+    def halves(src):
+        tt(("m2", 0, 18), (src, 0, 18), (src, 18, 36), A.add)
+        tt(("m2", 18, 36), (src, 18, 36), (src, 0, 18), A.subtract)
+        ts(("mean", 0, 18), ("m2", 0, 18), 0.5, None, A.mult)
+        ts(("dd", 0, 18), ("m2", 18, 36), HALF, None, A.mult)
+    halves("ab")
 
     head = [(0, CHUNK[0][1], 0), (CHUNK[0][1], COLS, AT[1])]
+    ts(readout("sol", 0, COLS), ("gl", COLS - 1, -1, -1), ("sc", 6, 7), None, A.mult)
+    for a, b, at in head:
+        ts(("sl", at, at + b - a), ("gl", COLS - 1 - a, COLS - 1 - b, -1), 0.5, -1.0, A.mult, A.add)
 
     def first_list():
         for a, b, at in head:
             scan(("sol", 16 * a, 16 * b), ("pure", 16 * a, 16 * b), ("r", 16 * a, 16 * b))
             ts(("sl", at, at + b - a), readout("sol", a, b), HALF, -1.0, A.mult, A.add)
-    first_list()
 
     def span(k, t):
         a, b = CHUNK[k]
@@ -384,21 +387,38 @@ def rank_program(g, core, T, topo):
         for hf, (a, b) in enumerate(PART):
             for k in range(4):
                 mm(3 - hf + k, "e", 128 * k, qx, a, b)
-                move("SV", ("tt", 4 * a + k, 4 * b, 4), bank(3 - hf + k, b - a))
+                n = (b - a) // OPT["cut"]
+                for c in range(a, b, n):
+                    move("SV", ("tt", 4 * c + k, 4 * (c + n), 4), bank(3 - hf + k, n, c - a))
         for k, i in enumerate((7, 0, 1, 6)):
             mm(i, "e", 128 * k, lx, 0, C)
-            for a in (0, C // 2):
-                move("SV", ("tq", 4 * a + k, 4 * a + 2 * C, 4), bank(i, C // 2, a))
+            n = C // (2 * OPT["cut"])
+            for a in range(0, C, n):
+                move("SV", ("tq", 4 * a + k, 4 * (a + n), 4), bank(i, n, a))
 
-        for c, q, cuts in ((0, OPT["gq"][0], OPT["ga"]), (1, OPT["gq"][1], OPT.get("gb", []))):
-            for a, b in zip([0] + cuts, cuts + [18]):
-                gather(q, ("w", MID + 2 + 32 * a + c, MID + 2 + 32 * b + c, 2), ("val", 0, C), ("lab", 18 * c + a, 18 * c + b))
-        for a, b, at in head:
-            gather(OPT["g0"], ("r0", 16 * a, 16 * b), ("sg", 0, C), ("sl", at, at + b - a), scale=0.5)
-            scan(("so0", 16 * a, 16 * b), ("pure", 16 * a, 16 * b), ("r0", 16 * a, 16 * b))
-            a = max(a, 1)
-            tt(("yy", a, b), readout("so0", a - 1, b - 1), readout("sol", a, b), A.add)
-            ts(("off", at, at + b - a), ("yy", a, b), SC, 0.5, A.mult, A.add)
+        def table(q, a, b):
+            c = a // 18
+            gather(q, ("w", MID + 2 + 32 * (a - 18 * c) + c, MID + 2 + 32 * (b - 18 * c) + c, 2), ("val", 0, C), ("lab", a, b))
+
+        def first(step, k):
+            a, b, at = head[k]
+            if step in "gs":
+                b = min(b, COLS - 1)
+            if step == "g":
+                gather("S", ("r0", 16 * a, 16 * b), ("sg", 0, C), ("sl", at, at + b - a), scale=0.5)
+            elif step == "s":
+                scan(("so0", 16 * a, 16 * b), ("pure", 16 * a, 16 * b), ("r0", 16 * a, 16 * b))
+            elif step == "a":
+                tt(("yy", max(a, 1), b), readout("so0", max(a, 1) - 1, b - 1), readout("sol", max(a, 1), b), A.add)
+            else:
+                ts(("off", at, at + b - max(a, 1)), ("yy", max(a, 1), b), SC, 0.5, A.mult, A.add)
+        for x in OPT["begin"]:
+            if len(x) == 2:
+                first(x[0], int(x[1]))
+                in_turn("F" if x[0] == "g" else "E")
+            else:
+                table(*x)
+                in_turn("F" if x[0] == "S" else "E")
         for c in range(2):
             for a in (0, C // 2):
                 b = a + C // 2
@@ -418,8 +438,10 @@ def rank_program(g, core, T, topo):
                 gather("S", ("r", 16 * a, 16 * b), win, ("off", AT[k], AT[k] + b - a), fn=F.Abs)
                 in_turn("S")
                 continue
-            gather("S", ("r", 16 * a, 16 * b), win, ("off", AT[k], AT[k] + b - a), add=BASE)
-            in_turn("S")
+            q = "V" if (k, t) in OPT["vg"] else "S"
+            gather(q, ("r", 16 * a, 16 * b), win, ("off", AT[k], AT[k] + b - a), add=BASE)
+            if q == "S":
+                in_turn("S")
             a -= min(k, 1)
             scan(("so", 16 * (a + k), 16 * (b + k)), ("chain", 16 * a, 16 * b), ("r", 16 * a, 16 * b), START)
             in_turn("V")
@@ -427,30 +449,58 @@ def rank_program(g, core, T, topo):
                 offsets(*steps[n - 1])
 
         done = ("r", 16 * STAGES, 400)
-        cuts = [0, ZPART[0][1], 16 * (CHUNK[-1][0] - STAGES), C]
+        cuts = sorted(set([0, 16 * (CHUNK[-1][0] - STAGES)] + [b for a, b in OPT["lpart"]]))
         for a, b in zip(cuts, cuts[1:]):
             scan(("so4", a, b), ("mask4", a, b), ("r", 16 * STAGES + a, 16 * STAGES + b))
-        for hf, (a, b) in enumerate(ZPART):
+        for hf, (a, b) in enumerate(OPT["lpart"]):
             ts((own, a // 4, b // 4), ("so4", a + 3, b, 4), SC4, T4, A.mult, A.add)
             send("al%d%d" % (r, hf), [(T[arr][:, a // 4:b // 4], T[own][:, a // 4:b // 4])], [(own, a // 4, b // 4)], [(arr, a // 4, b // 4)], OPT["list"])
 
-        for a in range(0, C, OPT["mos"]):
-            b = min(C, a + OPT["mos"])
-            gather("SV", ("zt", 4 * a, 4 * b), ("tt", 0, 4 * C), (own, a // 4, b // 4))
+        mine, theirs = own, arr
         if last:
-            scan(("sol", 16 * STAGES, 400), ("pure", 0, C), done)
-            ts(("sn", 0, 18), readout("sol", STAGES, COLS), HALF, -1.0, A.mult, A.add)
-            gather("S", ("rn", 0, C), ("nat", 0, C), ("sn", 0, 18))
-            gather("S", ("opr", 0, C), ("rn", 0, C), ("order", 0, 18))
+            mine, theirs = "ownn", "arrn"
+            for a, b in ((0, 8), (8, 18)):
+                gather("SV", ("rn", 16 * a, 16 * b), done, ("order", a, b))
+            scan(("soo", 0, C), ("pure", 0, C), ("rn", 0, C))
+            ts(("sout", 0, 18), readout("soo", 0, 18), HALF, -1.0, A.mult, A.add)
+            send("as", [(T.sin[:, 0:18], T.sout[:, 0:18])], [("sout", 0, 18)], [("sin", 0, 18)], OPT["list"])
+            for a, b in ((0, 8), (8, 18)):
+                gather("SV", ("ra", 16 * a, 16 * b), ("enc", 0, C), ("sin", a, b))
+            for dst, so, row in ((mine, "so5", "rn"), (theirs, "so6", "ra")):
+                for a, b in PART:
+                    scan((so, a, b), ("mask4", a, b), (row, a, b))
+                    ts((dst, a // 4, b // 4), (so, a + 3, b, 4), SC4, T4, A.mult, A.add)
+            gather("SV", ("opr", 0, C), ("nat", 0, C), ("sout", 0, 18))
+            cp(("qi", 0, 36), ("lab", 0, 36))
+            ts(("lo", 0, 36), ("qi", 0, 36), 15, None, A.bitwise_and)
+            ts(("hi", 0, 36), ("qi", 0, 36), 4, None, A.arith_shift_right)
+            ts(("tl", 0, 36), ("lo", 0, 36), 18.0, 17.0, A.mult, A.add)
+            tt(("nv", 0, 36), ("tl", 0, 36), ("hi", 0, 36), A.subtract)
+            halves("nv")
         else:
             gather("SV", ("r", 0, 16 * STAGES), done, ("ahead", 0, STAGES))
             first_list()
+        if r == 0:
+            for a, b, at in head:
+                gather("SV", ("r", 16 * a, 16 * b), ("lam", 0, C), ("sl", at, at + b - a), scale=2.0)
+            first_list()
+            theirs = "arrn"
+            for a, b in OPT["lpart"]:
+                a, b = a // 4, b // 4
+                ts(("d18", a, b), (arr, a, b), ("sc", 9, 10), 1.0 / 72, A.add, A.mult)
+                ts(("f1", a, b), (arr, a, b), -16.0, ("sc", 10, 11), A.mult, A.add)
+                ts(("f2", a, b), ("d18", a, b), 4.0 * 289, None, A.mult)
+                tt(("f1", a, b), ("f1", a, b), ("f2", a, b), A.add)
+                cp((theirs, a, b), ("f1", a, b))
+        for a in range(0, C, OPT["mos"]):
+            b = min(C, a + OPT["mos"])
+            gather("SV", ("zt", 4 * a, 4 * b), ("tt", 0, 4 * C), (mine, a // 4, b // 4))
 
         cut = ZPART[0][1]
         z0, z1, z2 = OPT["zv"]
         zq = (("V", 0, z0), ("S", z0, cut), ("V", cut, cut + z1), ("V", cut + z1, cut + z2), ("S", cut + z2, C))
         if OPT["zq"]:
-            zq = [("SV", a, b) for a, b in zip([0] + OPT["zq"], OPT["zq"] + [C])]
+            zq = OPT["zq"]
         for q, a, b in zq:
             if a < b:
                 gather(q, ("zp", 4 * a, 4 * b), ("tq", 0, 4 * C), (arr, a // 4, b // 4))
@@ -466,43 +516,35 @@ def rank_program(g, core, T, topo):
             sign(("cs", a, b), bank(2 + 5 * hf, b - a))
 
         def new_cols(a, b):
-            call = lambda e: e.tensor_tensor(T[xt][:, 4 * a:4 * b], T.h[:, 0:4 * C].indirect(T[arr][:, a // 4:b // 4]), T.zt[:, 4 * a:4 * b], A.add)
-            op({"V": (call, fetch("V", 4 * (b - a)))}, [("h", 0, 4 * C), (arr, a // 4, b // 4), ("zt", 4 * a, 4 * b)], [(xt, 4 * a, 4 * b)], listed=True)
-        exchange = [lambda: scan(("soc", 0, C), ("pure", 0, C), ("cs", 0, C)),
-                    lambda: tt(("m2", 0, 18), readout("soc", 0, 18), ("dd", 0, 18), A.mult),
-                    lambda: tt(("ab", 0, 18), ("mean", 0, 18), ("m2", 0, 18), A.add),
-                    lambda: tt(("ab", 18, 36), ("mean", 0, 18), ("m2", 0, 18), A.subtract),
-                    lambda: cp(("lab", 0, 36), ("ab", 0, 36))]
+            call = lambda e: e.tensor_tensor(T[xt][:, 4 * a:4 * b], T.h[:, 0:4 * C].indirect(T[theirs][:, a // 4:b // 4]), T.zt[:, 4 * a:4 * b], A.add)
+            op({"V": (call, fetch("V", 4 * (b - a)))}, [("h", 0, 4 * C), (theirs, a // 4, b // 4), ("zt", 4 * a, 4 * b)], [(xt, 4 * a, 4 * b)], listed=True)
         cuts = OPT["newlast" if last else "new"]
-        for n, (a, b) in enumerate(zip([0] + cuts, cuts + [C])):
+        for a, b in zip([0] + cuts, cuts + [C]):
             new_cols(a, b)
             in_turn("N")
-            for i in range(OPT["between"][n] if last else 0):
-                exchange.pop(0)()
-                in_turn("N")
         for a, b in PART:
             quant("x%d" % (r + 1), a, b, xt)
-        for step in exchange:
-            step()
+
+        scan(("soc", 0, C), ("pure", 0, C), ("cs", 0, C))
+        tt(("m2", 0, 18), readout("soc", 0, 18), ("dd", 0, 18), A.mult)
+        for c, o in enumerate((A.add, A.subtract)):
+            tt(("abn", 18 * c + 17, 18 * c - 1, -1) if last else ("ab", 18 * c, 18 * c + 18), ("mean", 0, 18), ("m2", 0, 18), o)
         if not last:
+            cp(("lab", 0, 36), ("ab", 0, 36))
             ts(("dd", 0, 18), ("m2", 0, 18), SC, -1.0, A.mult, A.mult)
 
     for r in range(3):
         one_round(r)
 
     moved[0] = 0
-    for c in range(2):
-        for a, b in ((0, 8), (8, 18)):
-            gather("SV", ("rowa", C * c + 16 * a, C * c + 16 * b), ("nat", 0, C), ("lab", 18 * c + a, 18 * c + b))
-        for a, b in ((0, 8), (8, 18)):
-            gather("SV", ("opr", C * c + C + 16 * a, C * c + C + 16 * b), ("rowa", C * c, C * c + C), ("order", a, b))
+    dma("Y", T.op[:, 0:C], T.opr[0:128:16, :], [("opr", 0, C)], [], -300)
     for hf, (a, b) in enumerate(PART):
-        pick("o", a, b, "x3", C, ("order", a // 16, b // 16))
-        mm(3 + hf, "v", 0, "o", a, b)
+        mm(3 + hf, "v", 0, "x3", a, b)
         move("SV", ("yo", a, b), bank(3 + hf, b - a))
-    dma("S", T.op[:, :], T.opr[0:128:16, :], [("opr", 0, 3 * C)], [], 0)
-    dma("Y", T.y[:, :], T.yo[:, :], [("yo", 0, C)], [], 4 * C)
-    dma("Y", T.oc[:, :], T.qo[:, :].bitcast(dt.uint8), [("qo", 0, C)], [], 0)
+        dma("Y", T.oc[:, 4 * a:4 * b], T.qx3[:, a:b].bitcast(dt.uint8), [("qx3", a, b)], [], -300)
+        dma("YS"[hf], T.y[:, a:b], T.yo[:, a:b], [("yo", a, b)], [], 0)
+    for c in range(2):
+        dma("YS"[c], T.op[:, C + C * c:2 * C + C * c], T.abn[:, 18 * c:18 * c + 18], [("abn", 18 * c, 18 * c + 18)], [], -300)
     for k in range(4):
-        dma("Y", T.osc[4 * k:4 * k + 4, :], T.po[32 * k:32 * k + 4, :], [("po", 0, C)], [], -300)
+        dma("YS"[k % 2], T.osc[4 * k:4 * k + 4, :], T.px3[32 * k:32 * k + 4, :], [("qx3", 0, C)], [], -300)
     finish()

@@ -4,17 +4,41 @@ from concourse.mybir import dt, AluOpType, ActivationFunctionType
 STEP = [4, 1, 2]
 STAGES = 7
 C = 288
-PART = [(0, 160), (160, 288)]
 COLS = 18 + STAGES
-ZPART = [(0, 160), (160, 288)]
-CHUNK = [(0, 9), (9, 13), (13, 17), (17, 21), (21, 25)]
-AT = [0, 10, 14, 18, 22]
 MID = 576
 BIG = 2.0 ** 40
 CARRY = 6000.0
 BASE = 2047 * CARRY + 1024
 TINY = -2.0 ** -100
-OPT = {"ga": [10], "zv": [88, 16, 56], "new": [160], "wake": 200.0, "grain": 30.0, "list": 1400.0, "tile": 5000.0, "gat": 1.56, "pe": 1.3, "vg": [], "cut": 1, "mos": 48, "load": 1600.0, "passes": 6, "turn": "SVNEFP", "assist": [], "lpart": [(0, 160), (160, 288)], "begin": ["g0", "g1", "s0", ("V", 0, 8), ("S", 18, 36), "a0", "s1", ("V", 8, 18), "o0", "a1", "o1"], "newlast": [160], "between": [1, 1, 2, 1, 0], "gq": "VS", "g0": "S", "hq": ["V", "V", "S", "S"], "zq": None}
+OPT = {"wake": 200.0, "list": 1400.0, "tile": 5000.0, "gat": 1.56, "pe": 1.3, "load": 1200.0, "rate": 0.3, "soon": 16,
+       "start": "Sm0:10 Vg0:0 Vm10:18 Sn0:10 Sn10:18 Sn18:20 Vu0:0 Vm18:25 Vp0:0 Sp0:0 Vx0:160 Vr0:10 Sr10:25 Vx160:288 Vs0:10 Vt0:0 Vt1:1 Vs10:25 Vl0:10 Vc0:25 Vl10:25", "passes": 120, "turn": "SVNMPDK",
+       "add": 1.0, "seed": 2, "shake": 400.0, "wide": 2400.0, "deal": 3000.0, "pool": "cb enc down eb lam".split(), "early": (6, 0), "lag": [1] * 6, "moves": 800, "reach": 30,
+       "cases": [(200.0, 1.0, 1.0, 1.0, 1.0), (130.0, 1.3, 1.0, 0.8, 1.0), (240.0, 1.0, 0.7, 0.7, 1.2), (200.0, 1.3, 1.3, 1.3, 1.5), (170.0, 1.1, 0.8, 1.0, 0.8)],
+       "part": 160, "zpart": 160, "cuts": [13, 21],
+       "chunk": [(0, 9), (9, 13), (13, 17), (17, 21), (21, 25)],
+       "head": [("V", 1, 9), ("S", 9, 25)],
+       "begin": ["e1", "e2", "e3", "v0", "v1", "g0", "g1", ("V", 0, 6), ("S", 18, 36), "s0", "s1", ("V", 6, 12), ("S", 12, 18), "o0", "a1", "o1"],
+       "mirror": [("P", 1, 0, 288), ("P", 0, 0, 96), ("SV", 0, 96, 288)],
+       "zq": [("V", 0, 0, 160), ("S", 2, 0, 160), ("V", 1, 0, 160), ("S", 3, 0, 160), ("V", 0, 160, 288), ("q", 0, 0, 160), ("S", 2, 160, 288), ("V", 1, 160, 288), ("S", 3, 160, 288),
+              ("q", 1, 160, 288)],
+       "new": [("S", 0, 72), ("V", 72, 160), ("V", 160, 200), ("S", 200, 288)],
+       "newl": [("S", 0, 72), ("V", 72, 160), ("V", 160, 200), ("S", 200, 288)],
+       "nturn": "h0 h1 g0 g3 c0 c1 n1 n0 n2 n3 x0 e0 x1".split(),
+       "lturn": "h0 h1 g0 g3 c0 c1 n1 n0 n2 n3 e0 x0 e1 x1 e2".split(),
+       "hq": ["SV", "SV", "SV", "SV"], "mos": 96, "mosp": 160, "cut": 144, "cutq": 144, "vg": [], "tq": "SV", "tt": "SV", "planar": [0],
+       "loads": ["sti", "ut", "x0", "x1", "tai", "tbi"], "lq": "SYSYSY", "rp0": [("SV", 0, 12), ("SV", 12, 25)], "sl0": [(0, 25)], "rowa": [(0, 10), (10, 18)], "late": "t",
+       "tail": "St0 Yt1 Yc2 Ss0 Ss1 Ss2 Ss3 Yy2", "yq": "VV"}
+OPT.update({"late": "", "tail": "Yc0 Sc1 Ss0 Ys1 Ss2 Ys3 Yy0 St0 Yt1 Sy1", "yq": "SV",
+            "nturn": "h0 h1 g0 g3 c0 c1 n1 n0 n2 n3 x0 x1 e0".split(), "lturn": "h0 h1 g0 g3 c0 c1 n1 n0 n2 x0 n3 e0 x1 e1 e2".split(),
+            "begin": ["e1", "e2", "v0", "e3", "v1", "g0", "g1", ("V", 0, 6), ("S", 18, 36), "s0", "s1", ("V", 6, 12), ("S", 12, 18), "o0", "a1", "o1"]})
+OPT.update({"nturn": "h0 h1 g0 g3 c0 c1 n1 n0 n2 n3 x0 e0 x1".split(), "zpart": 144, "cuts": [12, 20], "chunk": [(0, 8), (8, 12), (12, 16), (16, 20), (20, 25)],
+            "zq": [("V", 0, 0, 144), ("S", 2, 0, 144), ("V", 1, 0, 144), ("S", 3, 0, 144), ("V", 0, 144, 288), ("q", 0, 0, 144), ("S", 2, 144, 288), ("V", 1, 144, 288),
+                   ("S", 3, 144, 288), ("q", 1, 144, 288)],
+            "begin": ["e1", "e2", "e3", "v0", "v1", "g0", "g1", ("V", 0, 6), ("S", 18, 36), "s0", "s1", ("V", 6, 12), ("S", 12, 18), "o0", "a1", "k0", "o1"]})
+OPT.update({"late": "t", "mirror": [("P", 1, 0, 288), ("P", 0, 0, 96), ("V", 0, 96, 288)],
+            "pool": "cb eb enc down pi tm lam".split(),
+            "start": "Vk31:33 Vk5:7 Vk4:5 Vk7:8 Vk33:34 Vk10:11 Vk27:28 Vk8:10 Vk11:12 Vk28:29 Vk12:13 Vk14:15 Sm0:12 Sm12:25 Vg0:0 Vk29:30 Vk15:16 Vk13:14 "
+                     "Sn0:10 Sn10:18 Sn18:20 Vu0:0 Vk30:31 Vp0:0 Sp0:0 Vx0:160 Vr0:10 Sr10:25 Vx160:288 Vs0:10 Vs10:25 Vt0:0 Vt1:1 Vl0:25"})
 
 SCRATCH = {"ps": ("psum", [128, 4096], "float32")}
 
@@ -24,19 +48,20 @@ def _bufs(where, dtype, **cols):
         SCRATCH[k] = (where, [128, cols[k]], dtype)
 
 
-_bufs("sbuf", "bfloat16", xin=1152, xt1=1152, xt2=1152, xt3=1152, ut=512, vt=512, ones=516, eb=516, tm=16, ma=32, mb=32, m16=32,
+_bufs("sbuf", "bfloat16", xin=1152, xt1=1152, xt2=1152, xt3=1152, ut=512, vt=512, ones=128, eb=516, tm=16, ma=32, mb=32, m16=32,
       pure=400, chain=400, mask4=288, sg=288, cs=288, r0=400, so0=400, soc=288,
       tt=1152, tq=1152, zt=1152, zp=1152, h=1152, hg=1152)
 for _n, _c in [("u", 128), ("ur", 128), ("v", 128), ("w", 512), ("e", 512), ("z", 288), ("h", 288)] + [("x%d" % _r, 288) for _r in range(4)] + [("l%d" % _r, 288) for _r in range(3)]:
     SCRATCH["q" + _n] = ("sbuf", [128, _c], "float8_e4m3fn_x4")
     SCRATCH["p" + _n] = ("sbuf", [128, _c], "uint8")
-_bufs("sbuf", "int32", pi=8, pk=8, offui=8, tai=18, tbi=18, sti=18, qi=36, lo=36, hi=36, d18=72)
-_bufs("sbuf", "float32", pf=8, sc=12, enc=288, lam=288, nat=288, rowa=576, soo=288, val=288, ab=36, dd=18, mean=18, m2=36, yy=26, f1=72, f2=72, cb=8, gl=36, tl=36, nv=36, abn=36,
-      w=1160, r=400, so=496, rn=320, so4=288, sol=400, opr=288, yo=288, ra=288, so5=288, so6=288)
-_bufs("sbuf", "uint16", offu=8, l16=26, l4=18, order=18, ownn=72, arrn=72, sout=24, sin=24, ahead=8, sn=18, sl=28, lab=36, off=28, own0=72, own1=72, own2=72, arr0=72, arr1=72, arr2=72)
+_bufs("sbuf", "int32", pi=8, pk=8, dj=16, li=26, tai=18, tbi=18, sti=18, qi=54, lo=54, hi=54)
+_bufs("sbuf", "float32", pf=8, sc=12, enc=288, lam=288, turn=64, turned=64, rows=576, f1=54, val=288, ab=54, dd=18, mean=18, m2=36, yy=26, cb=18, down=26, tl=54, nv=36, abn=54,
+      w=1160, r=400, rp=400, r1=400, so1=400, so=512, rn=320, so4=288, sol=400, yo=288)
+_bufs("sbuf", "uint16", offu=8, l16=26, order=18, ahead=8, sn=18, lab=36, off=32, sl0=26, sl1=26, sl2=26, sh0=24, sh1=24, sh2=24, places=26,
+      own0=72, own1=72, own2=72, arr0=72, arr1=72, arr2=72, got0=24, got1=24, got2=24)
 
 DMAS = ["d%d" % _i for _i in range(26)]
-SEMAPHORES = ["cV", "cS", "cT", "cP", "left", "as"] + ["ax%d" % _r for _r in range(3)] + ["al%d%d" % (_r, _h) for _r in range(3) for _h in range(3)] + DMAS
+SEMAPHORES = ["cV", "cS", "cT", "cP", "left"] + ["ax%d" % _r for _r in range(3)] + ["al%d%d" % (_r, _h) for _r in range(3) for _h in range(4)] + DMAS
 CYCLE = 0.83
 ORDER = []
 
@@ -56,7 +81,10 @@ def plan(nodes):
 
     def place(turn, back):
         at, taken = {}, {}
-        for i in turn:
+        turn = list(turn)
+        while turn:
+            i = next(i for i in turn if all(p in at for p in (after[i] if back else nodes[i]["pre"])))
+            turn.remove(i)
             best = None
             for q in nodes[i]["on"]:
                 d = held(i, q)
@@ -79,16 +107,91 @@ def plan(nodes):
     ahead = [0.0] * n
     for i in range(n - 1, -1, -1):
         ahead[i] = max([nodes[i]["on"][first[i]][1]] + [ahead[j] + lag(i, first[i], j, h) for j, h in after[i].items()])
-    turn, best = sorted(range(n), key=lambda i: (-ahead[i], i)), None
+
+    def length(order, wake, slow, gat, pe, far):
+        end, free = {}, {}
+        for i, q in order:
+            x = nodes[i]
+            t = max([free.get(q, 0.0)] + [end[p] + (wake if h else 0.0) for p, h in x["pre"].items() if h or q is None])
+            d = x["on"][q][1]
+            end[i] = t + (d * far if x["kind"] != "call" else d * pe if q == "T" else slow * (60 + (d - 60) * gat if x["listed"] else d))
+            if q:
+                free[q] = end[i] if x["busy"] is None else t + x["busy"]
+        return max(end.values())
+    turn, best, seed, scale = sorted(range(n), key=lambda i: (-ahead[i], i)), None, OPT["seed"], None
     for k in range(OPT["passes"]):
         at = place(turn, False)
-        length = max(at[i][0] + nodes[i]["on"][at[i][1]][1] for i in range(n))
-        if best is None or length < best[0]:
-            best = (length, at)
+        order = [(i, at[i][1]) for i in sorted(range(n), key=lambda i: (at[i][0], i))]
+        worth = [length(order, *case) for case in OPT["cases"]]
+        scale = scale or worth
+        worth = sum(a / b for a, b in zip(worth, scale))
+        if best is None or worth < best[0]:
+            best = (worth, order, at)
+        at = best[2] if k % 3 == 2 else at
         late = place(sorted(range(n), key=lambda i: (-at[i][0], -i)), True)
-        turn = sorted(range(n), key=lambda i: (-late[i][0], i))
-    at = best[1]
-    return [(i, at[i][1]) for i in sorted(range(n), key=lambda i: (at[i][0], i))]
+        shake = []
+        for i in range(n):
+            seed = (seed * 1103515245 + 12345) % 2 ** 31
+            shake.append(OPT["shake"] * seed / 2 ** 31 if k % 3 == 2 else 0.0)
+        turn = sorted(range(n), key=lambda i: (-late[i][0] - shake[i], i))
+
+    cases = OPT["cases"]
+    took = [{q: [x["on"][q][1] * far if x["kind"] != "call" else x["on"][q][1] * pe if q == "T" else slow * (60 + (x["on"][q][1] - 60) * gat if x["listed"] else x["on"][q][1])
+                 for wake, slow, gat, pe, far in cases] for q in x["on"]} for x in nodes]
+    hard = [[p for p, h in x["pre"].items() if h] for x in nodes]
+    soft = [[p for p in x["pre"]] if None in x["on"] else [] for x in nodes]
+
+    def run(order):
+        total, blocks = 0.0, []
+        for c in range(len(cases)):
+            w = cases[c][0]
+            end, why, free, last = [0.0] * n, [None] * n, {}, {}
+            for i, q in order:
+                t, y = free.get(q, 0.0), (last.get(q), True)
+                for p in hard[i]:
+                    if end[p] + w > t:
+                        t, y = end[p] + w, (p, False)
+                for p in soft[i]:
+                    if end[p] > t:
+                        t, y = end[p], (p, False)
+                end[i], why[i] = t + took[i][q][c], y
+                if q:
+                    free[q], last[q] = end[i] if nodes[i]["busy"] is None else t + nodes[i]["busy"], i
+            i = max(range(n), key=lambda j: end[j])
+            total += end[i] / scale[c]
+            while i is not None:
+                p, queued = why[i]
+                if queued and p is not None and p not in nodes[i]["pre"]:
+                    blocks.append((p, i))
+                i = p
+        return total, blocks
+    order = best[1]
+    worth, blocks = run(order)
+    for k in range(OPT["moves"]):
+        seed = (seed * 1103515245 + 12345) % 2 ** 31
+        p, i = blocks[(seed >> 8) % len(blocks)]
+        where = {x[0]: j for j, x in enumerate(order)}
+        seed = (seed * 1103515245 + 12345) % 2 ** 31
+        how = (seed >> 8) % 100
+        tried = list(order)
+        if how < 30 and len(nodes[p]["on"]) > 1:
+            tried[where[p]] = (p, [q for q in nodes[p]["on"] if q != order[where[p]][1]][0])
+        elif how < 65:
+            end = min([where[j] for j in after[p]] + [n])
+            if end <= where[i]:
+                continue
+            to = min(end - 1, where[i] + (seed >> 16) % OPT["reach"])
+            tried.insert(to, tried.pop(where[p]))
+        else:
+            start = max([where[j] for j in nodes[p]["pre"]] + [-1]) + 1
+            to = max(start, where[p] - 1 - (seed >> 16) % OPT["reach"])
+            if to >= where[p]:
+                continue
+            tried.insert(to, tried.pop(where[p]))
+        w, b = run(tried)
+        if w <= worth:
+            order, worth, blocks = tried, w, b
+    return order
 
 
 def make_tracker(g, T):
@@ -110,22 +213,23 @@ def make_tracker(g, T):
         for x in wr + [x for x in rd if x[0] == "ps"]:
             for c, p, oq in reads.get(x[0], []):
                 if c & cols(x) and (oq != q or x in wr):
-                    pre[p] = pre.get(p, False) or oq != q
+                    pre[p] = True
         for x in wr:
             k, c = x[0], cols(x)
             writes[k] = [e for e in writes.get(k, []) if not e[0] <= c] + [(c, me)]
             reads[k] = [e for e in reads.get(k, []) if not e[0] <= c]
         for x in rd if kind != "remote" else []:
             reads.setdefault(x[0], []).append((cols(x), me, q if kind == "call" and not listed and len(on) == 1 else "any"))
-        nodes.append({"on": on, "kind": kind, "busy": busy, "pre": pre})
+        nodes.append({"on": on, "kind": kind, "busy": busy, "pre": pre, "listed": listed})
         return me
 
     turn = {}
 
-    def in_turn(name):
-        if name in turn and name in OPT["turn"]:
+    def in_turn(name, aside=False):
+        if name in turn and name[0] in OPT["turn"] and turn[name] < len(nodes) - 1:
             nodes[-1]["pre"].setdefault(turn[name], False)
-        turn[name] = len(nodes) - 1
+        if not aside:
+            turn[name] = len(nodes) - 1
 
     def finish():
         if not ORDER:
@@ -159,9 +263,11 @@ def make_tracker(g, T):
             if n["kind"] == "dma":
                 s, inc = DMAS[ndma], 16
                 ndma += 1
-            count[s] = count.get(s, 0) + inc
+            made = call(queues[q])
+            for x in made if isinstance(made, list) else [made]:
+                x.then_inc(T.sem[s], inc)
+                count[s] = count.get(s, 0) + inc
             token[i] = (s, count[s])
-            call(queues[q]).then_inc(T.sem[s], inc)
             clocks[token[i]] = dict(known[q])
             clocks[token[i]][s] = count[s]
         for s in sorted(count):
@@ -177,6 +283,12 @@ def rank_program(g, core, T, topo):
     A = AluOpType
     F = ActivationFunctionType
     op, in_turn, finish = make_tracker(g, T)
+    PART = [(0, OPT["part"]), (OPT["part"], C)]
+    ZPART = [(0, OPT["zpart"]), (OPT["zpart"], C)]
+    CHUNK = OPT["chunk"]
+    AT = [0]
+    for a, b in CHUNK:
+        AT.append(AT[-1] + (b - a + 1) // 2 * 2)
 
     def ap(x):
         if not isinstance(x, tuple):
@@ -203,7 +315,7 @@ def rank_program(g, core, T, topo):
         op({"V": (lambda e: e.tensor_scalar(ap(out), ap(in0), ap(s1), ap(s2), *ops), cycles(out, in0))}, rgs(in0, s1, s2), [out])
 
     def tt(out, in0, in1, o):
-        op({"V": (lambda e: e.tensor_tensor(ap(out), ap(in0), ap(in1), o), cycles(out, in0, in1, rate=2.0))}, [in0, in1], [out])
+        op({"V": (lambda e: e.tensor_tensor(ap(out), ap(in0), ap(in1), o), max(64, size(out) * OPT["add"]) * CYCLE if out[0][:2] == "xt" else cycles(out, in0, in1, rate=2.0))}, [in0, in1], [out])
 
     def cp(out, in_):
         move("V", out, in_)
@@ -216,7 +328,8 @@ def rank_program(g, core, T, topo):
 
     def move(qs, out, in_, scale=None):
         on = {"V": (lambda e: e.tensor_scalar(ap(out), ap(in_), scale, None, A.mult) if scale else e.tensor_copy(ap(out), ap(in_)), cycles(out, in_)),
-              "S": (lambda e: e.activation(ap(out), ap(in_), F.Copy, scale=scale if scale else 1.0), max(64, size(out)) * CYCLE)}
+              "S": (lambda e: e.activation(ap(out), ap(in_), F.Copy, scale=scale if scale else 1.0), max(64, size(out)) * CYCLE),
+              "P": (lambda e: e.affine_select(ap(out), ap(in_), [[1, size(out)]], A.is_ge, 0.0, 0, 0), 170 + 2 * size(out) * CYCLE)}
         op({q: on[q] for q in qs}, [in_], [out])
 
     def gather(qs, out, win, off, add=None, scale=None, fn=None):
@@ -226,23 +339,29 @@ def rank_program(g, core, T, topo):
               "V": lambda e: e.tensor_scalar(ap(out), src, add if add else scale, None, A.add if add else A.mult) if k else e.tensor_copy(ap(out), src)}
         op({q: (on[q], fetch(q, size(out))) for q in qs}, [win, off], [out], listed=True)
 
+    def gather_add(out, win, off, other):
+        call = lambda e: e.tensor_tensor(ap(out), ap(win).indirect(ap(off)), ap(other), A.add)
+        op({"V": (call, fetch("V", size(out)))}, [win, off, other], [out], listed=True)
+
     def iota(out, pat, base, cm):
         k = {} if SCRATCH[out[0]][2] == "int32" else {"allow_small_or_imprecise_dtypes": True}
         op({"P": (lambda e: e.iota(ap(out), pat, base, cm, **k), 130 + 2 * size(out) * CYCLE)}, [], [out])
         in_turn("P")
 
-    def scan(out, mask, row, first=0.0):
-        op({"V": (lambda e: e.tensor_tensor_scan(ap(out), ap(mask), ap(row), ap(first), A.mult, A.add), cycles(out, mask, row))}, rgs(mask, row, first), [out])
+    def scan(out, mask, row, first=0.0, op0=A.mult, op1=A.add):
+        op({"V": (lambda e: e.tensor_tensor_scan(ap(out), ap(mask), ap(row), ap(first), op0, op1), cycles(out, mask, row))}, rgs(mask, row, first), [out])
 
     def quant(q, a, b, src, at=None):
         x = (src, 4 * a, 4 * b) if at is None else (src, at, at + 4 * (b - a))
         op({"V": (lambda e: e.quantize_mx(T["q" + q][:, a:b], T["p" + q][:, a:b], ap(x)), 12 + 0.22 * size(x))}, [x], [("q" + q, a, b)])
 
-    def pick(dst, a, b, src, n, off):
+    def pick(q, dst, a, b, src, n, off):
         rd = [("q" + src, 0, n), off]
-        op({"V": (lambda e: e.tensor_copy(T["q" + dst][:, a:b].bitcast(dt.uint32), T["q" + src][:, 0:n].bitcast(dt.uint32).indirect(ap(off))), fetch("V", b - a))},
-           rd, [("q" + dst, a, b)], listed=True)
-        op({"S": (lambda e: e.activation(T["p" + dst][:, a:b], T["p" + src][:, 0:n].indirect(ap(off)), F.Copy), fetch("S", b - a))}, rd, [("p" + dst, a, b)], listed=True)
+        if q == "V":
+            op({"V": (lambda e: e.tensor_copy(T["q" + dst][:, a:b].bitcast(dt.uint32), T["q" + src][:, 0:n].bitcast(dt.uint32).indirect(ap(off))), fetch("V", b - a))},
+               rd, [("q" + dst, a, b)], listed=True)
+        else:
+            op({"S": (lambda e: e.activation(T["p" + dst][:, a:b], T["p" + src][:, 0:n].indirect(ap(off)), F.Copy), fetch("S", b - a))}, rd, [("p" + dst, a, b)], listed=True)
 
     def bank(i, n, at=0):
         return ("ps", 512 * i + at, 512 * i + at + n)
@@ -254,122 +373,206 @@ def rank_program(g, core, T, topo):
     def readout(buf, a, b):
         return (buf, 16 * a + 15, 16 * b, 16)
 
+    def pieces(a, b, n):
+        return [(c, min(b, c + n)) for c in range(a, b, n)]
+
     moved, loads = [0], {"S": [], "Y": []}
 
     def dma(q, dst, src, rd, wr, nbytes, behind=()):
         moved[0] += nbytes + 300
-        return op({q: (lambda e: e.dma_start(dst, src), OPT["load"] + 0.4 * moved[0])}, rd, wr, kind="dma", busy=50.0, behind=behind)
+        return op({q: (lambda e: e.dma_start(dst, src), OPT["load"] + OPT["rate"] * moved[0])}, rd, wr, kind="dma", busy=50.0, behind=behind)
 
     def load(q, dst, src, nbytes):
         loads[q].append(dma(q, ap(dst).bitcast(dt.uint8) if dst[0] == "qw" else ap(dst), src, [], [dst], nbytes, loads[q][-1:]))
 
     cut = 4 * PART[0][1]
-    load("S", ("sti", 0, 18), T.st[:, :], 72)
-    load("Y", ("tai", 0, 18), T.ta[:, :], 72)
-    load("S", ("tbi", 0, 18), T.tb[:, :], 72)
-    load("Y", ("xin", 0, cut), T.x[:, 0:cut], 2 * cut)
-    load("S", ("ut", 0, 512), T.u[:, :], 1024)
-    load("Y", ("xin", cut, 4 * C), T.x[:, cut:4 * C], 8 * C - 2 * cut)
+    first_loads = {"sti": (("sti", 0, 18), T.st[:, :], 72), "tai": (("tai", 0, 18), T.ta[:, :], 72), "tbi": (("tbi", 0, 18), T.tb[:, :], 72),
+                   "x0": (("xin", 0, cut), T.x[:, 0:cut], 2 * cut), "ut": (("ut", 0, 512), T.u[:, :], 1024),
+                   "x1": (("xin", cut, 4 * C), T.x[:, cut:4 * C], 8 * C - 2 * cut)}
+    for name, q in zip(OPT["loads"], OPT["lq"]):
+        load(q, *first_loads[name])
 
-    iota(("pi", 0, 5), [[1, 5]], 0, 1)
-    iota(("tm", 0, 16), [[1, 16]], 0, 0)
-    iota(("enc", 0, C), [[2, C]], 2, 0)
-    fill(("ones", 0, 516), 1.0)
-    fill(("w", MID, MID + 2), 0.0)
-    op({"P": (lambda e: e.affine_select(T.eb[:, :], T.ones[:, :], [[1, 516]], A.is_equal, 0.0, -3, -4), 170 + 2 * 516 * CYCLE)}, [("ones", 0, 516)], [("eb", 0, 516)])
-    in_turn("P")
-    iota(("offui", 0, 8), [[16, 8]], 0, 0)
-    iota(("lam", 0, C), [[1, 16], [-16, 18]], 16 * 17 + 1, 0)
-    iota(("cb", 0, 8), [[16, 8]], 16 * (18 - STAGES), 0)
-    iota(("nat", 0, C), [[-1, 18], [18, 16]], 17, 0)
-    for b in range(4):
-        quant("e", 128 * b, 128 * b + 128, "eb", 3 - b)
+    iota(("dj", 0, 16), [[1, 16]], 128, -1)
+    iota(("li", 0, 26), [[0, 26]], 0, 1)
+    for x, c in ((("ones", 0, 128), 1.0), (("eb", 0, 516), 0.0), (("w", MID, MID + 2), 0.0), (("turn", 0, 64), 0.0)):
+        fill(x, c)
+        in_turn("N")
+    for x in OPT["pool"]:
+        if x == "eb":
+            op({"P": (lambda e: e.affine_select(T.eb[:, 3:515:4], T.ones[:, :], [[1, 128]], A.is_equal, 0.0, 0, -1), 170 + 2 * 128 * CYCLE)}, [("ones", 0, 128)], [("eb", 3, 515, 4)])
+            in_turn("P")
+        elif x == "tm":
+            iota(("tm", 0, 16), [[1, 16]], 0, 0)
+        elif x == "pi":
+            iota(("pi", 0, 5), [[1, 5]], 0, 1)
+        elif x == "enc":
+            iota(("enc", 0, C), [[2, C]], 2, 0)
+        elif x == "down":
+            iota(("down", 0, 26), [[-1, 26]], COLS - 1, 0)
+        elif x == "lam":
+            iota(("lam", 0, C), [[1, 16], [-16, 18]], 16 * 17 + 1, 0)
+        else:
+            iota(("cb", 0, 18), [[16, 18]], 0, 0)
 
-    ts(("pk", 0, 2), ("pi", 0, 2), 15, None, A.bitwise_and)
-    ts(("pk", 2, 4), ("pi", 0, 5, 4), 2, 3, A.arith_shift_right, A.bitwise_and)
-    ts(("pk", 4, 5), ("pi", 0, 1), 3, None, A.bitwise_and)
-    cp(("pf", 0, 2), ("pk", 0, 2))
-    cp(("pf", 2, 5), ("pk", 2, 5))
     p16, q16, p4, q4, t4 = [("pf", j, j + 1) for j in range(5)]
-    SC, HALF, START, T4, SC4 = [("sc", j, j + 1) for j in range(5)]
-    for a, (here, behind) in enumerate([(p16, q16), (p4, q4)]):
-        ts(("ma", 16 * a, 16 * a + 16), ("tm", 0, 16), behind, BIG, A.is_equal, A.mult)
-        ts(("mb", 16 * a, 16 * a + 16), ("tm", 0, 16), here, None, A.not_equal)
-        tt(("m16", 16 * a, 16 * a + 16), ("ma", 16 * a, 16 * a + 16), ("mb", 16 * a, 16 * a + 16), A.max)
-    ts(("l16", 0, 26), ("ones", 0, 26), p16, None, A.mult)
-    ts(("l4", 0, 18), ("ones", 0, 18), t4, None, A.mult)
-    for a, b in ((0, 10), (10, 18), (18, COLS)):
-        gather("SV", ("pure", 16 * a, 16 * b), ("m16", 0, 16), ("l16", 0, b - a))
-    for a, b in ((0, 6), (6, 12), (12, 18)):
-        gather("SV", ("mask4", 16 * a, 16 * b), ("m16", 16, 20), ("l4", 0, b - a))
-    ts(("chain", 0, 400), ("pure", 0, 400), 1.0 / (2048 * BIG), None, A.max)
-    ts(SC, p16, 15.0, 1.0 / BIG, A.is_equal, A.max)
-    ts(HALF, SC, 0.5, None, A.mult)
-    ts(("sc", 8, 9), p16, 15.0, BIG, A.not_equal, A.mult)
-    ts(("sc", 6, 7), ("sc", 8, 9), 1.0, None, A.max)
-    ts(START, ("sc", 8, 9), 1.0, BASE + CARRY, A.max, A.mult)
-    ts(("sc", 7, 8), p4, 3.0, 1.0 / BIG, A.is_equal, A.max)
-    ts(SC4, ("sc", 7, 8), 2.0, None, A.mult)
-    ts(T4, t4, -4.0, None, A.add)
-    ts(("sc", 9, 10), t4, -1.0, -34.0, A.mult, A.add)
-    ts(("sc", 10, 11), t4, 17.0, 4.0 * 272, A.mult, A.add)
-    cp(("offu", 0, 8), ("offui", 0, 8))
-    ts(("ahead", 0, 8), ("cb", 0, 8), q16, None, A.add)
-    scan(("soo", 0, C), ("pure", 0, C), ("lam", 0, C))
-    ts(("order", 0, 18), readout("soo", 0, 18), SC, -1.0, A.mult, A.add)
+    SC, HALF, START, T4, SC4, QUART = [("sc", j, j + 1) for j in range(6)]
 
-    quant("u", 0, 128, "ut")
-    pick("ur", 0, 128, "u", 128, ("offu", 0, 8))
-    for a, b in PART:
-        quant("x0", a, b, "xin")
-    cp(("sn", 0, 18), ("sti", 0, 18))
-    for a, b, at in ((0, 8, 0), (8, 18, 8), (0, 2, 18)):
-        gather("SV", ("rn", 16 * at, 16 * (at + b - a)), ("enc", 0, C), ("sn", a, b))
+    def masks(a, here, behind):
+        return [lambda: ts(("ma", 16 * a, 16 * a + 16), ("tm", 0, 16), behind, BIG, A.is_equal, A.mult),
+                lambda: ts(("mb", 16 * a, 16 * a + 16), ("tm", 0, 16), here, None, A.not_equal),
+                lambda: tt(("m16", 16 * a, 16 * a + 16), ("ma", 16 * a, 16 * a + 16), ("mb", 16 * a, 16 * a + 16), A.max)]
+    m16, m4 = masks(0, p16, q16), masks(1, p4, q4)
+    m16[0] = lambda: ts(("ma", 0, 16), ("dj", 0, 16), 1.0, BIG, A.is_equal, A.mult)
+    m16[1] = lambda: ts(("mb", 0, 16), ("dj", 0, 16), 0.0, None, A.not_equal)
+    small = [lambda: ts(("pk", 1, 2), ("pi", 1, 2), 15, None, A.bitwise_and),
+             lambda: ts(("pk", 2, 4), ("pi", 0, 5, 4), 2, 3, A.arith_shift_right, A.bitwise_and),
+             lambda: ts(("pk", 4, 5), ("pi", 0, 1), 3, None, A.bitwise_and),
+             lambda: cp(("pf", 1, 5), ("pk", 1, 5)),
+             lambda: cp(("offu", 0, 8), ("cb", 0, 8)),
+             m16[0], m16[1],
+             lambda: cp(("l16", 0, 26), ("li", 0, 26)),
+             lambda: ts(SC, p16, 15.0, 1.0 / BIG, A.is_equal, A.max),
+             lambda: ts(("sc", 9, 10), p16, 18.0, None, A.mult),
+             m16[2],
+             lambda: ts(("sc", 8, 9), p16, 15.0, BIG, A.not_equal, A.mult),
+             lambda: ts(QUART, SC, 0.25, None, A.mult),
+             lambda: ts(("places", 0, 26), ("down", 0, 26), ("sc", 9, 10), None, A.add),
+             lambda: ts(HALF, SC, 0.5, None, A.mult),
+             lambda: ts(START, ("sc", 8, 9), 1.0, BASE + CARRY, A.max, A.mult),
+             m4[0], m4[1],
+             lambda: ts(SC4, p4, 3.0, 1.0 / BIG, A.is_equal, A.max),
+             lambda: ts(T4, t4, -4.0, None, A.add),
+             lambda: ts(("ahead", 0, STAGES), ("cb", 18 - STAGES, 18), q16, None, A.add),
+             lambda: ts(("tl", 36, 54), ("cb", 17, -1, -1), p16, None, A.add),
+             m4[2]]
+    small += [lambda j=j: ts(("mask4", j, C, 4), ("ones", 0, C // 4), ("m16", 16 + j, 17 + j), None, A.mult) for j in range(4)]
+    small += [lambda b=b: quant("e", 128 * b, 128 * b + 128, "eb", 3 - b) for b in range(4)]
+    small += [lambda: ts(("dj", 0, 16), ("dj", 0, 16), 15, None, A.bitwise_and), lambda: ts(("li", 0, 26), ("li", 0, 26), 15, None, A.bitwise_and),
+              lambda: cp(p16, ("li", 0, 1))]
+    made = []
 
-    def deal(dst, at, src, a):
-        loads["Y"].append(dma("Y", T[dst][:, at:at + 18], T[src][0:128:16, a:a + C], [(src, a, a + C)], [(dst, at, at + 18)], 72, loads["Y"][-1:]))
-    moved[0] = 0
-    deal("gl", 0, "rn", 0)
-    deal("gl", 18, "rn", 18)
+    def as_list(dst, row, a, b, cuts=(), shift=0):
+        cuts = [a] + [c for c in cuts if a < c < b] + [b]
+        for c, d in zip(cuts, cuts[1:]):
+            scan(("sol", 16 * c, 16 * d), ("pure", 16 * c, 16 * d), (row, 16 * c, 16 * d))
+        ts((dst, a + shift, b + shift), readout("sol", a, b), QUART, -1.0, A.mult, A.add)
+
+    for x in OPT["start"].split():
+        q, what, a, b = x[0], x[1], int(x[2:].split(":")[0]), int(x.split(":")[-1])
+        if what == "m":
+            gather(q, ("pure", 16 * a, 16 * b), ("m16", 0, 16), ("l16", 0, b - a))
+        elif what == "k":
+            for j in range(a, b):
+                small[j]()
+                made.append(j)
+                in_turn("N")
+        elif what == "g":
+            cp(("sn", 0, 18), ("sti", 0, 18))
+        elif what == "u":
+            quant("u", 0, 128, "ut")
+        elif what == "p":
+            pick(q, "ur", 0, 128, "u", 128, ("offu", 0, 8))
+        elif what == "x":
+            quant("x0", a, b, "xin")
+        elif what == "n":
+            gather(q, ("rn", 16 * a, 16 * b), ("enc", 0, C), ("sn", a % 18, a % 18 + b - a), scale=2.0)
+        elif what == "r":
+            gather(q, ("rp", 16 * a, 16 * b), ("rn", 0, 320), ("places", a, b))
+        elif what == "s":
+            scan(("sol", 16 * a, 16 * b), ("pure", 16 * a, 16 * b), ("rp", 16 * a, 16 * b))
+        elif what == "l":
+            ts(("sl0", a, b), readout("sol", a, b), QUART, -1.0, A.mult, A.add)
+        else:
+            cp(("lab", 18 * a, 18 * a + 18), (("tai", "tbi")[a], 0, 18))
+        in_turn("N" if q == "V" else "M")
+
     load("Y", ("qw", 0, 512), T.wc[:, :], 2048)
     load("Y", ("pw", 0, 512), T.ws[:, :], 512)
     load("Y", ("vt", 0, 512), T.v[:, :], 1024)
-    quant("v", 0, 128, "vt")
-    moved[0] = 8000
-    for c, src in enumerate(("tai", "tbi")):
-        cp(("lab", 18 * c, 18 * c + 18), (src, 0, 18))
-        for a, b in ((0, 6), (6, 12), (12, 18)):
-            gather("SV", ("rowa", C * c + 16 * a, C * c + 16 * b), ("lam", 0, C), ("lab", 18 * c + a, 18 * c + b))
-        deal("tl", 18 * c, "rowa", C * c)
-        ts(("ab", 18 * c, 18 * c + 18), ("tl", 18 * c + 17, 18 * c - 1, -1), -1.0, None, A.add)
 
     def halves(src):
         tt(("m2", 0, 18), (src, 0, 18), (src, 18, 36), A.add)
         tt(("m2", 18, 36), (src, 18, 36), (src, 0, 18), A.subtract)
         ts(("mean", 0, 18), ("m2", 0, 18), 0.5, None, A.mult)
         ts(("dd", 0, 18), ("m2", 18, 36), HALF, None, A.mult)
-    halves("ab")
 
-    head = [(0, CHUNK[0][1], 0), (CHUNK[0][1], COLS, AT[1])]
-    ts(readout("sol", 0, COLS), ("gl", COLS - 1, -1, -1), ("sc", 6, 7), None, A.mult)
-    for a, b, at in head:
-        ts(("sl", at, at + b - a), ("gl", COLS - 1 - a, COLS - 1 - b, -1), 0.5, -1.0, A.mult, A.add)
+    def later():
+        for j in range(len(small)):
+            if j not in made:
+                small[j]()
+                in_turn("N", True)
+        quant("v", 0, 128, "vt")
+        in_turn("N", True)
+        for c, src in enumerate(("tai", "tbi")):
+            cp(("turn", 32 * c, 32 * c + 18), (src, 0, 18))
+            in_turn("N", True)
+        op({"V": (lambda e: e.transpose(T.turned[:, :], T.turn[:, :]), 64 * CYCLE)}, [("turn", 0, 64)], [("turned", 0, 64)])
+        rows = [(T.rows[16 * k:16 * k + 1, C * c:C * c + C], T.turned[32 * (k // 2):32 * (k // 2) + 18, 32 * c + 16 * (k % 2):32 * c + 16 * (k % 2) + 16])
+                for k in range(8) for c in range(2)]
+        op({"Y": (lambda e: [e.dma_start(dst, src) for dst, src in rows], OPT["deal"])}, [("turned", 0, 64)], [("rows", 0, 2 * C)], kind="dma", busy=800.0, behind=loads["Y"][-1:])
+        deals = [(T.tl[:, 18 * c:18 * c + 18], T.rows[0:128:16, C * c:C * c + C]) for c in range(2)]
+        op({"Y": (lambda e: [e.dma_start(dst, src) for dst, src in deals], OPT["deal"])}, [("rows", 0, 2 * C)], [("tl", 0, 36)], kind="dma", busy=100.0)
+        ts(("qi", 0, 54), ("tl", 0, 54), -8.5, 1.0 / 18, A.add, A.mult)
+        ts(("f1", 0, 54), ("qi", 0, 54), 289.0, 272.0, A.mult, A.add)
+        ts(("tl", 0, 54), ("tl", 0, 54), -16.0, None, A.mult)
+        for c in range(3):
+            tt(("ab", 18 * c, 18 * c + 18), ("tl", 18 * c + 17, 18 * c - 1, -1), ("f1", 18 * c + 17, 18 * c - 1, -1), A.add)
+        cp(("order", 0, 18), ("ab", 36, 54))
+        halves("ab")
 
-    def first_list():
-        for a, b, at in head:
-            scan(("sol", 16 * a, 16 * b), ("pure", 16 * a, 16 * b), ("r", 16 * a, 16 * b))
-            ts(("sl", at, at + b - a), readout("sol", a, b), HALF, -1.0, A.mult, A.add)
+    def as_wide(dst, row, at):
+        for a, b in PART:
+            scan(("so4", a, b), ("mask4", a, b), (row, at + a, at + b))
+        ts((dst, 0, C // 4), ("so4", 3, C, 4), SC4, T4, A.mult, A.add)
 
-    def span(k, t):
-        a, b = CHUNK[k]
-        return max(a, t), b
+    def natural(at, n, out):
+        ts(("lo", at, at + n), ("qi", at, at + n), 15, None, A.bitwise_and)
+        ts(("hi", at, at + n), ("qi", at, at + n), 4, None, A.arith_shift_right)
+        ts(("tl", at, at + n), ("lo", at, at + n), 18.0, 17.0, A.mult, A.add)
+        tt(out, ("tl", at, at + n), ("hi", at, at + n), A.subtract)
+
+    def runs(t):
+        s, until = OPT["early"]
+        rest = [(a, b, AT[k]) for k, (a, b) in enumerate(CHUNK)][1:]
+        if t <= until:
+            return [(t, s, 0), (s, CHUNK[0][1], 6)] + rest
+        if t >= CHUNK[0][1]:
+            return [(t, rest[0][1], rest[0][2])] + rest[1:]
+        return [(t, CHUNK[0][1], 6 - s + t if t == until + 1 and until else 0)] + rest
+
+    def places_of(t, a, b):
+        segs = []
+        for c, d, at in runs(t):
+            lo, hi = max(a, c), min(b, d)
+            if lo < hi:
+                if segs and segs[-1][2] + segs[-1][1] - segs[-1][0] == at + lo - c:
+                    segs[-1][1] = hi
+                else:
+                    segs.append([lo, hi, at + lo - c])
+        return segs
+
+    def exchange(step, last):
+        if step == 0:
+            scan(("soc", 0, C), ("pure", 0, C), ("cs", 0, C))
+        elif step == 1:
+            tt(("m2", 0, 18), readout("soc", 0, 18), ("dd", 0, 18), A.mult)
+        elif step == 2:
+            for c, o in enumerate((A.add, A.subtract)):
+                tt(("abn", 18 * c + 17, 18 * c - 1, -1) if last else ("ab", 18 * c, 18 * c + 18), ("mean", 0, 18), ("m2", 0, 18), o)
+                in_turn("N")
+        else:
+            cp(("lab", 0, 36), ("ab", 0, 36))
+        in_turn("N")
+        if step == 3:
+            ts(("dd", 0, 18), ("m2", 0, 18), SC, -1.0, A.mult, A.mult)
 
     def one_round(r):
         partner = T.cores[rank ^ STEP[r]]
         rid, pid = topo.addr(partner, core)
         engines = topo.engines(core, partner)
         mask = sum(1 << e for e in engines)
-        qx, lx, own, arr, xt, last = "x%d" % r, "l%d" % r, "own%d" % r, "arr%d" % r, "xt%d" % (r + 1), r == 2
+        qx, lx, own, arr, got, xt, last = "x%d" % r, "l%d" % r, "own%d" % r, "arr%d" % r, "got%d" % r, "xt%d" % (r + 1), r == 2
+        sl, short, row = "sl%d" % r, "sh%d" % r, ["rp", "rp", "r"][r]
 
         def send(sem, pairs, rd, wr, time):
             def call(dst, src):
@@ -380,171 +583,202 @@ def rank_program(g, core, T, topo):
         for hf, (a, b) in enumerate(PART):
             mm(hf, "ur", 0, qx, a, b)
             sign(("sg", a, b), bank(hf, b - a))
-            tt(("val", a, b), ("sg", a, b), ("enc", a, b), A.mult)
+            in_turn("M")
 
         send("ax%d" % r, [(T["q" + lx][:, :].bitcast(dt.uint8), T["q" + qx][:, :].bitcast(dt.uint8)), (T["p" + lx][:, :], T["p" + qx][:, :])],
              [("q" + qx, 0, C), ("p" + qx, 0, C)], [("q" + lx, 0, C)], OPT["tile"])
-        for hf, (a, b) in enumerate(PART):
+
+        def lane(which, q, k, a, b):
+            if which == "t":
+                move(q, ("tt", C * k + a, C * k + b) if r in OPT["planar"] else ("tt", 4 * a + k, 4 * b, 4), bank(2 + k, b - a, a))
+            else:
+                move(q, ("tq", C * k + a, C * k + b), bank((6 + k) % 8, b - a, a))
+
+        def lanes(which, line=None):
             for k in range(4):
-                mm(3 - hf + k, "e", 128 * k, qx, a, b)
-                n = (b - a) // OPT["cut"]
-                for c in range(a, b, n):
-                    move("SV", ("tt", 4 * c + k, 4 * (c + n), 4), bank(3 - hf + k, n, c - a))
-        for k, i in enumerate((7, 0, 1, 6)):
-            mm(i, "e", 128 * k, lx, 0, C)
-            n = C // (2 * OPT["cut"])
-            for a in range(0, C, n):
-                move("SV", ("tq", 4 * a + k, 4 * (a + n), 4), bank(i, n, a))
+                if which == "q":
+                    mm((6 + k) % 8, "e", 128 * k, lx, 0, C)
+            for k, a, b in todo if which == "t" else [(k, a, b) for k in range(4) for a, b in pieces(0, C, OPT["cutq"])]:
+                lane(which, "SV", k, a, b)
+                if line:
+                    in_turn(line, True)
 
         def table(q, a, b):
             c = a // 18
             gather(q, ("w", MID + 2 + 32 * (a - 18 * c) + c, MID + 2 + 32 * (b - 18 * c) + c, 2), ("val", 0, C), ("lab", a, b))
 
+        head = OPT["head"]
+
         def first(step, k):
-            a, b, at = head[k]
-            if step in "gs":
-                b = min(b, COLS - 1)
+            q, a, b = head[k]
             if step == "g":
-                gather("S", ("r0", 16 * a, 16 * b), ("sg", 0, C), ("sl", at, at + b - a), scale=0.5)
+                if q == "V":
+                    gather_add(("r1", 16 * a, 16 * b), ("sg", 0, C), (sl, a - 1, b - 1), (row, 16 * a, 16 * b))
+                else:
+                    gather("S", ("r0", 16 * a, 16 * b), ("sg", 0, C), (sl, a - 1, b - 1))
             elif step == "s":
-                scan(("so0", 16 * a, 16 * b), ("pure", 16 * a, 16 * b), ("r0", 16 * a, 16 * b))
+                if q == "V":
+                    scan(("so1", 16 * a, 16 * b), ("pure", 16 * a, 16 * b), ("r1", 16 * a, 16 * b))
+                else:
+                    scan(("so0", 16 * a, 16 * b), ("pure", 16 * a, 16 * b), ("r0", 16 * a, 16 * b))
             elif step == "a":
-                tt(("yy", max(a, 1), b), readout("so0", max(a, 1) - 1, b - 1), readout("sol", max(a, 1), b), A.add)
+                tt(("yy", a, b), readout("so0", a, b), readout("sol", a, b), A.add)
             else:
-                ts(("off", at, at + b - max(a, 1)), ("yy", max(a, 1), b), SC, 0.5, A.mult, A.add)
+                for lo, hi, at in places_of(1, a, b):
+                    ts(("off", at, at + hi - lo), readout("so1", lo, hi) if q == "V" else ("yy", lo, hi), HALF, 0.5, A.mult, A.add)
         for x in OPT["begin"]:
-            if len(x) == 2:
+            if x[0] == "e":
+                if r:
+                    exchange(int(x[1]), False)
+            elif x[0] == "k":
+                if r == 0:
+                    ts(("chain", 0, 400), ("pure", 0, 400), 1.0 / (2048 * BIG), None, A.max)
+                    in_turn("N")
+            elif x[0] == "v":
+                a, b = PART[int(x[1])]
+                scan(("val", a, b), ("enc", a, b), ("sg", a, b), 0.0, A.max, A.mult)
+                in_turn("N")
+            elif len(x) == 2:
                 first(x[0], int(x[1]))
-                in_turn("F" if x[0] == "g" else "E")
+                in_turn("M" if x[0] == "g" and head[int(x[1])][0] == "S" else "N")
             else:
                 table(*x)
-                in_turn("F" if x[0] == "S" else "E")
-        for c in range(2):
-            for a in (0, C // 2):
-                b = a + C // 2
-                move("SV", ("w", MID - 2 * a - 2 + c, MID - 2 * b - 2 + c, -2), ("w", MID + 2 * a + 2 + c, MID + 2 * b + 2 + c, 2))
+                in_turn("M" if x[0] == "S" else "N")
+        for q, c, a, b in OPT["mirror"]:
+            move(q, ("w", MID - 2 * a - 2 + c, MID - 2 * b - 2 + c, -2), ("w", MID + 2 * a + 2 + c, MID + 2 * b + 2 + c, 2))
+            if q == "V":
+                in_turn("N")
+        if r == 0:
+            later()
+        todo = []
+        for k in range(4):
+            mm(2 + k, "e", 128 * k, qx, 0, C)
+            todo += [(k, a, b) for a, b in pieces(0, C, OPT["cut"])]
+        for which in "tq":
+            if which not in OPT["late"]:
+                lanes(which)
 
-        def offsets(k, t):
-            a, b = span(k, t + 1)
-            ts(("off", AT[k], AT[k] + b - a), readout("so", a + k, b + k), SC, MID - BASE - CARRY, A.mult, A.add)
-            in_turn("V")
-        steps = [(k, t) for t in range(1, STAGES + 1) for k in range(len(CHUNK))]
-        for n, (k, t) in enumerate(steps):
-            a, b = span(k, t)
-            win = ("w", MID if t == 1 else 0, MID + 2 * C + 2)
-            if t == STAGES:
-                if k == 0:
-                    offsets(*steps[n - 1])
-                gather("S", ("r", 16 * a, 16 * b), win, ("off", AT[k], AT[k] + b - a), fn=F.Abs)
+        def offsets(t, a, b, j):
+            for c, d, at in places_of(t + 1, a, b):
+                ts(("off", at, at + d - c), readout("so", c + j, d + j), SC, MID - BASE - CARRY, A.mult, A.add)
+                in_turn("V")
+        waiting = []
+        for t in range(1, STAGES + 1):
+            for k, (a, b, at) in enumerate(runs(t)):
+                win = ("w", MID if t == 1 else 0, MID + 2 * C + 2)
+                if t == STAGES:
+                    while waiting:
+                        offsets(*waiting.pop(0))
+                    gather("S", ("r", 16 * a, 16 * b), win, ("off", at, at + b - a), fn=F.Abs, scale=2.0)
+                    in_turn("S")
+                    continue
+                gather("S", ("r", 16 * a, 16 * b), win, ("off", at, at + b - a), add=BASE)
                 in_turn("S")
-                continue
-            q = "V" if (k, t) in OPT["vg"] else "S"
-            gather(q, ("r", 16 * a, 16 * b), win, ("off", AT[k], AT[k] + b - a), add=BASE)
-            if q == "S":
-                in_turn("S")
-            a -= min(k, 1)
-            scan(("so", 16 * (a + k), 16 * (b + k)), ("chain", 16 * a, 16 * b), ("r", 16 * a, 16 * b), START)
-            in_turn("V")
-            if n:
-                offsets(*steps[n - 1])
+                j = k + len(CHUNK) + 1 - len(runs(t))
+                c = a - min(k, 1)
+                scan(("so", 16 * (c + j), 16 * (b + j)), ("chain", 16 * c, 16 * b), ("r", 16 * c, 16 * b), START)
+                in_turn("V")
+                while len(waiting) >= OPT["lag"][t - 1]:
+                    offsets(*waiting.pop(0))
+                waiting.append((t, a, b, j))
+
+        for which in OPT["late"]:
+            lanes(which, "S")
 
         done = ("r", 16 * STAGES, 400)
-        cuts = sorted(set([0, 16 * (CHUNK[-1][0] - STAGES)] + [b for a, b in OPT["lpart"]]))
-        for a, b in zip(cuts, cuts[1:]):
-            scan(("so4", a, b), ("mask4", a, b), ("r", 16 * STAGES + a, 16 * STAGES + b))
-        for hf, (a, b) in enumerate(OPT["lpart"]):
-            ts((own, a // 4, b // 4), ("so4", a + 3, b, 4), SC4, T4, A.mult, A.add)
-            send("al%d%d" % (r, hf), [(T[arr][:, a // 4:b // 4], T[own][:, a // 4:b // 4])], [(own, a // 4, b // 4)], [(arr, a // 4, b // 4)], OPT["list"])
+        for hf, (a, b) in enumerate(OPT.get("lpart", ZPART)):
+            a, b = a // 16, b // 16
+            as_list(short, "r", STAGES + a, STAGES + b, OPT["cuts"], -STAGES)
+            send("al%d%d" % (r, hf), [(T[got][:, a + a % 2:b + a % 2], T[short][:, a:b])], [(short, a, b)], [(got, a + a % 2, b + a % 2)], OPT["list"])
 
-        mine, theirs = own, arr
         if last:
-            mine, theirs = "ownn", "arrn"
+            ts(("qi", 36, 54), readout("sol", STAGES, COLS), QUART, -1.0, A.mult, A.add)
+            natural(36, 18, ("abn", 53, 35, -1))
             for a, b in ((0, 8), (8, 18)):
                 gather("SV", ("rn", 16 * a, 16 * b), done, ("order", a, b))
-            scan(("soo", 0, C), ("pure", 0, C), ("rn", 0, C))
-            ts(("sout", 0, 18), readout("soo", 0, 18), HALF, -1.0, A.mult, A.add)
-            send("as", [(T.sin[:, 0:18], T.sout[:, 0:18])], [("sout", 0, 18)], [("sin", 0, 18)], OPT["list"])
-            for a, b in ((0, 8), (8, 18)):
-                gather("SV", ("ra", 16 * a, 16 * b), ("enc", 0, C), ("sin", a, b))
-            for dst, so, row in ((mine, "so5", "rn"), (theirs, "so6", "ra")):
-                for a, b in PART:
-                    scan((so, a, b), ("mask4", a, b), (row, a, b))
-                    ts((dst, a // 4, b // 4), (so, a + 3, b, 4), SC4, T4, A.mult, A.add)
-            gather("SV", ("opr", 0, C), ("nat", 0, C), ("sout", 0, 18))
+            as_wide(own, "rn", 0)
             cp(("qi", 0, 36), ("lab", 0, 36))
-            ts(("lo", 0, 36), ("qi", 0, 36), 15, None, A.bitwise_and)
-            ts(("hi", 0, 36), ("qi", 0, 36), 4, None, A.arith_shift_right)
-            ts(("tl", 0, 36), ("lo", 0, 36), 18.0, 17.0, A.mult, A.add)
-            tt(("nv", 0, 36), ("tl", 0, 36), ("hi", 0, 36), A.subtract)
+            natural(0, 36, ("nv", 0, 36))
             halves("nv")
         else:
-            gather("SV", ("r", 0, 16 * STAGES), done, ("ahead", 0, STAGES))
-            first_list()
-        if r == 0:
-            for a, b, at in head:
-                gather("SV", ("r", 16 * a, 16 * b), ("lam", 0, C), ("sl", at, at + b - a), scale=2.0)
-            first_list()
-            theirs = "arrn"
-            for a, b in OPT["lpart"]:
-                a, b = a // 4, b // 4
-                ts(("d18", a, b), (arr, a, b), ("sc", 9, 10), 1.0 / 72, A.add, A.mult)
-                ts(("f1", a, b), (arr, a, b), -16.0, ("sc", 10, 11), A.mult, A.add)
-                ts(("f2", a, b), ("d18", a, b), 4.0 * 289, None, A.mult)
-                tt(("f1", a, b), ("f1", a, b), ("f2", a, b), A.add)
-                cp((theirs, a, b), ("f1", a, b))
-        for a in range(0, C, OPT["mos"]):
-            b = min(C, a + OPT["mos"])
-            gather("SV", ("zt", 4 * a, 4 * b), ("tt", 0, 4 * C), (mine, a // 4, b // 4))
+            src = "r"
+            if r == 0:
+                src = "rp"
+                for a, b in ((0, 10), (10, 18)):
+                    gather("SV", ("rp", 16 * (STAGES + a), 16 * (STAGES + b)), ("lam", 0, C), (short, a, b), scale=4.0)
+            as_wide(own, src, 16 * STAGES)
+            gather("SV", (src, 0, 16 * STAGES), (src, 16 * STAGES, 400), ("ahead", 0, STAGES))
+            if r == 0:
+                as_list("sl1", src, 0, COLS, [STAGES])
+            else:
+                scan(("sol", 0, 16 * STAGES), ("pure", 0, 16 * STAGES), (src, 0, 16 * STAGES))
+                ts(("sl2", 0, COLS), readout("sol", 0, COLS), QUART, -1.0, A.mult, A.add)
+        send("al%d3" % r, [(T[arr][:, :], T[own][:, :])], [(own, 0, 72)], [(arr, 0, 72)], OPT["wide"])
+        if r in OPT["planar"]:
+            for k in range(4):
+                for a, b in pieces(0, C, OPT["mosp"]):
+                    gather("SV", ("zt", 4 * a + k, 4 * b, 4), ("tt", C * k, C * k + C), (short, a // 16, b // 16))
+        else:
+            for a, b in pieces(0, C, OPT["mos"]):
+                gather("SV", ("zt", 4 * a, 4 * b), ("tt", 0, 4 * C), (own, a // 4, b // 4))
 
-        cut = ZPART[0][1]
-        z0, z1, z2 = OPT["zv"]
-        zq = (("V", 0, z0), ("S", z0, cut), ("V", cut, cut + z1), ("V", cut + z1, cut + z2), ("S", cut + z2, C))
-        if OPT["zq"]:
-            zq = OPT["zq"]
-        for q, a, b in zq:
-            if a < b:
-                gather(q, ("zp", 4 * a, 4 * b), ("tq", 0, 4 * C), (arr, a // 4, b // 4))
+        for q, k, a, b in OPT["zq"]:
+            if q == "q":
+                quant("z", a, b, "zp")
+            else:
+                gather(q, ("zp", 4 * a + k, 4 * b, 4), ("tq", C * k, C * k + C), (got, a // 16 + a // 16 % 2, b // 16 + a // 16 % 2))
+            in_turn("M" if q == "S" else "N")
         for hf, (a, b) in enumerate(ZPART):
-            quant("z", a, b, "zp")
             for k in (0, 2, 1, 3):
                 mm(4 * hf + k, "w", 128 * k, "z", a, b)
                 move(OPT["hq"][k], ("h", 4 * a + k, 4 * b, 4), bank(4 * hf + k, b - a), 0.03125)
-        for hf, (a, b) in enumerate(ZPART):
-            quant("h", a, b, "h")
-            in_turn("N")
-            mm(2 + 5 * hf, "ur", 0, "h", a, b)
-            sign(("cs", a, b), bank(2 + 5 * hf, b - a))
 
-        def new_cols(a, b):
-            call = lambda e: e.tensor_tensor(T[xt][:, 4 * a:4 * b], T.h[:, 0:4 * C].indirect(T[theirs][:, a // 4:b // 4]), T.zt[:, 4 * a:4 * b], A.add)
-            op({"V": (call, fetch("V", 4 * (b - a)))}, [("h", 0, 4 * C), (theirs, a // 4, b // 4), ("zt", 4 * a, 4 * b)], [(xt, 4 * a, 4 * b)], listed=True)
-        cuts = OPT["newlast" if last else "new"]
-        for a, b in zip([0] + cuts, cuts + [C]):
-            new_cols(a, b)
-            in_turn("N")
-        for a, b in PART:
-            quant("x%d" % (r + 1), a, b, xt)
-
-        scan(("soc", 0, C), ("pure", 0, C), ("cs", 0, C))
-        tt(("m2", 0, 18), readout("soc", 0, 18), ("dd", 0, 18), A.mult)
-        for c, o in enumerate((A.add, A.subtract)):
-            tt(("abn", 18 * c + 17, 18 * c - 1, -1) if last else ("ab", 18 * c, 18 * c + 18), ("mean", 0, 18), ("m2", 0, 18), o)
-        if not last:
-            cp(("lab", 0, 36), ("ab", 0, 36))
-            ts(("dd", 0, 18), ("m2", 0, 18), SC, -1.0, A.mult, A.mult)
+        for x in OPT["lturn" if last else "nturn"]:
+            j = int(x[1])
+            if x[0] == "h":
+                a, b = ZPART[j]
+                quant("h", a, b, "h")
+                in_turn("N")
+                mm(2 + 5 * j, "ur", 0, "h", a, b)
+            elif x[0] == "c":
+                a, b = ZPART[j]
+                sign(("cs", a, b), bank(2 + 5 * j, b - a))
+                in_turn("M")
+            elif x[0] == "g":
+                q, a, b = OPT["newl" if last else "new"][j]
+                gather("S", ("hg", 4 * a, 4 * b), ("h", 0, 4 * C), (arr, a // 4, b // 4))
+                in_turn("M")
+            elif x[0] == "e":
+                exchange(j, last)
+            elif x[0] == "x":
+                quant("x%d" % (r + 1), PART[j][0], PART[j][1], xt)
+                in_turn("N")
+            else:
+                q, a, b = OPT["newl" if last else "new"][j]
+                if q == "V":
+                    gather_add((xt, 4 * a, 4 * b), ("h", 0, 4 * C), (arr, a // 4, b // 4), ("zt", 4 * a, 4 * b))
+                else:
+                    tt((xt, 4 * a, 4 * b), ("hg", 4 * a, 4 * b), ("zt", 4 * a, 4 * b), A.add)
+                in_turn("N")
 
     for r in range(3):
         one_round(r)
 
     moved[0] = 0
-    dma("Y", T.op[:, 0:C], T.opr[0:128:16, :], [("opr", 0, C)], [], -300)
+    dma("Y", T.op[:, 0:C], T.abn[:, 36:54], [("abn", 36, 54)], [], -300)
     for hf, (a, b) in enumerate(PART):
         mm(3 + hf, "v", 0, "x3", a, b)
-        move("SV", ("yo", a, b), bank(3 + hf, b - a))
-        dma("Y", T.oc[:, 4 * a:4 * b], T.qx3[:, a:b].bitcast(dt.uint8), [("qx3", a, b)], [], -300)
-        dma("YS"[hf], T.y[:, a:b], T.yo[:, a:b], [("yo", a, b)], [], 0)
-    for c in range(2):
-        dma("YS"[c], T.op[:, C + C * c:2 * C + C * c], T.abn[:, 18 * c:18 * c + 18], [("abn", 18 * c, 18 * c + 18)], [], -300)
-    for k in range(4):
-        dma("YS"[k % 2], T.osc[4 * k:4 * k + 4, :], T.px3[32 * k:32 * k + 4, :], [("qx3", 0, C)], [], -300)
+        move(OPT["yq"][hf], ("yo", a, b), bank(3 + hf, b - a))
+    for q, what, k in OPT["tail"].split():
+        k = int(k)
+        a, b = (PART + [(0, C)] * 2)[k]
+        if what == "c":
+            dma(q, T.oc[:, 4 * a:4 * b], T.qx3[:, a:b].bitcast(dt.uint8), [("qx3", a, b)], [], -300)
+        elif what == "y":
+            dma(q, T.y[:, a:b], T.yo[:, a:b], [("yo", a, b)], [], 0)
+        elif what == "t":
+            dma(q, T.op[:, C + C * k:2 * C + C * k], T.abn[:, 18 * k:18 * k + 18], [("abn", 18 * k, 18 * k + 18)], [], -300)
+        else:
+            dma(q, T.osc[4 * k:4 * k + 4, :], T.px3[32 * k:32 * k + 4, :], [("qx3", 0, C), ("px3", 0, C)], [], -300)
+        in_turn("D" + q)
     finish()

from concourse.bass import DstId, RemoteDMATransfer
from concourse.mybir import dt, AluOpType, ActivationFunctionType

STEP = [4, 1, 2]
STAGES = 7
C = 288
COLS = 18 + STAGES
MID = 576
BIG = 2.0 ** 40
CARRY = 6000.0
BASE = 2047 * CARRY + 1024
TINY = -2.0 ** -100
OPT = {"wake": 200.0, "list": 1400.0, "tile": 5000.0, "gat": 1.56, "pe": 1.3, "load": 1200.0, "rate": 0.3, "soon": 16,
       "start": "Sm0:10 Vg0:0 Vm10:18 Sn0:10 Sn10:18 Sn18:20 Vu0:0 Vm18:25 Vp0:0 Sp0:0 Vx0:160 Vr0:10 Sr10:25 Vx160:288 Vs0:10 Vt0:0 Vt1:1 Vs10:25 Vl0:10 Vc0:25 Vl10:25", "passes": 120, "turn": "SVNMPDK",
       "add": 1.0, "seed": 2, "shake": 400.0, "wide": 2400.0, "deal": 3000.0, "pool": "cb enc down eb lam".split(), "early": (6, 0), "lag": [1] * 6, "moves": 800, "reach": 30,
       "cases": [(200.0, 1.0, 1.0, 1.0, 1.0), (130.0, 1.3, 1.0, 0.8, 1.0), (240.0, 1.0, 0.7, 0.7, 1.2), (200.0, 1.3, 1.3, 1.3, 1.5), (170.0, 1.1, 0.8, 1.0, 0.8)],
       "part": 160, "zpart": 160, "cuts": [13, 21],
       "chunk": [(0, 9), (9, 13), (13, 17), (17, 21), (21, 25)],
       "head": [("V", 1, 9), ("S", 9, 25)],
       "begin": ["e1", "e2", "e3", "v0", "v1", "g0", "g1", ("V", 0, 6), ("S", 18, 36), "s0", "s1", ("V", 6, 12), ("S", 12, 18), "o0", "a1", "o1"],
       "mirror": [("P", 1, 0, 288), ("P", 0, 0, 96), ("SV", 0, 96, 288)],
       "zq": [("V", 0, 0, 160), ("S", 2, 0, 160), ("V", 1, 0, 160), ("S", 3, 0, 160), ("V", 0, 160, 288), ("q", 0, 0, 160), ("S", 2, 160, 288), ("V", 1, 160, 288), ("S", 3, 160, 288),
              ("q", 1, 160, 288)],
       "new": [("S", 0, 72), ("V", 72, 160), ("V", 160, 200), ("S", 200, 288)],
       "newl": [("S", 0, 72), ("V", 72, 160), ("V", 160, 200), ("S", 200, 288)],
       "nturn": "h0 h1 g0 g3 c0 c1 n1 n0 n2 n3 x0 e0 x1".split(),
       "lturn": "h0 h1 g0 g3 c0 c1 n1 n0 n2 n3 e0 x0 e1 x1 e2".split(),
       "hq": ["SV", "SV", "SV", "SV"], "mos": 96, "mosp": 160, "cut": 144, "cutq": 144, "vg": [], "tq": "SV", "tt": "SV", "planar": [0],
       "loads": ["sti", "ut", "x0", "x1", "tai", "tbi"], "lq": "SYSYSY", "rp0": [("SV", 0, 12), ("SV", 12, 25)], "sl0": [(0, 25)], "rowa": [(0, 10), (10, 18)], "late": "t",
       "tail": "St0 Yt1 Yc2 Ss0 Ss1 Ss2 Ss3 Yy2", "yq": "VV"}
OPT.update({"late": "", "tail": "Yc0 Sc1 Ss0 Ys1 Ss2 Ys3 Yy0 St0 Yt1 Sy1", "yq": "SV",
            "nturn": "h0 h1 g0 g3 c0 c1 n1 n0 n2 n3 x0 x1 e0".split(), "lturn": "h0 h1 g0 g3 c0 c1 n1 n0 n2 x0 n3 e0 x1 e1 e2".split(),
            "begin": ["e1", "e2", "v0", "e3", "v1", "g0", "g1", ("V", 0, 6), ("S", 18, 36), "s0", "s1", ("V", 6, 12), ("S", 12, 18), "o0", "a1", "o1"]})
OPT.update({"nturn": "h0 h1 g0 g3 c0 c1 n1 n0 n2 n3 x0 e0 x1".split(), "zpart": 144, "cuts": [12, 20], "chunk": [(0, 8), (8, 12), (12, 16), (16, 20), (20, 25)],
            "zq": [("V", 0, 0, 144), ("S", 2, 0, 144), ("V", 1, 0, 144), ("S", 3, 0, 144), ("V", 0, 144, 288), ("q", 0, 0, 144), ("S", 2, 144, 288), ("V", 1, 144, 288),
                   ("S", 3, 144, 288), ("q", 1, 144, 288)],
            "begin": ["e1", "e2", "e3", "v0", "v1", "g0", "g1", ("V", 0, 6), ("S", 18, 36), "s0", "s1", ("V", 6, 12), ("S", 12, 18), "o0", "a1", "k0", "o1"]})
OPT.update({"late": "t", "mirror": [("P", 1, 0, 288), ("P", 0, 0, 96), ("V", 0, 96, 288)],
            "pool": "cb eb enc down pi tm lam".split(),
            "start": "Vk31:33 Vk5:7 Vk4:5 Vk7:8 Vk33:34 Vk10:11 Vk27:28 Vk8:10 Vk11:12 Vk28:29 Vk12:13 Vk14:15 Sm0:12 Sm12:25 Vg0:0 Vk29:30 Vk15:16 Vk13:14 "
                     "Sn0:10 Sn10:18 Sn18:20 Vu0:0 Vk30:31 Vp0:0 Sp0:0 Vx0:160 Vr0:10 Sr10:25 Vx160:288 Vs0:10 Vs10:25 Vt0:0 Vt1:1 Vl0:25"})

SCRATCH = {"ps": ("psum", [128, 4096], "float32")}


def _bufs(where, dtype, **cols):
    for k in cols:
        SCRATCH[k] = (where, [128, cols[k]], dtype)


_bufs("sbuf", "bfloat16", xin=1152, xt1=1152, xt2=1152, xt3=1152, ut=512, vt=512, ones=128, eb=516, tm=16, ma=32, mb=32, m16=32,
      pure=400, chain=400, mask4=288, sg=288, cs=288, r0=400, so0=400, soc=288,
      tt=1152, tq=1152, zt=1152, zp=1152, h=1152, hg=1152)
for _n, _c in [("u", 128), ("ur", 128), ("v", 128), ("w", 512), ("e", 512), ("z", 288), ("h", 288)] + [("x%d" % _r, 288) for _r in range(4)] + [("l%d" % _r, 288) for _r in range(3)]:
    SCRATCH["q" + _n] = ("sbuf", [128, _c], "float8_e4m3fn_x4")
    SCRATCH["p" + _n] = ("sbuf", [128, _c], "uint8")
_bufs("sbuf", "int32", pi=8, pk=8, dj=16, li=26, tai=18, tbi=18, sti=18, qi=54, lo=54, hi=54)
_bufs("sbuf", "float32", pf=8, sc=12, enc=288, lam=288, turn=64, turned=64, rows=576, f1=54, val=288, ab=54, dd=18, mean=18, m2=36, yy=26, cb=18, down=26, tl=54, nv=36, abn=54,
      w=1160, r=400, rp=400, r1=400, so1=400, so=512, rn=320, so4=288, sol=400, yo=288)
_bufs("sbuf", "uint16", offu=8, l16=26, order=18, ahead=8, sn=18, lab=36, off=32, sl0=26, sl1=26, sl2=26, sh0=24, sh1=24, sh2=24, places=26,
      own0=72, own1=72, own2=72, arr0=72, arr1=72, arr2=72, got0=24, got1=24, got2=24)

DMAS = ["d%d" % _i for _i in range(26)]
SEMAPHORES = ["cV", "cS", "cT", "cP", "left"] + ["ax%d" % _r for _r in range(3)] + ["al%d%d" % (_r, _h) for _r in range(3) for _h in range(4)] + DMAS
CYCLE = 0.83
ORDER = []


def plan(nodes):
    wake, n = OPT["wake"], len(nodes)
    after = [{} for i in range(n)]
    for i in range(n):
        for p, hard in nodes[i]["pre"].items():
            after[p][i] = hard

    def held(i, q):
        return nodes[i]["on"][q][1] if nodes[i]["busy"] is None else nodes[i]["busy"]

    def lag(p, qp, i, hard):
        return nodes[p]["on"][qp][1] + wake if hard else nodes[p]["on"][qp][1] if None in nodes[i]["on"] else held(p, qp)

    def place(turn, back):
        at, taken = {}, {}
        turn = list(turn)
        while turn:
            i = next(i for i in turn if all(p in at for p in (after[i] if back else nodes[i]["pre"])))
            turn.remove(i)
            best = None
            for q in nodes[i]["on"]:
                d = held(i, q)
                if back:
                    t = max([nodes[i]["on"][q][1]] + [at[j][0] + lag(i, q, j, h) for j, h in after[i].items()]) - d
                else:
                    t = max([0.0] + [at[p][0] + lag(p, at[p][1], i, h) for p, h in nodes[i]["pre"].items()])
                for a, b in taken.get(q, []) if q else []:
                    if t + d <= a:
                        break
                    t = max(t, b)
                if best is None or t + d < best[0] + best[2]:
                    best = (t, q, d)
            t, q, d = best
            at[i] = (t + d if back else t, q)
            taken.setdefault(q, []).append((t, t + d))
            taken[q].sort()
        return at
    first = [list(x["on"])[0] for x in nodes]
    ahead = [0.0] * n
    for i in range(n - 1, -1, -1):
        ahead[i] = max([nodes[i]["on"][first[i]][1]] + [ahead[j] + lag(i, first[i], j, h) for j, h in after[i].items()])

    def length(order, wake, slow, gat, pe, far):
        end, free = {}, {}
        for i, q in order:
            x = nodes[i]
            t = max([free.get(q, 0.0)] + [end[p] + (wake if h else 0.0) for p, h in x["pre"].items() if h or q is None])
            d = x["on"][q][1]
            end[i] = t + (d * far if x["kind"] != "call" else d * pe if q == "T" else slow * (60 + (d - 60) * gat if x["listed"] else d))
            if q:
                free[q] = end[i] if x["busy"] is None else t + x["busy"]
        return max(end.values())
    turn, best, seed, scale = sorted(range(n), key=lambda i: (-ahead[i], i)), None, OPT["seed"], None
    for k in range(OPT["passes"]):
        at = place(turn, False)
        order = [(i, at[i][1]) for i in sorted(range(n), key=lambda i: (at[i][0], i))]
        worth = [length(order, *case) for case in OPT["cases"]]
        scale = scale or worth
        worth = sum(a / b for a, b in zip(worth, scale))
        if best is None or worth < best[0]:
            best = (worth, order, at)
        at = best[2] if k % 3 == 2 else at
        late = place(sorted(range(n), key=lambda i: (-at[i][0], -i)), True)
        shake = []
        for i in range(n):
            seed = (seed * 1103515245 + 12345) % 2 ** 31
            shake.append(OPT["shake"] * seed / 2 ** 31 if k % 3 == 2 else 0.0)
        turn = sorted(range(n), key=lambda i: (-late[i][0] - shake[i], i))

    cases = OPT["cases"]
    took = [{q: [x["on"][q][1] * far if x["kind"] != "call" else x["on"][q][1] * pe if q == "T" else slow * (60 + (x["on"][q][1] - 60) * gat if x["listed"] else x["on"][q][1])
                 for wake, slow, gat, pe, far in cases] for q in x["on"]} for x in nodes]
    hard = [[p for p, h in x["pre"].items() if h] for x in nodes]
    soft = [[p for p in x["pre"]] if None in x["on"] else [] for x in nodes]

    def run(order):
        total, blocks = 0.0, []
        for c in range(len(cases)):
            w = cases[c][0]
            end, why, free, last = [0.0] * n, [None] * n, {}, {}
            for i, q in order:
                t, y = free.get(q, 0.0), (last.get(q), True)
                for p in hard[i]:
                    if end[p] + w > t:
                        t, y = end[p] + w, (p, False)
                for p in soft[i]:
                    if end[p] > t:
                        t, y = end[p], (p, False)
                end[i], why[i] = t + took[i][q][c], y
                if q:
                    free[q], last[q] = end[i] if nodes[i]["busy"] is None else t + nodes[i]["busy"], i
            i = max(range(n), key=lambda j: end[j])
            total += end[i] / scale[c]
            while i is not None:
                p, queued = why[i]
                if queued and p is not None and p not in nodes[i]["pre"]:
                    blocks.append((p, i))
                i = p
        return total, blocks
    order = best[1]
    worth, blocks = run(order)
    for k in range(OPT["moves"]):
        seed = (seed * 1103515245 + 12345) % 2 ** 31
        p, i = blocks[(seed >> 8) % len(blocks)]
        where = {x[0]: j for j, x in enumerate(order)}
        seed = (seed * 1103515245 + 12345) % 2 ** 31
        how = (seed >> 8) % 100
        tried = list(order)
        if how < 30 and len(nodes[p]["on"]) > 1:
            tried[where[p]] = (p, [q for q in nodes[p]["on"] if q != order[where[p]][1]][0])
        elif how < 65:
            end = min([where[j] for j in after[p]] + [n])
            if end <= where[i]:
                continue
            to = min(end - 1, where[i] + (seed >> 16) % OPT["reach"])
            tried.insert(to, tried.pop(where[p]))
        else:
            start = max([where[j] for j in nodes[p]["pre"]] + [-1]) + 1
            to = max(start, where[p] - 1 - (seed >> 16) % OPT["reach"])
            if to >= where[p]:
                continue
            tried.insert(to, tried.pop(where[p]))
        w, b = run(tried)
        if w <= worth:
            order, worth, blocks = tried, w, b
    return order


def make_tracker(g, T):
    queues = {"V": g.vector, "S": g.scalar, "T": g.tensor, "P": g, "Y": g.sync}
    csem = {"V": "cV", "S": "cS", "T": "cT", "P": "cP"}
    nodes = []
    writes, reads = {}, {}

    def cols(x):
        if x[0] == "ps":
            return frozenset(range(x[1] // 512, (x[2] - 1) // 512 + 1))
        return frozenset(range(*x[1:]))

    def op(on, rd, wr, kind="call", listed=False, behind=(), busy=None):
        me, q = len(nodes), list(on)[0] if len(on) == 1 else "either"
        pre = {p: False for p in behind}
        for x in rd + wr:
            pre.update({p: True for c, p in writes.get(x[0], []) if c & cols(x)})
        for x in wr + [x for x in rd if x[0] == "ps"]:
            for c, p, oq in reads.get(x[0], []):
                if c & cols(x) and (oq != q or x in wr):
                    pre[p] = True
        for x in wr:
            k, c = x[0], cols(x)
            writes[k] = [e for e in writes.get(k, []) if not e[0] <= c] + [(c, me)]
            reads[k] = [e for e in reads.get(k, []) if not e[0] <= c]
        for x in rd if kind != "remote" else []:
            reads.setdefault(x[0], []).append((cols(x), me, q if kind == "call" and not listed and len(on) == 1 else "any"))
        nodes.append({"on": on, "kind": kind, "busy": busy, "pre": pre, "listed": listed})
        return me

    turn = {}

    def in_turn(name, aside=False):
        if name in turn and name[0] in OPT["turn"] and turn[name] < len(nodes) - 1:
            nodes[-1]["pre"].setdefault(turn[name], False)
        if not aside:
            turn[name] = len(nodes) - 1

    def finish():
        if not ORDER:
            ORDER.extend(plan(nodes))
        count, clocks, token = {}, {}, {}
        known = {q: {} for q in queues}
        ndma = 0
        for i, q in ORDER:
            n = nodes[i]
            call = n["on"][q][0]
            if n["kind"] == "arrival":
                token[i] = call
                clocks[call] = {call[0]: call[1]}
                count[call[0]] = call[1]
                continue
            best = {}
            for p, hard in n["pre"].items():
                if hard and known[q].get(token[p][0], 0) < token[p][1]:
                    best[token[p][0]] = max(best.get(token[p][0], 0), token[p][1])
            items = sorted(best.items())
            for s, v in items:
                if not any(o[0] != s and clocks[o].get(s, 0) >= v for o in items):
                    queues[q].wait_ge(T.sem[s], v)
            for s, v in items:
                for s2, v2 in clocks[(s, v)].items():
                    known[q][s2] = max(known[q].get(s2, 0), v2)
            if n["kind"] == "remote":
                count["left"] = count.get("left", 0) + call(g)
                continue
            s, inc = csem.get(q), 1
            if n["kind"] == "dma":
                s, inc = DMAS[ndma], 16
                ndma += 1
            made = call(queues[q])
            for x in made if isinstance(made, list) else [made]:
                x.then_inc(T.sem[s], inc)
                count[s] = count.get(s, 0) + inc
            token[i] = (s, count[s])
            clocks[token[i]] = dict(known[q])
            clocks[token[i]][s] = count[s]
        for s in sorted(count):
            g.wait_ge(T.sem[s], count[s])

    return op, in_turn, finish


def rank_program(g, core, T, topo):
    rank = T.rank_of(core)
    if rank is None:
        return
    A = AluOpType
    F = ActivationFunctionType
    op, in_turn, finish = make_tracker(g, T)
    PART = [(0, OPT["part"]), (OPT["part"], C)]
    ZPART = [(0, OPT["zpart"]), (OPT["zpart"], C)]
    CHUNK = OPT["chunk"]
    AT = [0]
    for a, b in CHUNK:
        AT.append(AT[-1] + (b - a + 1) // 2 * 2)

    def ap(x):
        if not isinstance(x, tuple):
            return x
        if len(x) == 3:
            return T[x[0]][:, x[1]:x[2]]
        return T[x[0]][:, x[1]:(x[2] if x[2] >= 0 else None):x[3]]

    def rgs(*xs):
        return [x for x in xs if isinstance(x, tuple)]

    def size(x):
        return len(range(*x[1:]))

    def cycles(out, *ins, rate=1.0):
        if all(SCRATCH[x[0]][2] in ("bfloat16", "uint16") for x in (out,) + ins):
            rate /= 2
        return max(64, size(out) * rate) * CYCLE

    def fetch(q, n):
        return (65 if q == "S" else 50) + n * OPT["gat"] * CYCLE

    def ts(out, in0, s1, s2, *ops):
        op({"V": (lambda e: e.tensor_scalar(ap(out), ap(in0), ap(s1), ap(s2), *ops), cycles(out, in0))}, rgs(in0, s1, s2), [out])

    def tt(out, in0, in1, o):
        op({"V": (lambda e: e.tensor_tensor(ap(out), ap(in0), ap(in1), o), max(64, size(out) * OPT["add"]) * CYCLE if out[0][:2] == "xt" else cycles(out, in0, in1, rate=2.0))}, [in0, in1], [out])

    def cp(out, in_):
        move("V", out, in_)

    def fill(out, c):
        op({"V": (lambda e: e.memset(ap(out), c), cycles(out))}, [], [out])

    def sign(out, in_):
        op({"S": (lambda e: e.activation(ap(out), ap(in_), F.Sign, bias=TINY), cycles(out, in_))}, [in_], [out])

    def move(qs, out, in_, scale=None):
        on = {"V": (lambda e: e.tensor_scalar(ap(out), ap(in_), scale, None, A.mult) if scale else e.tensor_copy(ap(out), ap(in_)), cycles(out, in_)),
              "S": (lambda e: e.activation(ap(out), ap(in_), F.Copy, scale=scale if scale else 1.0), max(64, size(out)) * CYCLE),
              "P": (lambda e: e.affine_select(ap(out), ap(in_), [[1, size(out)]], A.is_ge, 0.0, 0, 0), 170 + 2 * size(out) * CYCLE)}
        op({q: on[q] for q in qs}, [in_], [out])

    def gather(qs, out, win, off, add=None, scale=None, fn=None):
        src = ap(win).indirect(ap(off))
        k = {"bias": add} if add else {"scale": scale} if scale else {}
        on = {"S": lambda e: e.activation(ap(out), src, fn if fn else F.Identity if add else F.Copy, **k),
              "V": lambda e: e.tensor_scalar(ap(out), src, add if add else scale, None, A.add if add else A.mult) if k else e.tensor_copy(ap(out), src)}
        op({q: (on[q], fetch(q, size(out))) for q in qs}, [win, off], [out], listed=True)

    def gather_add(out, win, off, other):
        call = lambda e: e.tensor_tensor(ap(out), ap(win).indirect(ap(off)), ap(other), A.add)
        op({"V": (call, fetch("V", size(out)))}, [win, off, other], [out], listed=True)

    def iota(out, pat, base, cm):
        k = {} if SCRATCH[out[0]][2] == "int32" else {"allow_small_or_imprecise_dtypes": True}
        op({"P": (lambda e: e.iota(ap(out), pat, base, cm, **k), 130 + 2 * size(out) * CYCLE)}, [], [out])
        in_turn("P")

    def scan(out, mask, row, first=0.0, op0=A.mult, op1=A.add):
        op({"V": (lambda e: e.tensor_tensor_scan(ap(out), ap(mask), ap(row), ap(first), op0, op1), cycles(out, mask, row))}, rgs(mask, row, first), [out])

    def quant(q, a, b, src, at=None):
        x = (src, 4 * a, 4 * b) if at is None else (src, at, at + 4 * (b - a))
        op({"V": (lambda e: e.quantize_mx(T["q" + q][:, a:b], T["p" + q][:, a:b], ap(x)), 12 + 0.22 * size(x))}, [x], [("q" + q, a, b)])

    def pick(q, dst, a, b, src, n, off):
        rd = [("q" + src, 0, n), off]
        if q == "V":
            op({"V": (lambda e: e.tensor_copy(T["q" + dst][:, a:b].bitcast(dt.uint32), T["q" + src][:, 0:n].bitcast(dt.uint32).indirect(ap(off))), fetch("V", b - a))},
               rd, [("q" + dst, a, b)], listed=True)
        else:
            op({"S": (lambda e: e.activation(T["p" + dst][:, a:b], T["p" + src][:, 0:n].indirect(ap(off)), F.Copy), fetch("S", b - a))}, rd, [("p" + dst, a, b)], listed=True)

    def bank(i, n, at=0):
        return ("ps", 512 * i + at, 512 * i + at + n)

    def mm(i, st, sa, mv, a, b):
        call = lambda e: e.matmul_mx(ap(bank(i, b - a)), T["q" + st][:, sa:sa + 128], T["p" + st][:, sa:sa + 128], T["q" + mv][:, a:b], T["p" + mv][:, a:b], True, True)
        op({"T": (call, (b - a + 16) * CYCLE * OPT["pe"])}, [("q" + st, sa, sa + 128), ("p" + st, sa, sa + 128), ("q" + mv, a, b), ("p" + mv, a, b)], [bank(i, b - a)])

    def readout(buf, a, b):
        return (buf, 16 * a + 15, 16 * b, 16)

    def pieces(a, b, n):
        return [(c, min(b, c + n)) for c in range(a, b, n)]

    moved, loads = [0], {"S": [], "Y": []}

    def dma(q, dst, src, rd, wr, nbytes, behind=()):
        moved[0] += nbytes + 300
        return op({q: (lambda e: e.dma_start(dst, src), OPT["load"] + OPT["rate"] * moved[0])}, rd, wr, kind="dma", busy=50.0, behind=behind)

    def load(q, dst, src, nbytes):
        loads[q].append(dma(q, ap(dst).bitcast(dt.uint8) if dst[0] == "qw" else ap(dst), src, [], [dst], nbytes, loads[q][-1:]))

    cut = 4 * PART[0][1]
    first_loads = {"sti": (("sti", 0, 18), T.st[:, :], 72), "tai": (("tai", 0, 18), T.ta[:, :], 72), "tbi": (("tbi", 0, 18), T.tb[:, :], 72),
                   "x0": (("xin", 0, cut), T.x[:, 0:cut], 2 * cut), "ut": (("ut", 0, 512), T.u[:, :], 1024),
                   "x1": (("xin", cut, 4 * C), T.x[:, cut:4 * C], 8 * C - 2 * cut)}
    for name, q in zip(OPT["loads"], OPT["lq"]):
        load(q, *first_loads[name])

    iota(("dj", 0, 16), [[1, 16]], 128, -1)
    iota(("li", 0, 26), [[0, 26]], 0, 1)
    for x, c in ((("ones", 0, 128), 1.0), (("eb", 0, 516), 0.0), (("w", MID, MID + 2), 0.0), (("turn", 0, 64), 0.0)):
        fill(x, c)
        in_turn("N")
    for x in OPT["pool"]:
        if x == "eb":
            op({"P": (lambda e: e.affine_select(T.eb[:, 3:515:4], T.ones[:, :], [[1, 128]], A.is_equal, 0.0, 0, -1), 170 + 2 * 128 * CYCLE)}, [("ones", 0, 128)], [("eb", 3, 515, 4)])
            in_turn("P")
        elif x == "tm":
            iota(("tm", 0, 16), [[1, 16]], 0, 0)
        elif x == "pi":
            iota(("pi", 0, 5), [[1, 5]], 0, 1)
        elif x == "enc":
            iota(("enc", 0, C), [[2, C]], 2, 0)
        elif x == "down":
            iota(("down", 0, 26), [[-1, 26]], COLS - 1, 0)
        elif x == "lam":
            iota(("lam", 0, C), [[1, 16], [-16, 18]], 16 * 17 + 1, 0)
        else:
            iota(("cb", 0, 18), [[16, 18]], 0, 0)

    p16, q16, p4, q4, t4 = [("pf", j, j + 1) for j in range(5)]
    SC, HALF, START, T4, SC4, QUART = [("sc", j, j + 1) for j in range(6)]

    def masks(a, here, behind):
        return [lambda: ts(("ma", 16 * a, 16 * a + 16), ("tm", 0, 16), behind, BIG, A.is_equal, A.mult),
                lambda: ts(("mb", 16 * a, 16 * a + 16), ("tm", 0, 16), here, None, A.not_equal),
                lambda: tt(("m16", 16 * a, 16 * a + 16), ("ma", 16 * a, 16 * a + 16), ("mb", 16 * a, 16 * a + 16), A.max)]
    m16, m4 = masks(0, p16, q16), masks(1, p4, q4)
    m16[0] = lambda: ts(("ma", 0, 16), ("dj", 0, 16), 1.0, BIG, A.is_equal, A.mult)
    m16[1] = lambda: ts(("mb", 0, 16), ("dj", 0, 16), 0.0, None, A.not_equal)
    small = [lambda: ts(("pk", 1, 2), ("pi", 1, 2), 15, None, A.bitwise_and),
             lambda: ts(("pk", 2, 4), ("pi", 0, 5, 4), 2, 3, A.arith_shift_right, A.bitwise_and),
             lambda: ts(("pk", 4, 5), ("pi", 0, 1), 3, None, A.bitwise_and),
             lambda: cp(("pf", 1, 5), ("pk", 1, 5)),
             lambda: cp(("offu", 0, 8), ("cb", 0, 8)),
             m16[0], m16[1],
             lambda: cp(("l16", 0, 26), ("li", 0, 26)),
             lambda: ts(SC, p16, 15.0, 1.0 / BIG, A.is_equal, A.max),
             lambda: ts(("sc", 9, 10), p16, 18.0, None, A.mult),
             m16[2],
             lambda: ts(("sc", 8, 9), p16, 15.0, BIG, A.not_equal, A.mult),
             lambda: ts(QUART, SC, 0.25, None, A.mult),
             lambda: ts(("places", 0, 26), ("down", 0, 26), ("sc", 9, 10), None, A.add),
             lambda: ts(HALF, SC, 0.5, None, A.mult),
             lambda: ts(START, ("sc", 8, 9), 1.0, BASE + CARRY, A.max, A.mult),
             m4[0], m4[1],
             lambda: ts(SC4, p4, 3.0, 1.0 / BIG, A.is_equal, A.max),
             lambda: ts(T4, t4, -4.0, None, A.add),
             lambda: ts(("ahead", 0, STAGES), ("cb", 18 - STAGES, 18), q16, None, A.add),
             lambda: ts(("tl", 36, 54), ("cb", 17, -1, -1), p16, None, A.add),
             m4[2]]
    small += [lambda j=j: ts(("mask4", j, C, 4), ("ones", 0, C // 4), ("m16", 16 + j, 17 + j), None, A.mult) for j in range(4)]
    small += [lambda b=b: quant("e", 128 * b, 128 * b + 128, "eb", 3 - b) for b in range(4)]
    small += [lambda: ts(("dj", 0, 16), ("dj", 0, 16), 15, None, A.bitwise_and), lambda: ts(("li", 0, 26), ("li", 0, 26), 15, None, A.bitwise_and),
              lambda: cp(p16, ("li", 0, 1))]
    made = []

    def as_list(dst, row, a, b, cuts=(), shift=0):
        cuts = [a] + [c for c in cuts if a < c < b] + [b]
        for c, d in zip(cuts, cuts[1:]):
            scan(("sol", 16 * c, 16 * d), ("pure", 16 * c, 16 * d), (row, 16 * c, 16 * d))
        ts((dst, a + shift, b + shift), readout("sol", a, b), QUART, -1.0, A.mult, A.add)

    for x in OPT["start"].split():
        q, what, a, b = x[0], x[1], int(x[2:].split(":")[0]), int(x.split(":")[-1])
        if what == "m":
            gather(q, ("pure", 16 * a, 16 * b), ("m16", 0, 16), ("l16", 0, b - a))
        elif what == "k":
            for j in range(a, b):
                small[j]()
                made.append(j)
                in_turn("N")
        elif what == "g":
            cp(("sn", 0, 18), ("sti", 0, 18))
        elif what == "u":
            quant("u", 0, 128, "ut")
        elif what == "p":
            pick(q, "ur", 0, 128, "u", 128, ("offu", 0, 8))
        elif what == "x":
            quant("x0", a, b, "xin")
        elif what == "n":
            gather(q, ("rn", 16 * a, 16 * b), ("enc", 0, C), ("sn", a % 18, a % 18 + b - a), scale=2.0)
        elif what == "r":
            gather(q, ("rp", 16 * a, 16 * b), ("rn", 0, 320), ("places", a, b))
        elif what == "s":
            scan(("sol", 16 * a, 16 * b), ("pure", 16 * a, 16 * b), ("rp", 16 * a, 16 * b))
        elif what == "l":
            ts(("sl0", a, b), readout("sol", a, b), QUART, -1.0, A.mult, A.add)
        else:
            cp(("lab", 18 * a, 18 * a + 18), (("tai", "tbi")[a], 0, 18))
        in_turn("N" if q == "V" else "M")

    load("Y", ("qw", 0, 512), T.wc[:, :], 2048)
    load("Y", ("pw", 0, 512), T.ws[:, :], 512)
    load("Y", ("vt", 0, 512), T.v[:, :], 1024)

    def halves(src):
        tt(("m2", 0, 18), (src, 0, 18), (src, 18, 36), A.add)
        tt(("m2", 18, 36), (src, 18, 36), (src, 0, 18), A.subtract)
        ts(("mean", 0, 18), ("m2", 0, 18), 0.5, None, A.mult)
        ts(("dd", 0, 18), ("m2", 18, 36), HALF, None, A.mult)

    def later():
        for j in range(len(small)):
            if j not in made:
                small[j]()
                in_turn("N", True)
        quant("v", 0, 128, "vt")
        in_turn("N", True)
        for c, src in enumerate(("tai", "tbi")):
            cp(("turn", 32 * c, 32 * c + 18), (src, 0, 18))
            in_turn("N", True)
        op({"V": (lambda e: e.transpose(T.turned[:, :], T.turn[:, :]), 64 * CYCLE)}, [("turn", 0, 64)], [("turned", 0, 64)])
        rows = [(T.rows[16 * k:16 * k + 1, C * c:C * c + C], T.turned[32 * (k // 2):32 * (k // 2) + 18, 32 * c + 16 * (k % 2):32 * c + 16 * (k % 2) + 16])
                for k in range(8) for c in range(2)]
        op({"Y": (lambda e: [e.dma_start(dst, src) for dst, src in rows], OPT["deal"])}, [("turned", 0, 64)], [("rows", 0, 2 * C)], kind="dma", busy=800.0, behind=loads["Y"][-1:])
        deals = [(T.tl[:, 18 * c:18 * c + 18], T.rows[0:128:16, C * c:C * c + C]) for c in range(2)]
        op({"Y": (lambda e: [e.dma_start(dst, src) for dst, src in deals], OPT["deal"])}, [("rows", 0, 2 * C)], [("tl", 0, 36)], kind="dma", busy=100.0)
        ts(("qi", 0, 54), ("tl", 0, 54), -8.5, 1.0 / 18, A.add, A.mult)
        ts(("f1", 0, 54), ("qi", 0, 54), 289.0, 272.0, A.mult, A.add)
        ts(("tl", 0, 54), ("tl", 0, 54), -16.0, None, A.mult)
        for c in range(3):
            tt(("ab", 18 * c, 18 * c + 18), ("tl", 18 * c + 17, 18 * c - 1, -1), ("f1", 18 * c + 17, 18 * c - 1, -1), A.add)
        cp(("order", 0, 18), ("ab", 36, 54))
        halves("ab")

    def as_wide(dst, row, at):
        for a, b in PART:
            scan(("so4", a, b), ("mask4", a, b), (row, at + a, at + b))
        ts((dst, 0, C // 4), ("so4", 3, C, 4), SC4, T4, A.mult, A.add)

    def natural(at, n, out):
        ts(("lo", at, at + n), ("qi", at, at + n), 15, None, A.bitwise_and)
        ts(("hi", at, at + n), ("qi", at, at + n), 4, None, A.arith_shift_right)
        ts(("tl", at, at + n), ("lo", at, at + n), 18.0, 17.0, A.mult, A.add)
        tt(out, ("tl", at, at + n), ("hi", at, at + n), A.subtract)

    def runs(t):
        s, until = OPT["early"]
        rest = [(a, b, AT[k]) for k, (a, b) in enumerate(CHUNK)][1:]
        if t <= until:
            return [(t, s, 0), (s, CHUNK[0][1], 6)] + rest
        if t >= CHUNK[0][1]:
            return [(t, rest[0][1], rest[0][2])] + rest[1:]
        return [(t, CHUNK[0][1], 6 - s + t if t == until + 1 and until else 0)] + rest

    def places_of(t, a, b):
        segs = []
        for c, d, at in runs(t):
            lo, hi = max(a, c), min(b, d)
            if lo < hi:
                if segs and segs[-1][2] + segs[-1][1] - segs[-1][0] == at + lo - c:
                    segs[-1][1] = hi
                else:
                    segs.append([lo, hi, at + lo - c])
        return segs

    def exchange(step, last):
        if step == 0:
            scan(("soc", 0, C), ("pure", 0, C), ("cs", 0, C))
        elif step == 1:
            tt(("m2", 0, 18), readout("soc", 0, 18), ("dd", 0, 18), A.mult)
        elif step == 2:
            for c, o in enumerate((A.add, A.subtract)):
                tt(("abn", 18 * c + 17, 18 * c - 1, -1) if last else ("ab", 18 * c, 18 * c + 18), ("mean", 0, 18), ("m2", 0, 18), o)
                in_turn("N")
        else:
            cp(("lab", 0, 36), ("ab", 0, 36))
        in_turn("N")
        if step == 3:
            ts(("dd", 0, 18), ("m2", 0, 18), SC, -1.0, A.mult, A.mult)

    def one_round(r):
        partner = T.cores[rank ^ STEP[r]]
        rid, pid = topo.addr(partner, core)
        engines = topo.engines(core, partner)
        mask = sum(1 << e for e in engines)
        qx, lx, own, arr, got, xt, last = "x%d" % r, "l%d" % r, "own%d" % r, "arr%d" % r, "got%d" % r, "xt%d" % (r + 1), r == 2
        sl, short, row = "sl%d" % r, "sh%d" % r, ["rp", "rp", "r"][r]

        def send(sem, pairs, rd, wr, time):
            def call(dst, src):
                return lambda e: (e.remote_dma(dst, src, T.sem[sem], T.sem.left, pid, rid, mask), len(engines))[1]
            sent = [op({"P": (call(dst, src), time)}, rd, [], kind="remote", busy=200.0) for dst, src in pairs]
            op({None: ((sem, len(pairs) * len(engines)), 0.0)}, [], wr, kind="arrival", behind=sent)

        for hf, (a, b) in enumerate(PART):
            mm(hf, "ur", 0, qx, a, b)
            sign(("sg", a, b), bank(hf, b - a))
            in_turn("M")

        send("ax%d" % r, [(T["q" + lx][:, :].bitcast(dt.uint8), T["q" + qx][:, :].bitcast(dt.uint8)), (T["p" + lx][:, :], T["p" + qx][:, :])],
             [("q" + qx, 0, C), ("p" + qx, 0, C)], [("q" + lx, 0, C)], OPT["tile"])

        def lane(which, q, k, a, b):
            if which == "t":
                move(q, ("tt", C * k + a, C * k + b) if r in OPT["planar"] else ("tt", 4 * a + k, 4 * b, 4), bank(2 + k, b - a, a))
            else:
                move(q, ("tq", C * k + a, C * k + b), bank((6 + k) % 8, b - a, a))

        def lanes(which, line=None):
            for k in range(4):
                if which == "q":
                    mm((6 + k) % 8, "e", 128 * k, lx, 0, C)
            for k, a, b in todo if which == "t" else [(k, a, b) for k in range(4) for a, b in pieces(0, C, OPT["cutq"])]:
                lane(which, "SV", k, a, b)
                if line:
                    in_turn(line, True)

        def table(q, a, b):
            c = a // 18
            gather(q, ("w", MID + 2 + 32 * (a - 18 * c) + c, MID + 2 + 32 * (b - 18 * c) + c, 2), ("val", 0, C), ("lab", a, b))

        head = OPT["head"]

        def first(step, k):
            q, a, b = head[k]
            if step == "g":
                if q == "V":
                    gather_add(("r1", 16 * a, 16 * b), ("sg", 0, C), (sl, a - 1, b - 1), (row, 16 * a, 16 * b))
                else:
                    gather("S", ("r0", 16 * a, 16 * b), ("sg", 0, C), (sl, a - 1, b - 1))
            elif step == "s":
                if q == "V":
                    scan(("so1", 16 * a, 16 * b), ("pure", 16 * a, 16 * b), ("r1", 16 * a, 16 * b))
                else:
                    scan(("so0", 16 * a, 16 * b), ("pure", 16 * a, 16 * b), ("r0", 16 * a, 16 * b))
            elif step == "a":
                tt(("yy", a, b), readout("so0", a, b), readout("sol", a, b), A.add)
            else:
                for lo, hi, at in places_of(1, a, b):
                    ts(("off", at, at + hi - lo), readout("so1", lo, hi) if q == "V" else ("yy", lo, hi), HALF, 0.5, A.mult, A.add)
        for x in OPT["begin"]:
            if x[0] == "e":
                if r:
                    exchange(int(x[1]), False)
            elif x[0] == "k":
                if r == 0:
                    ts(("chain", 0, 400), ("pure", 0, 400), 1.0 / (2048 * BIG), None, A.max)
                    in_turn("N")
            elif x[0] == "v":
                a, b = PART[int(x[1])]
                scan(("val", a, b), ("enc", a, b), ("sg", a, b), 0.0, A.max, A.mult)
                in_turn("N")
            elif len(x) == 2:
                first(x[0], int(x[1]))
                in_turn("M" if x[0] == "g" and head[int(x[1])][0] == "S" else "N")
            else:
                table(*x)
                in_turn("M" if x[0] == "S" else "N")
        for q, c, a, b in OPT["mirror"]:
            move(q, ("w", MID - 2 * a - 2 + c, MID - 2 * b - 2 + c, -2), ("w", MID + 2 * a + 2 + c, MID + 2 * b + 2 + c, 2))
            if q == "V":
                in_turn("N")
        if r == 0:
            later()
        todo = []
        for k in range(4):
            mm(2 + k, "e", 128 * k, qx, 0, C)
            todo += [(k, a, b) for a, b in pieces(0, C, OPT["cut"])]
        for which in "tq":
            if which not in OPT["late"]:
                lanes(which)

        def offsets(t, a, b, j):
            for c, d, at in places_of(t + 1, a, b):
                ts(("off", at, at + d - c), readout("so", c + j, d + j), SC, MID - BASE - CARRY, A.mult, A.add)
                in_turn("V")
        waiting = []
        for t in range(1, STAGES + 1):
            for k, (a, b, at) in enumerate(runs(t)):
                win = ("w", MID if t == 1 else 0, MID + 2 * C + 2)
                if t == STAGES:
                    while waiting:
                        offsets(*waiting.pop(0))
                    gather("S", ("r", 16 * a, 16 * b), win, ("off", at, at + b - a), fn=F.Abs, scale=2.0)
                    in_turn("S")
                    continue
                gather("S", ("r", 16 * a, 16 * b), win, ("off", at, at + b - a), add=BASE)
                in_turn("S")
                j = k + len(CHUNK) + 1 - len(runs(t))
                c = a - min(k, 1)
                scan(("so", 16 * (c + j), 16 * (b + j)), ("chain", 16 * c, 16 * b), ("r", 16 * c, 16 * b), START)
                in_turn("V")
                while len(waiting) >= OPT["lag"][t - 1]:
                    offsets(*waiting.pop(0))
                waiting.append((t, a, b, j))

        for which in OPT["late"]:
            lanes(which, "S")

        done = ("r", 16 * STAGES, 400)
        for hf, (a, b) in enumerate(OPT.get("lpart", ZPART)):
            a, b = a // 16, b // 16
            as_list(short, "r", STAGES + a, STAGES + b, OPT["cuts"], -STAGES)
            send("al%d%d" % (r, hf), [(T[got][:, a + a % 2:b + a % 2], T[short][:, a:b])], [(short, a, b)], [(got, a + a % 2, b + a % 2)], OPT["list"])

        if last:
            ts(("qi", 36, 54), readout("sol", STAGES, COLS), QUART, -1.0, A.mult, A.add)
            natural(36, 18, ("abn", 53, 35, -1))
            for a, b in ((0, 8), (8, 18)):
                gather("SV", ("rn", 16 * a, 16 * b), done, ("order", a, b))
            as_wide(own, "rn", 0)
            cp(("qi", 0, 36), ("lab", 0, 36))
            natural(0, 36, ("nv", 0, 36))
            halves("nv")
        else:
            src = "r"
            if r == 0:
                src = "rp"
                for a, b in ((0, 10), (10, 18)):
                    gather("SV", ("rp", 16 * (STAGES + a), 16 * (STAGES + b)), ("lam", 0, C), (short, a, b), scale=4.0)
            as_wide(own, src, 16 * STAGES)
            gather("SV", (src, 0, 16 * STAGES), (src, 16 * STAGES, 400), ("ahead", 0, STAGES))
            if r == 0:
                as_list("sl1", src, 0, COLS, [STAGES])
            else:
                scan(("sol", 0, 16 * STAGES), ("pure", 0, 16 * STAGES), (src, 0, 16 * STAGES))
                ts(("sl2", 0, COLS), readout("sol", 0, COLS), QUART, -1.0, A.mult, A.add)
        send("al%d3" % r, [(T[arr][:, :], T[own][:, :])], [(own, 0, 72)], [(arr, 0, 72)], OPT["wide"])
        if r in OPT["planar"]:
            for k in range(4):
                for a, b in pieces(0, C, OPT["mosp"]):
                    gather("SV", ("zt", 4 * a + k, 4 * b, 4), ("tt", C * k, C * k + C), (short, a // 16, b // 16))
        else:
            for a, b in pieces(0, C, OPT["mos"]):
                gather("SV", ("zt", 4 * a, 4 * b), ("tt", 0, 4 * C), (own, a // 4, b // 4))

        for q, k, a, b in OPT["zq"]:
            if q == "q":
                quant("z", a, b, "zp")
            else:
                gather(q, ("zp", 4 * a + k, 4 * b, 4), ("tq", C * k, C * k + C), (got, a // 16 + a // 16 % 2, b // 16 + a // 16 % 2))
            in_turn("M" if q == "S" else "N")
        for hf, (a, b) in enumerate(ZPART):
            for k in (0, 2, 1, 3):
                mm(4 * hf + k, "w", 128 * k, "z", a, b)
                move(OPT["hq"][k], ("h", 4 * a + k, 4 * b, 4), bank(4 * hf + k, b - a), 0.03125)

        for x in OPT["lturn" if last else "nturn"]:
            j = int(x[1])
            if x[0] == "h":
                a, b = ZPART[j]
                quant("h", a, b, "h")
                in_turn("N")
                mm(2 + 5 * j, "ur", 0, "h", a, b)
            elif x[0] == "c":
                a, b = ZPART[j]
                sign(("cs", a, b), bank(2 + 5 * j, b - a))
                in_turn("M")
            elif x[0] == "g":
                q, a, b = OPT["newl" if last else "new"][j]
                gather("S", ("hg", 4 * a, 4 * b), ("h", 0, 4 * C), (arr, a // 4, b // 4))
                in_turn("M")
            elif x[0] == "e":
                exchange(j, last)
            elif x[0] == "x":
                quant("x%d" % (r + 1), PART[j][0], PART[j][1], xt)
                in_turn("N")
            else:
                q, a, b = OPT["newl" if last else "new"][j]
                if q == "V":
                    gather_add((xt, 4 * a, 4 * b), ("h", 0, 4 * C), (arr, a // 4, b // 4), ("zt", 4 * a, 4 * b))
                else:
                    tt((xt, 4 * a, 4 * b), ("hg", 4 * a, 4 * b), ("zt", 4 * a, 4 * b), A.add)
                in_turn("N")

    for r in range(3):
        one_round(r)

    moved[0] = 0
    dma("Y", T.op[:, 0:C], T.abn[:, 36:54], [("abn", 36, 54)], [], -300)
    for hf, (a, b) in enumerate(PART):
        mm(3 + hf, "v", 0, "x3", a, b)
        move(OPT["yq"][hf], ("yo", a, b), bank(3 + hf, b - a))
    for q, what, k in OPT["tail"].split():
        k = int(k)
        a, b = (PART + [(0, C)] * 2)[k]
        if what == "c":
            dma(q, T.oc[:, 4 * a:4 * b], T.qx3[:, a:b].bitcast(dt.uint8), [("qx3", a, b)], [], -300)
        elif what == "y":
            dma(q, T.y[:, a:b], T.yo[:, a:b], [("yo", a, b)], [], 0)
        elif what == "t":
            dma(q, T.op[:, C + C * k:2 * C + C * k], T.abn[:, 18 * k:18 * k + 18], [("abn", 18 * k, 18 * k + 18)], [], -300)
        else:
            dma(q, T.osc[4 * k:4 * k + 4, :], T.px3[32 * k:32 * k + 4, :], [("qx3", 0, C), ("px3", 0, C)], [], -300)
        in_turn("D" + q)
    finish()
